import numpy as np, ml_dtypes
CORES = [23,119,17,113]
N = 4
BF = ml_dtypes.bfloat16
def gentries(a):
    return np.ascontiguousarray(a.reshape(8, 16, -1).transpose(0, 2, 1)).reshape(8, -1)
def gtable(e):
    e = np.asarray(e); return np.ascontiguousarray(e.reshape(8, -1, 16).transpose(0, 2, 1)).reshape(128, -1).astype(np.int32)
S, B, D, T, J, L = 4096, 1024, 7, 4, 77, 4096
REC = np.array([0, 256, 128, 85, 64, 51, 42, 36], np.int64)
def sums(rng, tot, lo, hi, n):
    x = rng.integers(lo, hi + 1, n); e = int(tot - np.sum(x))
    room = np.repeat(np.arange(n), hi - x if e > 0 else x - lo)
    np.add.at(x, rng.permutation(room)[:abs(e)], 1 if e > 0 else -1)
    return x
def durs(rng):
    x = rng.integers(1, D + 1, (N, 8, B))
    for q in range(N):
        for g in range(8): x[q, g, :B - 1] = sums(rng, int(rng.integers(S // 8 * 7, S // 2 * 3 + 1)), 1, D, B - 1)
    return x
def gains(rng, e):
    return (1.0 + rng.random((N, 128, T))) * np.exp2(rng.integers(-e, 1, (N, 128, T))) * rng.choice(np.array([-1.0, 1.0]), (N, 128, T))
def pack(A, v, x, m, u):
    return {"am": np.ascontiguousarray(A.reshape(N, 128, B)).astype(np.float32).astype(BF), "ve": np.ascontiguousarray(v.reshape(N, 128, B)).astype(np.float32).astype(BF),
            "du": np.stack([gtable(a) for a in x]), "mp": np.stack([gtable(a) for a in m]), "gain": u.astype(np.float32)}
def setup_inputs(rng):
    return pack(rng.integers(-256, 257, (N, 8, 16, B)), rng.integers(-64, 65, (N, 8, 16, B)), durs(rng), rng.integers(0, B, (N, 8, B)), gains(rng, 1))
def setup_inputs_spread(rng):
    A = rng.integers(-256, 257, (N, 8, 16, B)) >> rng.integers(0, 2, (N, 8, 1, B)); v = rng.integers(-64, 65, (N, 8, 16, B)) >> rng.integers(0, 5, (N, 8, 1, B))
    x = durs(rng); x[:, 1::4] = np.sort(x[:, 1::4], axis=2); x[:, 2::4] = np.sort(x[:, 2::4], axis=2)[..., ::-1]
    m = np.minimum((B * rng.random((N, 8, B)) ** 3).astype(np.int64), B - 1)
    return pack(A, v, x, m, gains(rng, 0) * np.exp2(rng.integers(-1, 1, (N, 1, T))))
def setup_inputs_ends(rng):
    A = 256 * rng.choice(np.array([-1, 1]), (N, 8, 16, B)); one = 256 * rng.choice(np.array([-1, 1]), (N, 8, 1, B))
    for g in (0, 1, 4, 5): A[:, g] = one[:, g]
    for q in range(N):
        for g in (1, 5):
            i = int(rng.integers(0, 16)); A[q, g, i] = -A[q, g, i]
    A[:, 7, :, B - 1] = 256; A[:, 6, :, B - 1] = -256
    v = 64 * rng.choice(np.array([-1, 1]), (N, 8, 16, B))
    x = np.where(rng.random((N, 8, B)) < rng.choice(np.array([0.3, 0.5, 0.7]), (N, 8, 1)), D, 1)
    for q in range(N): x[q, (q + 8 - N) % 8] = D; x[q, (q + 11 - N) % 8] = 1
    return pack(A, v, x, (B - 1) * rng.integers(0, 2, (N, 8, B)), gains(rng, 1))
def setup_inputs_corners(rng):
    A = rng.integers(-256, 257, (N, 8, 16, B)); v = rng.choice(np.array([-64, -63, -1, 0, 0, 1, 63, 64]), (N, 8, 16, B))
    c = rng.integers(64, 257, 16) * rng.choice(np.array([-1, 1]), 16)
    for i in (0, 15): A[:, :, i] = c[i]; v[:, :, i] = 0
    x = rng.choice(np.array([1, D]), (N, 8, B)); m = rng.integers(0, B, (N, 8, B)); last = (S - 1, S, S + 1, S - 2, B - 1, D * (B - 1), S, S - 1)
    for q in range(N):
        for g in range(8):
            x[q, g, :B - 1] = sums(rng, last[(q + g) % 8], 1, D, B - 1); w = (q + 3 * g) % 4
            if w == 0: m[q, g] = np.arange(B)
            elif w == 1: m[q, g] = 0
            elif w == 2: m[q, g] = B - 1
    return pack(A, v, x, m, gains(rng, 0))
def setup_inputs_crowd(rng):
    mid = rng.integers(24, 49, (N, 8, 16)) * rng.choice(np.array([-1, 1]), (N, 8, 16))
    A = np.repeat(mid[..., None], B, axis=3); v = rng.integers(-3, 4, (N, 8, 16, B)); x = rng.integers(1, 4, (N, 8, B)); m = rng.integers(0, B, (N, 8, B))
    for q in range(N):
        for g in range(8):
            if g % 2 == 0:
                n = int(rng.choice(np.array([0, 1, 7, 8, 9, 15, 16])))
                if q == 0: n = (8, 9, 16, 0)[g // 2]
                if q == 1: n = (15, 7, 9, 8)[g // 2]
                o = rng.permutation(16); A[q, g] = rng.integers(112, 257, (16, B)); A[q, g, o[:n]] = -rng.integers(112, 257, (n, B))
                if n < 16: A[q, g, o[n]] = mid[(q + 1) % N, g + 1, o[n]]
            if (q + g // 2) % 2 == 1: x[q, g] = rng.integers(D - 2, D + 1, B)
            w = (q + g) % 4; a = int(rng.integers(0, B))
            if w < 2: m[q, g] = a
            if w == 1: m[q, g, int(rng.integers(0, B))] = (a + 1) % B
            if w == 2: m[q, g] = rng.choice(np.array([0, a, B - 1]), B)
    return pack(A, v, x, m, gains(rng, 0))
def setup_inputs_calm(rng):
    A = rng.integers(14, 27, (N, 8, 16, B)) * rng.choice(np.array([-1, 1]), (N, 8, 16, B)); A[:, ::2] = -rng.integers(32, 65, (N, 4, 16, B))
    A[:, 1::2, 3::4] = rng.integers(6, 9, (N, 4, 4, B)) * rng.choice(np.array([-1, 1]), (N, 4, 4, B)); A[:, ::2, 3::4] = -rng.integers(10, 14, (N, 4, 4, B))
    A[:, ::2, 11::4] = 2 + ((np.arange(B) + rng.integers(0, 2, (N, 4, 2, 1))) & 1)
    A[:, 1::2, 11::4] = 4 + ((np.arange(B) + rng.integers(0, 2, (N, 4, 2, 1))) & 1)
    v = rng.integers(0, 4, (N, 8, 16, B)); v[:, :, 3::4] = 0
    g0 = 2 * int(rng.integers(0, 4)); g1 = 2 * int(rng.integers(0, 4))
    two = rng.permutation(np.array([1, 2, 4, 5, 6, 9, 10, 12, 13, 14])); i0 = int(two[0]); i1 = int(two[1])
    A[:, g0, i0] = -256; A[:, g0 + 1, i0] = 256
    A[:, g1, i1] = -rng.integers(240, 257, (N, B)); A[:, g1 + 1, i1] = rng.integers(240, 257, (N, B))
    x = rng.integers(1, 5, (N, 8, B))
    for q in range(N):
        for g in range(0, 8, 2): x[q, g] = rng.integers(1, D, B); x[q, g, :B - 1] = sums(rng, S - 1 - (B - 1) + (0, 1, 2, -1)[(q + g // 2) % 4], 1, D - 1, B - 1)
    m = rng.integers(0, B, (N, 8, B))
    u = gains(rng, 0); u = np.sign(u) * (0.875 + 0.125 * np.abs(u))
    row = np.arange(128); full = (row % 8 == 0) | (row % 4 == 3); least = (row % 16 == 11) | (row % 16 == 15)
    low = np.zeros(128, bool); low[[16 * ((g0 + 7) % 8) + i0, 16 * g0 + i0, 16 * (g0 + 1) + i0]] = True
    near = np.zeros(128, bool); near[[16 * ((g1 + 7) % 8) + i1, 16 * (g1 + 1) + i1]] = True
    big = row == 16 * g1 + i1
    rest = ~(full | low | near | big)
    u[:, full] = 2.0 * np.sign(u[:, full]); u[:, least] = 2.5 * np.sign(u[:, least])
    u[:, low] = rng.choice(np.array([-1.0, 1.0]), (N, 3, 1)) * (0.125 + (rng.integers(0, 256, (N, 3, T)) + 0.47) * 2.0 ** -17)
    u[:, near] = 0.125 * np.sign(u[:, near])
    u[:, big] = rng.choice(np.array([-2.5, 2.5]), (N, 1, 1)) * np.where(np.arange(T) == 0, 1.0, -1.0 / (T - 1))
    y = np.mean(reference(**pack(A, v, x, m, u))["yo"].astype(np.float64) ** 2, axis=2)
    aim = (2.0 * T * (S // L) / 72.0) ** 2
    have = np.sum(y[:, ~rest], axis=1) / 128.0; more = np.sum(y[:, rest], axis=1) / 128.0
    c = np.clip(np.sqrt(np.maximum(aim - have, 0.0) / more), 0.125, 2.2)
    u[:, rest] = u[:, rest] * c[:, None, None]
    return pack(A, v, x, m, u)
def check_ranges(d):
    bad = []
    for k, lo, hi in (("am", -256, 256), ("ve", -64, 64), ("du", 1, D), ("mp", 0, B - 1)):
        a = np.asarray(d[k]).astype(np.float64)
        if not (np.min(a) >= lo and np.max(a) <= hi) or np.any(a != np.floor(a)): bad.append("range of " + k)
    u = np.abs(np.asarray(d["gain"]).astype(np.float64))
    if not np.all((u >= 0.125) & (u <= 2.5)): bad.append("range of gain")
    return bad
def reference(am, ve, du, mp, gain):
    A = am.astype(np.float32).astype(np.int64).reshape(N, 8, 16, B); v = ve.astype(np.float32).astype(np.int64).reshape(N, 8, 16, B)
    d = np.stack([gentries(a) for a in du]).astype(np.int64); m = np.stack([gentries(a) for a in mp]).astype(np.int64)
    u = gain.astype(np.float64).reshape(N, 8, 16, T); out = np.zeros((N, 8, 16, L)); n = np.arange(S)
    for t in range(T):
        O = np.add.accumulate(d, axis=2) - d
        seg, ks, ys = [], [], []
        for q in range(N):
            b = np.stack([np.searchsorted(O[q, g], n, side="right") - 1 for g in range(8)])
            k = n - np.take_along_axis(O[q], b, 1)
            w = np.minimum(k * np.take_along_axis(REC[d[q]], b, 1), 256)
            dif = np.roll(A[q], -1, axis=2) - A[q]
            ys.append(256 * np.take_along_axis(A[q], b[:, None, :], 2) + np.take_along_axis(dif, b[:, None, :], 2) * w[:, None, :])
            seg.append(b); ks.append(k)
        A2, v2, d2 = [], [], []
        for r in range(N):
            q = (r + 1 + t % (N - 1)) % N
            X = np.roll(ys[q], -1, axis=0); P = np.roll(O[q], -1, axis=0)
            at = (np.take_along_axis(np.take_along_axis(P, m[r], 1), seg[r], 1) + J * ks[r]) & (S - 1)
            z = (ys[r] * np.take_along_axis(X, at[:, None, :], 2)) * 2.0 ** -30
            out[r] += u[r, :, :, t][:, :, None] * np.add.reduce(np.tanh(z).reshape(8, 16, S // L, L), axis=2)
            if t < T - 1:
                s = np.take_along_axis(X, np.minimum(O[r], S - 1)[:, None, :], 2)
                up = np.add.reduce((s > 256 * A[r]).astype(np.int64), axis=1) >= 9; live = O[r] < S
                nd = np.where(up, np.where(d[r] == D, D - 1, d[r] + 1), np.where(d[r] == 1, 2, d[r] - 1))
                nv = np.clip(v[r] + (s >> 12), -64, 64); na = A[r] + nv
                na = np.where(na > 256, 512 - na, na); na = np.where(na < -256, -512 - na, na)
                d2.append(np.where(live, nd, d[r])); v2.append(np.where(live[:, None, :], nv, v[r])); A2.append(np.where(live[:, None, :], na, A[r]))
        if t < T - 1: A, v, d = np.stack(A2), np.stack(v2), np.stack(d2)
    return {"yo": out.reshape(N, 128, L).astype(np.float32)}

def check_inputs(d):
    bad = list(check_ranges(d))
    if not bad:
        for name, y in reference(**d).items():
            for q in range(N):
                v = np.abs(np.asarray(y[q], np.float64)); s = np.sqrt(np.mean(v * v))
                if v.max() > 12 * s or s < 2.0 ** -4: bad.append('%s of rank %d is uneven or too small' % (name, q))
    return bad

@@ -1,0 +1,616 @@
+import numpy as np
+from concourse.mybir import AluOpType as ALU, ActivationFunctionType as AF
+
+S, B, NB = 4096, 1024, 4
+WIN = 7200
+REC = [0, 256, 128, 85, 64, 51, 42, 36]
+F32, BF, I32, U16 = "float32", "bfloat16", "int32", "uint16"
+OPT = {
+    "ch": [512, 512, 1024, 1024, 1024],
+    "oc": 512,
+    "fold": "aa",
+    "dvn": "a",
+    "gain": ["aaaa", "aaaa", "aaaa", "aava"],
+    "small": "a", "qs": 2, "early": 1, "rounds": 3, "seq": 1, "split": 32, "ny": 2, "emod": "a", "tries": 2500, "seed": 1,
+    "boost": {"walk": -150.0, "lists": -150.0, "table": 300.0, "walka": -150.0, "out": 500.0, "start": 1000.0},
+    "cy": 1.04, "pe": 0.52, "ga": 1.56, "sc": 3.8, "fix": 60, "hop": 140, "bw": 150.0, "bwon": 400.0, "look": 0.5,
+}
+
+
+def _sb(n, dt):
+    return ("sbuf", [128, n], dt)
+
+
+SCRATCH = {
+    "X0": _sb(S + 8, F32), "X1": _sb(S + 8, F32), "X2": _sb(S + 8, F32),
+    "Y0": _sb(S, F32), "Y1": _sb(S, F32), "LUs0": _sb(128, U16), "LUs1": _sb(128, U16), "ds0": _sb(64, BF), "ds1": _sb(64, BF),
+    "I4": _sb(128, F32), "n4kI": _sb(128, BF), "Hq": _sb(256, BF), "Ys": _sb(S, F32), "Z": _sb(S, F32), "inc": _sb(3072, F32),
+    "tab": _sb(2056, F32), "Rr": _sb(B, BF), "rt": _sb(16, BF),
+    "wM": _sb(WIN, BF), "wQ": _sb(WIN, BF), "zer": _sb(2064, BF), "one": _sb(2064, BF), "c192": _sb(512, BF),
+    "A": _sb(B, BF), "As": _sb(B, BF), "v": _sb(B + 16, BF), "F": _sb(B, BF), "cmp": _sb(B, BF), "cl": _sb(B, BF), "c4": _sb(B, F32),
+    "dvn": _sb(448, BF), "Pw": _sb(B, BF), "G": _sb(B, BF), "V": _sb(B, BF),
+    "d": _sb(72, BF), "dl": _sb(4 * 72, BF), "di": _sb(64, I32), "mi": _sb(64, I32), "ma": _sb(64, I32),
+    "mb": _sb(64, I32), "mu": _sb(64, U16), "gn": _sb(4, F32),
+    "IO": _sb(128, F32), "LU": _sb(128, U16), "dj": _sb(64, U16), "LV": _sb(64, U16), "deu": _sb(32, U16),
+    "deb": _sb(64, BF), "dtab": _sb(16, BF), "jm": _sb(28, F32), "jt": _sb(28, F32), "sg": _sb(64, BF), "c2": _sb(64, F32),
+    "rst": _sb(128, BF), "lastc": _sb(8, BF),
+    "Rb": _sb(264, BF), "xf": _sb(256, F32), "xu": _sb(256, U16), "ini": _sb(4, F32),
+    "P": _sb(64, F32), "H": _sb(64, BF), "tH": _sb(64, F32), "lo": _sb(64, BF),
+    "ef": _sb(256, F32), "ei": _sb(256, I32), "ej": _sb(256, I32), "eu0": _sb(256, U16), "eu1": _sb(256, U16), "c77": _sb(256, F32),
+    "II": _sb(144, BF), "nI": _sb(128, BF), "p2I": _sb(128, BF), "n128I": _sb(128, BF),
+    "bl2": _sb(128, BF), "Tri": _sb(128, BF), "TriC": _sb(128, BF), "TrS": _sb(128, BF), "TrSC": _sb(128, BF),
+    "F1": _sb(128, BF), "F2": _sb(128, BF), "W1": _sb(144, BF), "U1": _sb(144, BF), "V1": _sb(144, BF),
+    "Tri4": _sb(128, F32), "TriC4": _sb(128, F32), "Rq": _sb(260, F32),
+    "REP": _sb(2064, BF), "I2": _sb(128, BF),
+    "pi": _sb(4, I32), "pj": _sb(4, I32), "col": _sb(16, F32),
+    "ps": ("psum", [128, 4096], F32),
+}
+SEMAPHORES = ["cv", "ca", "cp", "cg"] + ["s%d" % i for i in range(100)] + ["ax%d" % t for t in range(4)] + ["ad%d" % t for t in range(4)]
+PLANNED = []
+ORDER = {}
+SIZE = {F32: 4, BF: 2, I32: 4, U16: 2}
+
+
+def bits(m):
+    return bin(m).count("1")
+
+
+def hits(a, b):
+    return a[0] == b[0] and a[1] < b[2] and b[1] < a[2]
+
+
+def plan(ops):
+    n = len(ops)
+    acc = {}
+    for k, o in enumerate(ops):
+        deps = set(o["after"])
+        for lst, isw in ((o["rs"], False), (o["ws"], True)):
+            for sp in lst:
+                for asp, aw, j in acc.get(sp[0], []):
+                    if (aw or isw) and hits(sp, asp):
+                        deps.add(j)
+        for sp in o["ws"]:
+            acc[sp[0]] = [x for x in acc.get(sp[0], []) if not (sp[1] <= x[0][1] and x[0][2] <= sp[2])] + [(sp, True, k)]
+        for sp in o["rs"]:
+            acc.setdefault(sp[0], []).append((sp, False, k))
+        o["deps"] = deps
+    succ = [[] for _ in ops]
+    for k, o in enumerate(ops):
+        for j in o["deps"]:
+            succ[j].append(k)
+    lev = [0.0] * n
+    for k in range(n - 1, -1, -1):
+        lev[k] = ops[k]["cost"] + ops[k]["lat"] + ops[k]["wire"] + max([lev[j] for j in succ[k]] + [0.0])
+    lev = [lev[k] + OPT["boost"].get(ops[k]["tag"], 0.0) for k in range(n)]
+    if OPT["seq"]:
+        lev = [OPT["boost"].get(ops[k]["tag"], 0.0) - k for k in range(n)]
+        for k in range(n - 1, -1, -1):
+            lev[k] = max([lev[k]] + [lev[j] + 1e-3 for j in succ[k]])
+    dur = [o["cost"] + o["lat"] + o["wire"] for o in ops]
+    hold = []
+    for o in ops:
+        h = [(o["e"], 0.0, o["cost"])] if o["cost"] else []
+        h += [(b, 0.0, o["cost"] + (0 if o["e"] == "p" else 100)) for b in o["banks"]]
+        if o["wire"]:
+            h.append(("link", o["cost"] + o["lat"], o["wire"]))
+        hold.append(h)
+    pred = [sorted(o["deps"]) for o in ops]
+
+    def place(prio, back):
+        before, after = (succ, pred) if back else (pred, succ)
+        left = [len(x) for x in before]
+        ready = [0.0] * n
+        start = [0.0] * n
+        busy = {}
+        free = [k for k in range(n) if not left[k]]
+        while free:
+            k = max(free, key=lambda j: prio[j])
+            free.remove(k)
+            hs = [(r, dur[k] - a - w if back else a, w) for r, a, w in hold[k]]
+            t = ready[k]
+            moved = True
+            while moved:
+                moved = False
+                for r, a, w in hs:
+                    line = busy.setdefault(r, [])
+                    i, j = 0, len(line)
+                    while i < j:
+                        m = (i + j) // 2
+                        if line[m][1] > t + a + 1e-6:
+                            j = m
+                        else:
+                            i = m + 1
+                    while i < len(line) and line[i][0] < t + a + w - 1e-6:
+                        t = line[i][1] - a
+                        moved = len(hs) > 1
+                        i += 1
+            for r, a, w in hs:
+                busy[r].append((t + a, t + a + w))
+                busy[r].sort()
+            start[k] = t
+            for j in after[k]:
+                ready[j] = max(ready[j], t + dur[k])
+                left[j] -= 1
+                if not left[j]:
+                    free.append(j)
+        return start, max(start[k] + dur[k] for k in range(n))
+
+    start, span = place(lev, False)
+    best = (span, start)
+    for _ in range(OPT["rounds"]):
+        back, _s = place([start[k] + dur[k] for k in range(n)], True)
+        start, span = place([back[k] + dur[k] for k in range(n)], False)
+        if span < best[0]:
+            best = (span, start)
+    rnd = np.random.RandomState(OPT["seed"])
+    for it in range(OPT["tries"]):
+        width = (300.0, 1000.0, 3000.0)[it % 3]
+        lo = rnd.rand() * best[0]
+        prio = [-best[1][k] + (width * rnd.randn() if lo - 15000 < best[1][k] < lo + 15000 else 0.0) for k in range(n)]
+        start, span = place(prio, False)
+        if it % 4 == 3:
+            back, _s = place([start[k] + dur[k] for k in range(n)], True)
+            start, span = place([back[k] + dur[k] for k in range(n)], False)
+        if span <= best[0]:
+            best = (span, start)
+    PLANNED.append(best[0])
+    return sorted(range(n), key=lambda k: (best[1][k], k))
+
+
+def rank_program(g, core, T, topo):
+    rank = T.rank_of(core)
+    if rank is None:
+        return
+    n_r = len(T.cores)
+    Q = {"v": g.vector, "a": g.scalar, "p": g.tensor, "s": g.sync, "g": g}
+    csem = {"v": "cv", "a": "ca", "p": "cp", "g": "cg"}
+    kind = {k: SCRATCH[k][2] for k in SCRATCH}
+    kind.update({"am": BF, "ve": BF, "du": I32, "mp": I32, "gain": F32, "yo": F32})
+    ops = []
+    nsem = [0]
+    tag = ["start"]
+    cy, fix, hop = OPT["cy"], OPT["fix"], OPT["hop"]
+    CH = OPT["ch"]
+
+    def R(name, a=None, b=None, s=1, p=None):
+        t = T[name]
+        a0 = 0 if a is None else a
+        b0 = t.shape[1] if b is None else b
+        rows = slice(None) if p is None else slice(p[0], p[1])
+        return (t[rows, a0:b0:s] if s != 1 else t[rows, a0:b0], name, a0, b0, None, len(range(a0, b0, s)))
+
+    def PS(bank, a=0, b=512, s=1):
+        return R("ps", 512 * bank + a, 512 * bank + b, s)
+
+    def IND(win, off):
+        return (win[0].indirect(off[0]), win[1], win[2], win[3], off, 16 * off[5])
+
+    def ap(x):
+        return x[0] if isinstance(x, tuple) else x
+
+    def newsem():
+        nsem[0] += 1
+        return "s%d" % (nsem[0] - 1)
+
+    def rec(e, fns, reads, writes, cost, lat=hop, wire=0.0, tok=None, after=(), pre=None):
+        reads = [x for x in reads if isinstance(x, tuple)]
+        reads = reads + [x[4] for x in reads + list(writes) if x[4] is not None]
+        rs, ws = [x[1:4] for x in reads], [x[1:4] for x in writes]
+        banks = set(b for x in rs + ws if x[0] == "ps" for b in range(x[1] // 512, (x[2] + 511) // 512))
+        ops.append({"e": e, "fns": fns, "rs": rs, "ws": ws, "cost": cost, "lat": lat, "wire": wire, "tok": tok,
+                    "after": list(after), "banks": banks, "pre": pre, "tag": tag[0]})
+        return len(ops) - 1
+
+    def price(o, i, base):
+        if o[4] is not None:
+            return fix + o[5] * OPT["sc"] * cy
+        if i[4] is not None:
+            return fix + o[5] * OPT["ga"] * cy
+        return fix + max(64, o[5] * base) * cy
+
+    def half(*xs):
+        return 0.5 if all(SIZE[kind[x[1]]] == 2 for x in xs) else 1.0
+
+    def dma(e, pairs, add=False, after=(), pre=None):
+        s = newsem()
+        if add:
+            fns = [lambda o=o, i=i: Q[e].dma_start(o[0], i[0], accum_op=ALU.add).then_inc(T.sem[s], 16) for o, i in pairs]
+        else:
+            fns = [lambda o=o, i=i: Q[e].dma_start(o[0], i[0]).then_inc(T.sem[s], 16) for o, i in pairs]
+        by = max(o[5] * SIZE[kind[o[1]]] for o, i in pairs) * 128 * (2 if add else 1)
+        rec(e, fns, [p[1] for p in pairs], [p[0] for p in pairs], len(pairs) * (1000 if e == "g" else 60), 1900 + by / 500.0,
+            tok=(s, 16 * len(pairs)), after=after, pre=pre)
+
+    def turn(o, i, a=None, b=None, c=None, d=None):
+        return [(R(o, a, b, p=(16, 128)), R(i, c, d, p=(0, 112))), (R(o, a, b, p=(0, 16)), R(i, c, d, p=(112, 128)))]
+
+    def back(o, i, n):
+        return [(R(o, 0, n, p=(0, 112)), R(i, p=(16, 128))), (R(o, 0, n, p=(112, 128)), R(i, p=(0, 16)))]
+
+    def cp(o, i):
+        rec("v", [lambda: g.vector.tensor_copy(o[0], i[0])], [i], [o], price(o, i, half(o, i)))
+
+    def tt(o, a, b, f):
+        rec("v", [lambda: g.vector.tensor_tensor(o[0], a[0], b[0], f)], [a, b], [o], price(o, a, 1 if "ps" in (a[1], b[1]) else 2))
+
+    def ts(o, a, s1, f0, s2=None, f1=None):
+        if f1 is None:
+            fn = lambda: g.vector.tensor_scalar(o[0], a[0], ap(s1), None, f0)
+        else:
+            fn = lambda: g.vector.tensor_scalar(o[0], a[0], ap(s1), ap(s2), f0, f1)
+        rec("v", [fn], [a, s1, s2], [o], price(o, a, half(o, a)))
+
+    def scan(o, a, b, ini, f0, f1):
+        rec("v", [lambda: g.vector.tensor_tensor_scan(o[0], a[0], b[0], ap(ini), f0, f1)], [a, b, ini], [o], price(o, a, 1))
+
+    def ms(o, c):
+        rec("v", [lambda: g.vector.memset(o[0], c)], [], [o], price(o, o, half(o)))
+
+    def act(o, i, f=AF.Copy, bias=None, scale=1.0):
+        if bias is None:
+            fn = lambda: g.scalar.activation(o[0], i[0], f, scale=ap(scale))
+        else:
+            fn = lambda: g.scalar.activation(o[0], i[0], f, bias=ap(bias), scale=ap(scale))
+        rec("a", [fn], [i, bias, scale], [o], price(o, i, 1))
+
+    def lin(e, o, i, mul, add):
+        if e == "a":
+            act(o, i, AF.Identity, bias=add, scale=mul)
+        else:
+            ts(o, i, mul, ALU.mult, add, ALU.add)
+
+    def group(items):
+        last = len(items) - 1
+        fns = [lambda k=k, o=o, l=l, r=r: g.tensor.matmul(o[0], l[0], r[0], k == 0, k == last) for k, (o, l, r) in enumerate(items)]
+        cost = sum(max(64, r[5]) * OPT["pe"] * (4 if kind[r[1]] == F32 else 1) for o, l, r in items)
+        rec("p", fns, [x for o, l, r in items for x in (l, r)], [o for o, l, r in items], cost)
+
+    def sel(o, i, pat, cmp_op, base, cm):
+        rec("g", [lambda: g.affine_select(o[0], i[0], pat, cmp_op, 0.0, base, cm)], [i], [o], 170 + 2 * o[5] * cy)
+
+    def partner(t):
+        return T.cores[(rank + 1 + t % (n_r - 1)) % n_r]
+
+    def client(t):
+        return T.cores[(rank - 1 - t % (n_r - 1)) % n_r]
+
+    def send(t, o, i, rsem, ltok, guard=()):
+        dst = client(t)
+        rid, pid, _ = topo.addr(dst)
+        m = topo.mask(core, dst)
+        bw = OPT["bwon"] if topo.chip(dst) == topo.chip(core) else OPT["bw"]
+        return rec("g", [lambda: g.remote_dma(o[0], i[0], T.sem[rsem], T.sem[ltok[0]], pid, rid, m)], [i], list(guard), 700, 1000,
+                   wire=i[5] * SIZE[kind[i[1]]] * 128 / bw, tok=ltok)
+
+    def landed(t, o, rsem, sends):
+        rec("r", [], [], [o], 0, 1000, tok=(rsem, len(sends) * bits(topo.mask(partner(t), core))), after=sends)
+
+    I, SB = R("II", 0, 128), R("II", 16, 144)
+    nI, p2I, n128I = R("nI"), R("p2I"), R("n128I")
+    XB = ["X0", "X1", "X2", "X0"]
+    d, dprev = R("d", 8, 72), R("d", 7, 71)
+    sm = OPT["small"]
+
+    def col(k):
+        return R("col", k, k + 1)
+
+    def start():
+        dma("s", back("di", "du", 64))
+        dma("s", back("A", "am", B))
+        dma("s", back("v", "ve", B))
+        dma("s", [(R("As"), R("am"))])
+        dma("s", [(R("mi"), R("mp")), (R("gn"), R("gain"))])
+        one = R("one", 0, 128)
+        ms(one, 1.0)
+        ms(R("wM", 0, 4112), 1.0)
+        ms(R("zer", 0, B), 0.0)
+        ms(R("zer", B, 2064), 0.0)
+        ms(R("one", 128, 2064), 1.0)
+        rec("g", [lambda: g.iota(T.pi[:, 0:1], [[1, 1]], 0, 1)], [], [R("pi")], 140)
+        rec("g", [lambda: g.iota(T.jm[:], [[16, 28]], -448, 0, allow_small_or_imprecise_dtypes=True)], [], [R("jm")], 200)
+        sel(I, one, [[-1, 128]], ALU.is_equal, 0, 1)
+        sel(R("bl2"), one, [[-16, 8], [0, 16]], ALU.is_ge, 0, 1)
+        sel(R("bl2"), R("bl2"), [[16, 8], [0, 16]], ALU.is_ge, 15, -1)
+        sel(R("Tri"), R("bl2"), [[1, 128]], ALU.is_ge, 0, -1)
+        sel(R("TriC"), R("bl2"), [[-1, 128]], ALU.is_gt, 0, 1)
+        sel(R("TrS"), R("bl2"), [[1, 128]], ALU.is_gt, 0, -1)
+        sel(R("TrSC"), R("bl2"), [[-1, 128]], ALU.is_ge, 0, 1)
+        sel(R("I2"), one, [[-1, 16], [-16, 8]], ALU.is_equal, 0, 1)
+        ms(R("d", 0, 8), 0.0)
+        cp(d, R("di"))
+        ms(R("W1"), 0.0)
+        ts(R("W1", 15, 143, 16), R("II", 0, 128, 16), -1.0, ALU.mult)
+        ms(R("rst"), 1.0)
+        ms(R("rst", 0, 128, 64), 0.0)
+        ts(R("pj", 0, 1), R("pi", 0, 1), 15, ALU.bitwise_and)
+        cp(col(0), R("pj", 0, 1))
+        ts(R("lastc", 0, 1), col(0), 15.0, ALU.is_equal)
+        ms(R("rt", 0, 1), 0.0)
+        ms(R("rt", 8, 16), 0.0)
+        for k in range(1, 8):
+            ms(R("rt", k, k + 1), REC[k] / 256.0)
+        ts(nI, I, -1.0, ALU.mult)
+        tt(R("F1"), R("Tri"), R("TrS"), ALU.add)
+        tt(R("F2"), R("TriC"), R("TrSC"), ALU.add)
+        ms(R("Rb", 0, 1), 0.0)
+        ms(R("tab", 2048, 2056), 0.0)
+        cp(R("II", 128, 144), R("II", 0, 16))
+        ts(p2I, I, 2.0, ALU.mult)
+        ts(n128I, I, -128.0, ALU.mult)
+        ms(R("c192"), -192.0)
+        ms(col(2), 191.5 + 2.0 ** -13)
+        for x in XB[:3]:
+            ms(R(x, S, S + 8), 0.0)
+        for t in range(NB):
+            ms(R("dl", 72 * t, 72 * t + 8), 0.0)
+        ms(R("deb", 0, 36), 0.0)
+        if OPT["dvn"] == "a":
+            ms(R("v", B, B + 16), 0.0)
+            ts(R("jm"), R("jm"), col(0), ALU.add)
+        else:
+            ms(R("dtab"), 0.0)
+            ms(R("dtab", 1, 2), -1.0)
+        ms(R("V1"), 0.0)
+        cp(R("V1", 15, 127, 16), R("bl2", 16, 128, 16))
+        cp(R("V1", 127, 128), R("bl2", 0, 1))
+        if OPT["emod"] == "a":
+            act(R("I4"), I)
+            act(R("n4kI"), I, AF.Copy, scale=-4096.0)
+            ms(col(8), 127.5 + 2.0 ** -13)
+        act(R("Tri4"), R("Tri"))
+        act(R("TriC4"), R("TriC"))
+        ms(R("Rq", 0, 4), 0.0)
+        ts(col(3), col(0), 1.0, ALU.is_equal, 64.0, ALU.mult)
+        ts(col(4), col(0), 2.0, ALU.is_equal, col(3), ALU.add)
+        ts(col(5), col(0), 3.0, ALU.is_equal, -77.0, ALU.mult)
+        tt(col(6), col(4), col(5), ALU.add)
+        ts(col(7), col(0), 77.0, ALU.mult, -1232.0, ALU.add)
+        ms(R("U1"), 0.0)
+        ts(R("U1", 15, 143, 16), R("bl2", 0, 128, 16), col(6), ALU.mult)
+        ms(R("c77"), 1232.0)
+        act(R("Pw"), R("zer", 0, B))
+        act(R("REP"), R("zer"))
+        act(R("REP", 8, 2056, 16), R("I2"))
+        ts(R("ma"), R("mi"), 15, ALU.bitwise_and)
+        ts(R("mb"), R("mi"), 4, ALU.logical_shift_right)
+        ts(R("ma"), R("ma"), 64.0, ALU.mult)
+        tt(R("mb"), R("ma"), R("mb"), ALU.add)
+        cp(R("mu"), R("mb"))
+
+    def refill(w, src):
+        dma("s", [(R(w, 0, 2056), R(src, 0, 2056)), (R(w, 2056, 4112), R(src, 0, 2056))])
+
+    def lists(t):
+        o = R("dl", 72 * t + 8, 72 * t + 72)
+        landed(t, o, "ad%d" % t, [send(t, o, d, "ad%d" % t, (newsem(), bits(topo.mask(core, client(t)))))])
+        group([(PS(4, 0, 64), R("Tri"), d), (PS(4, 0, 64), R("TriC"), dprev), (PS(4, 63, 64), I, R("lastc", 0, 1))])
+        group([(PS(4, 64, 128), R("TrS"), d), (PS(4, 64, 128), R("TrSC"), dprev)])
+        group([(PS(4, 128, 192), I, d)])
+        scan(R("IO"), R("rst"), PS(4, 0, 128), 0.0, ALU.mult, ALU.add)
+        cp(R("LU", 0, 64), R("IO", 0, 64))
+        cp(R("dj"), PS(4, 128, 192))
+        act(R("Rr"), IND(R("rt"), R("dj")))
+
+        def places(a, b):
+            s2 = PS(4, 384, 384 + b - a)
+            group([(PS(5, a, b), R("W1", 15 - i, 143 - i), R("wM", 16 + 16 * a + i, 16 + 16 * b, 16)) for i in range(16)])
+            act(R("Rb", 1 + a, 1 + b), PS(5, a, b), AF.Identity, bias=1.0)
+            group([(s2, R("F1"), R("Rb", 1 + a, 1 + b)), (s2, R("F2"), R("Rb", a, b))])
+            scan(R("xf", a, b), s2, R("zer", 0, b - a), 0.0 if a == 0 else R("xf", a - 1, a), ALU.add, ALU.add)
+            cp(R("xu", a, b), R("xf", a, b))
+
+        c = OPT["split"]
+        if c:
+            cp(IND(R("wM", 16, WIN), R("LU", 0, c)), R("zer", 0, 16 * c))
+            ts(R("LV", c, 64), R("IO", c, 64), -16.0 * c, ALU.add)
+            places(0, c)
+            cp(IND(R("wM", 16 + 16 * c, WIN), R("LV", c, 64)), R("zer", 0, B - 16 * c))
+            places(c, 128)
+        else:
+            cp(IND(R("wM", 16, WIN), R("LU", 0, 64)), R("zer", 0, B))
+            places(0, 128)
+        places(128, 256)
+        tag[0] = "late"
+        ts(R("LU", 64, 128), R("IO", 64, 128), 4096.0, ALU.min)
+        dma("s", turn("LUs%d" % (t % 2), "LU") + turn("ds%d" % (t % 2), "d", None, None, 8, 72))
+        if t < NB - 1:
+            ts(R("deb", 36, 64), R("IO", 100, 128), 4096.0, ALU.is_ge)
+            if OPT["dvn"] == "a":
+                tt(R("jt"), R("deb", 36, 64), R("jm"), ALU.mult)
+                ts(R("deu", 0, 28), R("jt"), 1024.0, ALU.add)
+                act(R("dvn"), IND(R("v"), R("deu", 0, 28)), AF.Copy, scale=-1.0)
+            else:
+                ts(R("deu", 0, 28), R("IO", 100, 128), 4096.0, ALU.is_ge)
+                tt(R("dvn"), IND(R("dtab"), R("deu", 0, 28)), R("v", 576, B), ALU.mult)
+
+    def table(t):
+        act(R("tab", 1, 2047, 2), R("A", 1, B))
+        act(R("tab", 2047, 2048), R("A", 0, 1))
+        group([(PS(0), nI, R("A", 0, 512)), (PS(0), I, R("A", 1, 513))])
+        group([(PS(1), nI, R("A", 512, B)), (PS(1, 0, 511), I, R("A", 513, B)), (PS(1, 511, 512), I, R("A", 0, 1))])
+        tt(R("tab", 0, 2048, 2), R("ps", 0, B), R("Rr"), ALU.mult)
+        tt(R("ini", 0, 1), R("A", 0, 1), R("tab", 0, 1), ALU.subtract)
+
+    edges = [sum(CH[:k]) for k in range(len(CH) + 1)]
+    ytok, ysend = {}, {}
+    ring = [0]
+
+    def make_y(t):
+        ytok[t] = (newsem(), len(CH) * bits(topo.mask(core, client(t))))
+        ysend[t] = []
+        y = "Y%d" % (t % OPT["ny"])
+        for k in range(len(CH)):
+            a, b = edges[k], edges[k + 1]
+            o = 1024 * (ring[0] % 3)
+            ring[0] += 1
+            act(R("inc", o, o + b - a), IND(R("tab"), R("xu", a // 16, b // 16)))
+            scan(R(y, a, b), R("wM", 16 + a, 16 + b), R("inc", o, o + b - a), R("ini", 0, 1) if k == 0 else R(y, a - 1, a), ALU.mult, ALU.add)
+            guard = [R(XB[0], 0, S)] if t == 2 and k == len(CH) - 1 else []
+            ysend[t].append(send(t, R(XB[t], a, b), R(y, a, b), "ax%d" % t, ytok[t], guard))
+        landed(t, R(XB[t], 0, S), "ax%d" % t, ysend[t])
+
+    def y_turn(t, early):
+        for k in range(4):
+            late = k >= early
+            dma("s", turn("Ys", "Y%d" % (t % OPT["ny"]), 1024 * k, 1024 * k + 1024, 1024 * k, 1024 * k + 1024),
+                after=ysend[t] if late else (), pre=ytok[t] if late else None)
+
+    def reading(t):
+        group([(PS(6, 0, 64), R("TrS"), R("dl", 72 * t + 8, 72 * t + 72)), (PS(6, 0, 64), R("TrSC"), R("dl", 72 * t + 7, 72 * t + 71))])
+        scan(R("P"), PS(6, 0, 64), R("zer", 0, 64), 0.0, ALU.add, ALU.add)
+        lin(sm, R("H"), R("P"), 1 / 64.0, 128.0)
+        lin(sm, R("tH"), R("H"), -64.0, 8192.0)
+        tt(R("lo"), R("P"), R("tH"), ALU.add)
+        dma("s", [((T.Pw[1:128:16, :],) + R("Pw")[1:], R("H")), ((T.Pw[2:128:16, :],) + R("Pw")[1:], R("lo"))])
+        act(R("G"), IND(R("Pw"), R("mu")))
+        rows = [(PS(6, i, 512, 16), R("REP", 5 + 128 * i, 133 + 128 * i), R("ds%d" % (t % 2), 0, 32)) for i in range(16)]
+        group([(PS(6), nI, R("G", 0, 512)), (PS(6), I, R("G", 1, 513))] + rows)
+        rows = [(PS(7, i, 512 if i < 15 else 496, 16), R("REP", 5 + 128 * i, 133 + 128 * i), R("ds%d" % (t % 2), 32, 64 if i < 15 else 63)) for i in range(16)]
+        group([(PS(7), nI, R("G", 512, B)), (PS(7, 0, 511), I, R("G", 513, B)), (PS(7, 511, 512), I, R("G", B - 1, B))] + rows)
+        act(R("V"), R("ps", 3072, 4096))
+        refill("wQ", "zer")
+        w = 64 // OPT["qs"]
+        for c in range(0, 64, w):
+            cp(IND(R("wQ", 16, WIN), R("LUs%d" % (t % 2), c, c + w)), R("V", 16 * c, 16 * (c + w)))
+        cp(R("wQ", 16, 17), R("G", 0, 1))
+        group([(PS(6, 0, 256), R("U1", 15 - i, 143 - i), R("wQ", 16 + i, 16 + S, 16)) for i in range(16)])
+        act(R("Rq", 4, 260), PS(6, 0, 256))
+        group([(PS(7, 0, 256), R("Tri4"), R("Rq", 4, 260)), (PS(7, 0, 256), R("TriC4"), R("Rq", 3, 259))])
+        scan(R("ef"), PS(7, 0, 256), R("c77"), col(7), ALU.add, ALU.add)
+        if OPT["emod"] == "v":
+            cp(R("ei"), R("ef"))
+            ts(R("ej"), R("ei"), S - 1, ALU.bitwise_and)
+            cp(R("eu%d" % (t % 2)), R("ej"))
+        else:
+            act(R("Hq"), R("ef"), AF.Identity, bias=col(8), scale=1 / 4096.0)
+            group([(PS(6, 0, 256), R("I4"), R("ef")), (PS(6, 0, 256), R("n4kI"), R("Hq"))])
+            ts(R("eu%d" % (t % 2)), PS(6, 0, 256), 128.0 * 4096.0, ALU.add)
+
+    def output(t):
+        last = t == NB - 1
+        cuts = list(range(0, S + 1, OPT["oc"]))
+        if last:
+            cuts = sorted(set(cuts + [S - 512]))
+        stores = [1024, 2048, 3072, 3584, S] if last else [2048, S]
+        done = 0
+        for a, b in zip(cuts[:-1], cuts[1:]):
+            z = R("Z", a, b)
+            tt(z, IND(R(XB[t], 0, S), R("eu%d" % (t % 2), a // 16, b // 16)), R("Ys", a, b), ALU.mult)
+            act(z, z, AF.Tanh, scale=2.0 ** -14)
+            if OPT["gain"][t][a // 1024] == "a" and not (last and b == S):
+                act(z, z, AF.Copy, scale=R("gn", t, t + 1))
+            else:
+                ts(z, z, R("gn", t, t + 1), ALU.mult)
+            if b in stores:
+                dma("s" if t == 0 else "g", [(R("yo", done, b), R("Z", done, b))], add=t > 0)
+                done = b
+
+    def walk(t):
+        xw = R(XB[t], 0, S + 8)
+        at = R("LUs%d" % (t % 2), 64, 128)
+        tt(R("cmp"), IND(xw, at), R("As"), ALU.is_gt)
+        act(R("F"), IND(xw, at), AF.Identity, bias=col(2), scale=1 / 16.0)
+        group([(PS(4, 192, 256), n128I, R("deb"))] + [(PS(4, 192, 256), R("V1", 15 - i, 143 - i), R("cmp", i, B, 16)) for i in range(16)])
+        act(R("sg"), PS(4, 192, 256), AF.Sign, bias=-8.5)
+        o1, o2 = PS(4, 256, 320), PS(4, 320, 384)
+        group([(o1, I, d), (o1, I, R("deb")), (o1, I, R("sg"))])
+        group([(o2, p2I, d), (o2, p2I, R("deb")), (o2, p2I, R("sg"))])
+        ts(R("c2"), o2, 2.0, ALU.max, 14.0, ALU.min)
+        tt(d, R("c2"), o1, ALU.subtract)
+        tag[0] = "walka"
+        for h in range(2):
+            a, b = 512 * h, 512 * h + 512
+            group([(PS(h), I, R("c192")), (PS(h), I, R("v", a, b)), (PS(h), SB, R("F", a, b))])
+            ts(R("v", a, b), PS(h), -64.0, ALU.max, 64.0, ALU.min)
+        for h in range(2):
+            a, b = 512 * h, 512 * h + 512
+            dead = [(PS(3, 64, 512), I, R("dvn"))] if h else []
+            group([(PS(2 + h), I, R("A", a, b))] + dead + [(PS(2 + h), I, R("v", a, b))])
+            if OPT["fold"][h] == "v":
+                ts(R("cl", a, b), PS(2 + h), -256.0, ALU.max, 256.0, ALU.min)
+                dead = [(PS(3, 64, 512), nI, R("dvn"))] if h else []
+                group([(PS(2 + h), nI, R("A", a, b))] + dead + [(PS(2 + h), nI, R("v", a, b)), (PS(2 + h), p2I, R("cl", a, b))])
+                act(R("A", a, b), PS(2 + h))
+            else:
+                c = R("c4", a, b)
+                act(c, PS(2 + h), AF.Abs, bias=256.0, scale=-1.0)
+                act(c, c, AF.Abs, bias=512.0, scale=-1.0)
+        for h in range(2):
+            if OPT["fold"][h] == "a":
+                act(R("A", 512 * h, 512 * h + 512), R("c4", 512 * h, 512 * h + 512), AF.Identity, bias=-256.0)
+        if t + 1 < NB - 1:
+            dma("s", turn("As", "A"))
+
+    start()
+    for t in range(NB):
+        tag[0] = "lists"
+        lists(t)
+        tag[0] = "table"
+        table(t)
+        tag[0] = "y"
+        make_y(t)
+        if t < NB - 1:
+            refill("wM", "one")
+        tag[0] = "read"
+        reading(t)
+        tag[0] = "out"
+        if t > 0:
+            output(t - 1)
+        y_turn(t, OPT["early"] if t == NB - 1 else 0)
+        if t < NB - 1:
+            tag[0] = "walk"
+            walk(t)
+    output(NB - 1)
+
+    cnt = {"v": 0, "a": 0, "p": 0, "g": 0}
+    known = {e: {} for e in Q}
+    total = {}
+    acc = {}
+
+    def wait(e, tok):
+        if known[e].get(tok[0], 0) < tok[1]:
+            Q[e].wait_ge(T.sem[tok[0]], tok[1])
+            known[e][tok[0]] = tok[1]
+
+    def whole(sp):
+        return (sp[0], sp[1] // 512 * 512, (sp[2] + 511) // 512 * 512) if sp[0] == "ps" else sp
+
+    key = tuple((o["e"], o["cost"], o["wire"]) for o in ops)
+    if key not in ORDER:
+        ORDER[key] = plan(ops)
+    for k in ORDER[key]:
+        o = ops[k]
+        e = o["e"]
+        rs, ws = [whole(x) for x in o["rs"]], [whole(x) for x in o["ws"]]
+        if e != "r":
+            need = {}
+            for lst, isw in ((rs, False), (ws, True)):
+                for sp in lst:
+                    for asp, aw, ae, tok in acc.get(sp[0], []):
+                        if hits(sp, asp):
+                            if sp[0] == "ps":
+                                if ae == e and (e == "p" or not (aw or isw)):
+                                    continue
+                            elif not (aw or isw):
+                                continue
+                            need[tok[0]] = max(need.get(tok[0], 0), tok[1])
+            if o["pre"]:
+                wait(e, o["pre"])
+            for s in need:
+                wait(e, (s, need[s]))
+        tok = o["tok"]
+        for fn in o["fns"]:
+            if tok is None:
+                cnt[e] += 1
+                fn().then_inc(T.sem[csem[e]], 1)
+            else:
+                fn()
+        tok = tok or (csem[e], cnt[e])
+        for sp in ws:
+            acc[sp[0]] = [x for x in acc.get(sp[0], []) if not (sp[1] <= x[0][1] and x[0][2] <= sp[2])] + [(sp, True, e, tok)]
+        for sp in rs:
+            acc[sp[0]] = [x for x in acc.get(sp[0], []) if x[1] or x[3][0] != tok[0] or not (sp[1] <= x[0][1] and x[0][2] <= sp[2])] + [(sp, False, e, tok)]
+        total[tok[0]] = max(total.get(tok[0], 0), tok[1])
+    for s in total:
+        if max(known[e].get(s, 0) for e in known) < total[s]:
+            wait("g", (s, total[s]))

@@ -2,19 +2,27 @@ import numpy as np
 from concourse.mybir import AluOpType as ALU, ActivationFunctionType as AF
 
 S, B, NB = 4096, 1024, 4
-WIN = 7200
-REC = [0, 256, 128, 85, 64, 51, 42, 36]
+WIN = 7216
 F32, BF, I32, U16 = "float32", "bfloat16", "int32", "uint16"
 OPT = {
     "ch": [512, 512, 1024, 1024, 1024],
+    "ways": [[(1024, "M", 0), (2048, "P", 0), (3072, "M", 0), (4096, "P", 0)],
+             [(1024, "D", 0), (2048, "D", 0), (3072, "D", 1), (4096, "D", 1)],
+             [(1024, "M", 0), (2048, "M", 0), (3072, "P", 1), (4096, "P", 1)],
+             [(512, "M", 0), (1024, "M", 0), (2048, "M", 0), (3072, "D", 0), (4096, "D", 0)]],
+    "npe": 1024,
     "oc": 512,
-    "fold": "aa",
-    "dvn": "a",
-    "gain": ["aaaa", "aaaa", "aaaa", "aava"],
-    "small": "a", "qs": 2, "early": 1, "rounds": 3, "seq": 1, "split": 32, "ny": 2, "emod": "a", "tries": 2500, "seed": 1,
-    "boost": {"walk": -150.0, "lists": -150.0, "table": 300.0, "walka": -150.0, "out": 500.0, "start": 1000.0},
-    "cy": 1.04, "pe": 0.52, "ga": 1.56, "sc": 3.8, "fix": 60, "hop": 140, "bw": 150.0, "bwon": 400.0, "look": 0.5,
+    "gain": ["aaaa", "aaaa", "aaaa", "aaaa"],
+    "banks": {"L": 0, "M": [0, 1, 0], "Q": 2, "W": [3, 4, 5]},
+    "evA": "aa", "evD": "aa", "evO": "aa", "cont": 0, "nys": 1, "early": 1, "rounds": 6, "seq": 1, "flow": 0, "look": 300.0, "tries": 6000, "seed": 1,
+    "weigh": {},
+    "boost": {"upd": 0.0, "lists": 0.0, "table": 0.0, "y": 0.0, "serve": 0.0, "late": -60.0, "read": -150.0, "out": -100.0, "start": 0.0, "start2": -150.0},
+    "fig": {"cy": 1.04, "pe": 0.52, "ga": 1.56, "sc": 3.8, "fix": 60, "hop": 120, "bw": 140.0, "bwon": 350.0, "lbw": 600.0, "row": 30.0,
+            "far": 750.0, "wake": 300.0, "call": 600.0},
+    "cases": [{}, {"bw": 70.0, "wake": 600.0, "call": 900.0}, {"cy": 0.88, "pe": 0.45, "ga": 1.2, "sc": 2.2}, {"cy": 1.2, "pe": 0.62, "ga": 1.9, "sc": 5.2}],
 }
+XB = ["X0", "X1", "X2", "X0"]
+HB = ["X0", "X1", "X2", "Y0"]
 
 
 def _sb(n, dt):
@@ -22,31 +30,29 @@ def _sb(n, dt):
 
 
 SCRATCH = {
-    "X0": _sb(S + 8, F32), "X1": _sb(S + 8, F32), "X2": _sb(S + 8, F32),
-    "Y0": _sb(S, F32), "Y1": _sb(S, F32), "LUs0": _sb(128, U16), "LUs1": _sb(128, U16), "ds0": _sb(64, BF), "ds1": _sb(64, BF),
-    "I4": _sb(128, F32), "n4kI": _sb(128, BF), "Hq": _sb(256, BF), "Ys": _sb(S, F32), "Z": _sb(S, F32), "inc": _sb(3072, F32),
-    "tab": _sb(2056, F32), "Rr": _sb(B, BF), "rt": _sb(16, BF),
-    "wM": _sb(WIN, BF), "wQ": _sb(WIN, BF), "zer": _sb(2064, BF), "one": _sb(2064, BF), "c192": _sb(512, BF),
-    "A": _sb(B, BF), "As": _sb(B, BF), "v": _sb(B + 16, BF), "F": _sb(B, BF), "cmp": _sb(B, BF), "cl": _sb(B, BF), "c4": _sb(B, F32),
-    "dvn": _sb(448, BF), "Pw": _sb(B, BF), "G": _sb(B, BF), "V": _sb(B, BF),
-    "d": _sb(72, BF), "dl": _sb(4 * 72, BF), "di": _sb(64, I32), "mi": _sb(64, I32), "ma": _sb(64, I32),
-    "mb": _sb(64, I32), "mu": _sb(64, U16), "gn": _sb(4, F32),
-    "IO": _sb(128, F32), "LU": _sb(128, U16), "dj": _sb(64, U16), "LV": _sb(64, U16), "deu": _sb(32, U16),
-    "deb": _sb(64, BF), "dtab": _sb(16, BF), "jm": _sb(28, F32), "jt": _sb(28, F32), "sg": _sb(64, BF), "c2": _sb(64, F32),
-    "rst": _sb(128, BF), "lastc": _sb(8, BF),
-    "Rb": _sb(264, BF), "xf": _sb(256, F32), "xu": _sb(256, U16), "ini": _sb(4, F32),
-    "P": _sb(64, F32), "H": _sb(64, BF), "tH": _sb(64, F32), "lo": _sb(64, BF),
-    "ef": _sb(256, F32), "ei": _sb(256, I32), "ej": _sb(256, I32), "eu0": _sb(256, U16), "eu1": _sb(256, U16), "c77": _sb(256, F32),
-    "II": _sb(144, BF), "nI": _sb(128, BF), "p2I": _sb(128, BF), "n128I": _sb(128, BF),
-    "bl2": _sb(128, BF), "Tri": _sb(128, BF), "TriC": _sb(128, BF), "TrS": _sb(128, BF), "TrSC": _sb(128, BF),
-    "F1": _sb(128, BF), "F2": _sb(128, BF), "W1": _sb(144, BF), "U1": _sb(144, BF), "V1": _sb(144, BF),
-    "Tri4": _sb(128, F32), "TriC4": _sb(128, F32), "Rq": _sb(260, F32),
-    "REP": _sb(2064, BF), "I2": _sb(128, BF),
-    "pi": _sb(4, I32), "pj": _sb(4, I32), "col": _sb(16, F32),
+    "X0": _sb(S, F32), "X1": _sb(S, F32), "X2": _sb(S, F32), "Y0": _sb(S + 8, F32), "Y1": _sb(S + 8, F32),
+    "Ys0": _sb(S, F32), "Z": _sb(3072, F32), "Tr": _sb(1536, F32), "inc": _sb(3072, F32), "tab": _sb(2056, F32),
+    "W0": _sb(WIN, BF), "W1": _sb(WIN, BF), "zer": _sb(2064, BF), "one": _sb(128, BF), "c192": _sb(512, BF),
+    "A": _sb(B, BF), "v": _sb(B + 16, BF), "cmp": _sb(B, BF), "cl": _sb(B, BF), "D": _sb(B, F32), "dvn": _sb(448, BF),
+    "mA": _sb(3 * 1088, BF), "cA": _sb(3 * 1088, BF), "F": _sb(3 * B, BF), "cF": _sb(3 * B, BF),
+    "sg": _sb(3 * 64, BF), "csg": _sb(3 * 64, BF), "LU": _sb(64, U16), "LUs": _sb(3 * 64, U16), "cLU": _sb(3 * 64, U16),
+    "hl": _sb(4 * 128, BF), "chl": _sb(4 * 128, BF),
+    "OH0": _sb(8 + 1056, BF), "OH1": _sb(8 + 1056, BF), "LP0": _sb(34, U16), "LP1": _sb(34, U16), "ot": _sb(16, BF), "Pw": _sb(B, BF), "G": _sb(8 + B, BF), "val": _sb(528, BF),
+    "d": _sb(80, BF), "di": _sb(64, I32), "mi": _sb(64, I32), "ma": _sb(64, I32), "mb": _sb(64, I32), "mu": _sb(64, U16), "gn": _sb(4, F32),
+    "IO": _sb(98, F32), "dj": _sb(64, U16), "deu": _sb(32, U16), "jm": _sb(28, F32), "jt": _sb(28, F32),
+    "c2": _sb(64, F32), "rst": _sb(98, BF), "cv": _sb(8, BF), "Rb": _sb(264, BF), "xu": _sb(256, U16),
+    "Cq": _sb(264, F32), "Hq": _sb(256, BF), "eu0": _sb(256, U16), "eu1": _sb(256, U16), "c38": _sb(256, BF),
+    "II": _sb(144, BF), "nI": _sb(128, BF), "p2I": _sb(128, BF), "n2I": _sb(128, BF), "n128I": _sb(128, BF), "n2kI": _sb(128, BF),
+    "bl2": _sb(128, BF), "B8": _sb(128, BF), "TrS": _sb(128, BF), "TrSC": _sb(128, BF), "TP": _sb(512, BF),
+    "F1": _sb(128, BF), "F2": _sb(128, BF), "V1": _sb(144, BF), "Tri4": _sb(144, F32), "TriC4": _sb(144, F32),
+    "J": _sb(160, BF), "TB": _sb(160, BF), "TM": _sb(14 * 128, BF), "mk": _sb(16, F32),
+    "WR": _sb(128, BF), "WJ": _sb(128, BF), "WL": _sb(128, BF), "MA": _sb(128, BF), "MB": _sb(128, BF), "ME": _sb(128, BF), "MO": _sb(128, BF),
+    "Gd": _sb(512, F32), "pi": _sb(4, I32), "pj": _sb(4, I32), "col": _sb(24, F32),
     "ps": ("psum", [128, 4096], F32),
 }
-SEMAPHORES = ["cv", "ca", "cp", "cg"] + ["s%d" % i for i in range(100)] + ["ax%d" % t for t in range(4)] + ["ad%d" % t for t in range(4)]
+SEMAPHORES = ["cv", "ca", "cp", "cg"] + ["s%d" % i for i in range(112)] + ["r%d" % i for i in range(24)] + ["x%d" % t for t in range(NB)]
 PLANNED = []
+DEBUG = []
 ORDER = {}
 SIZE = {F32: 4, BF: 2, I32: 4, U16: 2}
 
@@ -78,23 +84,57 @@ def plan(ops):
     for k, o in enumerate(ops):
         for j in o["deps"]:
             succ[j].append(k)
-    lev = [0.0] * n
-    for k in range(n - 1, -1, -1):
-        lev[k] = ops[k]["cost"] + ops[k]["lat"] + ops[k]["wire"] + max([lev[j] for j in succ[k]] + [0.0])
-    lev = [lev[k] + OPT["boost"].get(ops[k]["tag"], 0.0) for k in range(n)]
+    times = [[timing(o, dict(OPT["fig"], **m)) for o in ops] for m in OPT["cases"]]
+    dur = [x[0] + x[1] + max(x[2], x[3]) + x[4] for x in times[0]]
     if OPT["seq"]:
         lev = [OPT["boost"].get(ops[k]["tag"], 0.0) - k for k in range(n)]
         for k in range(n - 1, -1, -1):
             lev[k] = max([lev[k]] + [lev[j] + 1e-3 for j in succ[k]])
-    dur = [o["cost"] + o["lat"] + o["wire"] for o in ops]
+    else:
+        lev = [0.0] * n
+        for k in range(n - 1, -1, -1):
+            lev[k] = dur[k] * OPT["weigh"].get(ops[k]["tag"], 1.0) + max([lev[j] for j in succ[k]] + [0.0])
     hold = []
-    for o in ops:
-        h = [(o["e"], 0.0, o["cost"])] if o["cost"] else []
-        h += [(b, 0.0, o["cost"] + (0 if o["e"] == "p" else 100)) for b in o["banks"]]
-        if o["wire"]:
-            h.append(("link", o["cost"] + o["lat"], o["wire"]))
+    for o, x in zip(ops, times[0]):
+        h = [(o["e"], 0.0, x[0])] if x[0] else []
+        h += [(b, 0.0, x[0] + (0 if o["e"] == "p" else 100)) for b in o["banks"]]
+        if x[2]:
+            h.append(("dma", x[0] + x[1], x[2]))
+        if x[3]:
+            h.append((o["move"][2], x[0] + x[1], x[3]))
         hold.append(h)
     pred = [sorted(o["deps"]) for o in ops]
+
+    def replay(order, tm):
+        done, at = [0.0] * n, {}
+        for k in order:
+            o, x = ops[k], tm[k]
+            e = o["e"]
+            t = max([at.get(e, 0.0) if x[0] else 0.0] + [done[j] for j in pred[k]])
+            for b in o["banks"]:
+                u = at.get(b)
+                if u and u[0] != e:
+                    t = max(t, u[1])
+            t += x[0]
+            if x[0]:
+                at[e] = t
+            t += x[1]
+            if x[2]:
+                t = max(t, at.get("dma", 0.0))
+                at["dma"] = t + x[2]
+            end = t + x[2]
+            if x[3]:
+                r = o["move"][2]
+                at[r] = max(t, at.get(r, 0.0)) + x[3]
+                end = max(end, at[r])
+            done[k] = end + x[4]
+            for b in o["banks"]:
+                at[b] = (e, done[k])
+        return max(done)
+
+    def judge(start):
+        order = sorted(range(n), key=lambda k: (start[k], k))
+        return [replay(order, tm) for tm in times]
 
     def place(prio, back):
         before, after = (succ, pred) if back else (pred, succ)
@@ -135,31 +175,120 @@ def plan(ops):
                     free.append(j)
         return start, max(start[k] + dur[k] for k in range(n))
 
-    start, span = place(lev, False)
-    best = (span, start)
+    def flow(prio, look):
+        left = [len(x) for x in pred]
+        ready = [0.0] * n
+        start = [0.0] * n
+        at = {}
+        free = {}
+        for k in range(n):
+            if not left[k]:
+                free.setdefault(ops[k]["e"], []).append(k)
+        for _ in range(n):
+            pick = None
+            for e, line in free.items():
+                if line:
+                    can = [max([ready[k]] + [at.get(r, 0.0) - a for r, a, w in hold[k]]) for k in line]
+                    t = min(can)
+                    if pick is None or t < pick[0]:
+                        pick = (t, e, can)
+            t, e, can = pick
+            i = max((i for i in range(len(can)) if can[i] <= t + look), key=lambda i: prio[free[e][i]])
+            k = free[e].pop(i)
+            start[k] = can[i]
+            for r, a, w in hold[k]:
+                at[r] = can[i] + a + w
+            for j in succ[k]:
+                ready[j] = max(ready[j], can[i] + dur[k])
+                left[j] -= 1
+                if not left[j]:
+                    free.setdefault(ops[j]["e"], []).append(j)
+        return start, max(start[k] + dur[k] for k in range(n))
+
+    start, span = flow(lev, OPT["look"]) if OPT["flow"] else place(lev, False)
+    base = judge(start)
+
+    def score(start):
+        return sum(a / b for a, b in zip(judge(start), base))
+
+    best = (score(start), start, span)
     for _ in range(OPT["rounds"]):
         back, _s = place([start[k] + dur[k] for k in range(n)], True)
         start, span = place([back[k] + dur[k] for k in range(n)], False)
-        if span < best[0]:
-            best = (span, start)
+        best = min(best, (score(start), start, span))
     rnd = np.random.RandomState(OPT["seed"])
     for it in range(OPT["tries"]):
         width = (300.0, 1000.0, 3000.0)[it % 3]
-        lo = rnd.rand() * best[0]
+        lo = rnd.rand() * best[2]
         prio = [-best[1][k] + (width * rnd.randn() if lo - 15000 < best[1][k] < lo + 15000 else 0.0) for k in range(n)]
-        start, span = place(prio, False)
+        start, span = flow(prio, OPT["look"] * 2 * rnd.rand()) if OPT["flow"] > 1 and it % 2 == 0 else place(prio, False)
         if it % 4 == 3:
             back, _s = place([start[k] + dur[k] for k in range(n)], True)
             start, span = place([back[k] + dur[k] for k in range(n)], False)
-        if span <= best[0]:
-            best = (span, start)
-    PLANNED.append(best[0])
+        best = min(best, (score(start), start, span))
+    PLANNED.append([round(x / 1000.0, 1) for x in [best[2]] + judge(best[1])])
+    DEBUG.append((ops, dur, best[1]))
     return sorted(range(n), key=lambda k: (best[1][k], k))
+
+
+def timing(o, p):
+    c = o["cost"]
+    busy = c[0] + p["cy"] * (c[1] + c[2] * p["ga"] + c[3] * p["sc"]) + c[4] * p["pe"]
+    if o["move"] is None:
+        return (busy, 0.0, 0.0, 0.0, p["hop"])
+    kind, by, link = o["move"]
+    if kind == "local":
+        return (busy, 900.0, by / p["lbw"] + 8 * p["row"] * link, 0.0, 900.0 + p["hop"])
+    if kind == "landed":
+        return (0.0, 0.0, 0.0, 0.0, p["far"] + p["wake"])
+    wire = by / p["bw"] if link else 0.0
+    if kind == "onward":
+        return (0.0, 2 * p["far"] + p["wake"] + p["call"], 0.0, wire, 0.0)
+    return (p["call"], p["far"], by / (300.0 if link else p["bwon"]) + (16 if link else 8) * p["row"], wire, p["hop"])
+
+
+def helpers(core, dst, T, topo):
+    every = range(128)
+    idle = [c for c in every if c not in T.cores and topo.die(c) == topo.die(core)]
+    far = [c for c in idle if topo.mates(topo.chip(c), topo.chip(dst)) and topo.may_write(c, dst)] if topo.chip(dst) != topo.chip(core) else []
+    if not far:
+        return {"D": []}
+    near = [c for c in idle if topo.chip(c) == topo.chip(core)]
+    out = [c for c in near if topo.may_write(c, far[0])][0]
+    return {"D": [], "P": [[c for c in near if c != out][0]], "M": [out, far[0]]}
+
+
+def pieces(t):
+    a = 0
+    for k, (b, way, late) in enumerate(OPT["ways"][t]):
+        yield k, a, b, way, late
+        a = b
+
+
+def handing_on(g, core, T, topo):
+    n_r = len(T.cores)
+    left = 0
+    for t in range(NB):
+        for k, a, b, way, late in pieces(t):
+            for r, src in enumerate(T.cores):
+                dst = T.cores[(r - 1 - t % (n_r - 1)) % n_r]
+                stops = [src] + helpers(src, dst, T, topo)[way] + [dst]
+                if core in stops:
+                    i = stops.index(core)
+                    to = stops[i + 1]
+                    rid, pid, _ = topo.addr(to)
+                    g.wait_ge(T.sem["s%d" % (8 * t + k)], bits(topo.mask(stops[i - 1], core)))
+                    g.remote_dma(T[XB[t] if to == dst else HB[t]][:, a:b], T[HB[t]][:, a:b], T.sem["x%d" % t if to == dst else "s%d" % (8 * t + k)],
+                                 T.sem["cg"], pid, rid, topo.mask(core, to))
+                    left += bits(topo.mask(core, to))
+    if left:
+        g.wait_ge(T.sem["cg"], left)
 
 
 def rank_program(g, core, T, topo):
     rank = T.rank_of(core)
     if rank is None:
+        handing_on(g, core, T, topo)
         return
     n_r = len(T.cores)
     Q = {"v": g.vector, "a": g.scalar, "p": g.tensor, "s": g.sync, "g": g}
@@ -167,17 +296,25 @@ def rank_program(g, core, T, topo):
     kind = {k: SCRATCH[k][2] for k in SCRATCH}
     kind.update({"am": BF, "ve": BF, "du": I32, "mp": I32, "gain": F32, "yo": F32})
     ops = []
-    nsem = [0]
+    nsem = [0, 0]
     tag = ["start"]
-    cy, fix, hop = OPT["cy"], OPT["fix"], OPT["hop"]
+    now = [0]
+    fix = OPT["fig"]["fix"]
     CH = OPT["ch"]
+    NPE = OPT["npe"]
+    BK = OPT["banks"]
 
     def R(name, a=None, b=None, s=1, p=None):
+        if name in ("OH", "LP"):
+            name += str(now[0] % 2)
         t = T[name]
         a0 = 0 if a is None else a
         b0 = t.shape[1] if b is None else b
         rows = slice(None) if p is None else slice(p[0], p[1])
         return (t[rows, a0:b0:s] if s != 1 else t[rows, a0:b0], name, a0, b0, None, len(range(a0, b0, s)))
+
+    def RS(name, a, n, s):
+        return R(name, a, a + (n - 1) * s + 1, s)
 
     def PS(bank, a=0, b=512, s=1):
         return R("ps", 512 * bank + a, 512 * bank + b, s)
@@ -192,21 +329,21 @@ def rank_program(g, core, T, topo):
         nsem[0] += 1
         return "s%d" % (nsem[0] - 1)
 
-    def rec(e, fns, reads, writes, cost, lat=hop, wire=0.0, tok=None, after=(), pre=None):
+    def rec(e, fns, reads, writes, cost, move=None, tok=None, after=(), pre=None):
         reads = [x for x in reads if isinstance(x, tuple)]
         reads = reads + [x[4] for x in reads + list(writes) if x[4] is not None]
         rs, ws = [x[1:4] for x in reads], [x[1:4] for x in writes]
         banks = set(b for x in rs + ws if x[0] == "ps" for b in range(x[1] // 512, (x[2] + 511) // 512))
-        ops.append({"e": e, "fns": fns, "rs": rs, "ws": ws, "cost": cost, "lat": lat, "wire": wire, "tok": tok,
+        ops.append({"e": e, "fns": fns, "rs": rs, "ws": ws, "cost": cost, "move": move, "tok": tok,
                     "after": list(after), "banks": banks, "pre": pre, "tag": tag[0]})
         return len(ops) - 1
 
     def price(o, i, base):
         if o[4] is not None:
-            return fix + o[5] * OPT["sc"] * cy
+            return (fix, 0, 0, o[5], 0)
         if i[4] is not None:
-            return fix + o[5] * OPT["ga"] * cy
-        return fix + max(64, o[5] * base) * cy
+            return (fix, 0, o[5], 0, 0)
+        return (fix, max(64, o[5] * base), 0, 0, 0)
 
     def half(*xs):
         return 0.5 if all(SIZE[kind[x[1]]] == 2 for x in xs) else 1.0
@@ -217,8 +354,8 @@ def rank_program(g, core, T, topo):
             fns = [lambda o=o, i=i: Q[e].dma_start(o[0], i[0], accum_op=ALU.add).then_inc(T.sem[s], 16) for o, i in pairs]
         else:
             fns = [lambda o=o, i=i: Q[e].dma_start(o[0], i[0]).then_inc(T.sem[s], 16) for o, i in pairs]
-        by = max(o[5] * SIZE[kind[o[1]]] for o, i in pairs) * 128 * (2 if add else 1)
-        rec(e, fns, [p[1] for p in pairs], [p[0] for p in pairs], len(pairs) * (1000 if e == "g" else 60), 1900 + by / 500.0,
+        by = sum(int(np.prod(i[0].shape)) * SIZE[kind[o[1]]] for o, i in pairs) * (2 if add else 1)
+        rec(e, fns, [p[1] for p in pairs], [p[0] for p in pairs], (len(pairs) * (1000 if e == "g" else 60), 0, 0, 0, 0), ("local", by, len(pairs)),
             tok=(s, 16 * len(pairs)), after=after, pre=pre)
 
     def turn(o, i, a=None, b=None, c=None, d=None):
@@ -233,40 +370,47 @@ def rank_program(g, core, T, topo):
     def tt(o, a, b, f):
         rec("v", [lambda: g.vector.tensor_tensor(o[0], a[0], b[0], f)], [a, b], [o], price(o, a, 1 if "ps" in (a[1], b[1]) else 2))
 
-    def ts(o, a, s1, f0, s2=None, f1=None):
+    def ts(o, a, s1, f0, s2=None, f1=None, also=()):
         if f1 is None:
             fn = lambda: g.vector.tensor_scalar(o[0], a[0], ap(s1), None, f0)
         else:
             fn = lambda: g.vector.tensor_scalar(o[0], a[0], ap(s1), ap(s2), f0, f1)
-        rec("v", [fn], [a, s1, s2], [o], price(o, a, half(o, a)))
+        rec("v", [fn], [a, s1, s2] + list(also), [o], price(o, a, half(o, a)))
 
-    def scan(o, a, b, ini, f0, f1):
-        rec("v", [lambda: g.vector.tensor_tensor_scan(o[0], a[0], b[0], ap(ini), f0, f1)], [a, b, ini], [o], price(o, a, 1))
+    def scan(o, a, b, ini, f0, f1, after=(), pre=None):
+        rec("v", [lambda: g.vector.tensor_tensor_scan(o[0], a[0], b[0], ap(ini), f0, f1)], [a, b, ini], [o], price(o, a, 1), after=after, pre=pre)
 
     def ms(o, c):
         rec("v", [lambda: g.vector.memset(o[0], c)], [], [o], price(o, o, half(o)))
 
-    def act(o, i, f=AF.Copy, bias=None, scale=1.0):
+    def act(o, i, f=AF.Copy, bias=None, scale=1.0, also=()):
         if bias is None:
             fn = lambda: g.scalar.activation(o[0], i[0], f, scale=ap(scale))
         else:
             fn = lambda: g.scalar.activation(o[0], i[0], f, bias=ap(bias), scale=ap(scale))
-        rec("a", [fn], [i, bias, scale], [o], price(o, i, 1))
+        rec("a", [fn], [i, bias, scale] + list(also), [o], price(o, i, 1))
 
-    def lin(e, o, i, mul, add):
+    def mul(e, o, i, c):
         if e == "a":
-            act(o, i, AF.Identity, bias=add, scale=mul)
+            act(o, i, AF.Copy, scale=c)
         else:
-            ts(o, i, mul, ALU.mult, add, ALU.add)
+            ts(o, i, c, ALU.mult)
 
-    def group(items):
-        last = len(items) - 1
-        fns = [lambda k=k, o=o, l=l, r=r: g.tensor.matmul(o[0], l[0], r[0], k == 0, k == last) for k, (o, l, r) in enumerate(items)]
-        cost = sum(max(64, r[5]) * OPT["pe"] * (4 if kind[r[1]] == F32 else 1) for o, l, r in items)
-        rec("p", fns, [x for o, l, r in items for x in (l, r)], [o for o, l, r in items], cost)
+    def group(items, first=True, last=True, hold=()):
+        end = len(items) - 1
+        fns = [lambda k=k, o=o, l=l, r=r: g.tensor.matmul(o[0], l[0], r[0], first and k == 0, last and k == end) for k, (o, l, r) in enumerate(items)]
+        cost = (0, 0, 0, 0, sum(max(64, r[5]) * (4 if kind[r[1]] == F32 else 1) for o, l, r in items))
+        rec("p", fns, [x for o, l, r in items for x in (l, r)], [o for o, l, r in items] + list(hold), cost)
 
     def sel(o, i, pat, cmp_op, base, cm):
-        rec("g", [lambda: g.affine_select(o[0], i[0], pat, cmp_op, 0.0, base, cm)], [i], [o], 170 + 2 * o[5] * cy)
+        rec("g", [lambda: g.affine_select(o[0], i[0], pat, cmp_op, 0.0, base, cm)], [i], [o], (170, 2 * o[5], 0, 0, 0))
+
+    def iota(o, pat, base, cm):
+        if kind[o[1]] == I32:
+            fn = lambda: g.iota(o[0], pat, base, cm)
+        else:
+            fn = lambda: g.iota(o[0], pat, base, cm, allow_small_or_imprecise_dtypes=True)
+        rec("g", [fn], [], [o], (130, 2 * o[5], 0, 0, 0))
 
     def partner(t):
         return T.cores[(rank + 1 + t % (n_r - 1)) % n_r]
@@ -274,292 +418,373 @@ def rank_program(g, core, T, topo):
     def client(t):
         return T.cores[(rank - 1 - t % (n_r - 1)) % n_r]
 
-    def send(t, o, i, rsem, ltok, guard=()):
-        dst = client(t)
+    def send(dst, o, i, rsem, ltok, guard=(), after=()):
         rid, pid, _ = topo.addr(dst)
         m = topo.mask(core, dst)
-        bw = OPT["bwon"] if topo.chip(dst) == topo.chip(core) else OPT["bw"]
-        return rec("g", [lambda: g.remote_dma(o[0], i[0], T.sem[rsem], T.sem[ltok[0]], pid, rid, m)], [i], list(guard), 700, 1000,
-                   wire=i[5] * SIZE[kind[i[1]]] * 128 / bw, tok=ltok)
+        link = None if topo.chip(dst) == topo.chip(core) else "port"
+        return rec("g", [lambda: g.remote_dma(o[0], i[0], T.sem[rsem], T.sem[ltok[0]], pid, rid, m)], [i], list(guard), (0, 0, 0, 0, 0),
+                   ("remote", i[5] * SIZE[kind[i[1]]] * 128, link), tok=ltok, after=after)
 
-    def landed(t, o, rsem, sends):
-        rec("r", [], [], [o], 0, 1000, tok=(rsem, len(sends) * bits(topo.mask(partner(t), core))), after=sends)
+    def landed(o, rsem, count, sends):
+        rec("r", [], [], [o], (0, 0, 0, 0, 0), ("landed", 0, None), tok=(rsem, count), after=sends)
+
+    def newr():
+        nsem[1] += 1
+        return "r%d" % (nsem[1] - 1)
+
+    small = ("s0", sum(bits(topo.mask(core, client(t))) * (4 if t < NB - 1 else 1) + bits(topo.mask(core, partner(t))) * (2 if t < NB - 1 else 0) for t in range(NB)))
+    nsem[0] = 1
+
+    def post(dst, src, o, i, guard=()):
+        r = newr()
+        k = send(dst, o, i, r, small, guard)
+        landed(o, r, bits(topo.mask(src, core)), [k])
+        return k
 
     I, SB = R("II", 0, 128), R("II", 16, 144)
-    nI, p2I, n128I = R("nI"), R("p2I"), R("n128I")
-    XB = ["X0", "X1", "X2", "X0"]
+    nI, p2I, n2I, n128I = R("nI"), R("p2I"), R("n2I"), R("n128I")
     d, dprev = R("d", 8, 72), R("d", 7, 71)
-    sm = OPT["small"]
+    L = BK["L"]
+    wide = [0]
+
+    def wbank():
+        wide[0] += 1
+        return BK["W"][wide[0] % len(BK["W"])]
 
     def col(k):
         return R("col", k, k + 1)
 
+    def TS(s):
+        if s < 0:
+            return R("TM", 128 * (-s - 1), 128 * -s)
+        if s > 8:
+            return R("TM", 128 * (22 - s), 128 * (23 - s))
+        return R("TB", 15 - s, 143 - s)
+
     def start():
         dma("s", back("di", "du", 64))
         dma("s", back("A", "am", B))
-        dma("s", back("v", "ve", B))
-        dma("s", [(R("As"), R("am"))])
-        dma("s", [(R("mi"), R("mp")), (R("gn"), R("gain"))])
-        one = R("one", 0, 128)
+        dma("s", [(R("mA", 64, 1088), R("am"))])
+        one = R("one")
         ms(one, 1.0)
-        ms(R("wM", 0, 4112), 1.0)
-        ms(R("zer", 0, B), 0.0)
-        ms(R("zer", B, 2064), 0.0)
-        ms(R("one", 128, 2064), 1.0)
-        rec("g", [lambda: g.iota(T.pi[:, 0:1], [[1, 1]], 0, 1)], [], [R("pi")], 140)
-        rec("g", [lambda: g.iota(T.jm[:], [[16, 28]], -448, 0, allow_small_or_imprecise_dtypes=True)], [], [R("jm")], 200)
-        sel(I, one, [[-1, 128]], ALU.is_equal, 0, 1)
+        ms(R("zer"), 0.0)
+        ms(R("W0", 0, 544), 0.0)
+        dma("s", [(R("W0", 544, 2064), R("zer", 0, 1520)), (R("W0", 2064, 4128), R("zer"))])
+        iota(R("pi", 0, 1), [[1, 1]], 0, 1)
+        iota(R("J"), [[1, 160]], 0, 0)
         sel(R("bl2"), one, [[-16, 8], [0, 16]], ALU.is_ge, 0, 1)
         sel(R("bl2"), R("bl2"), [[16, 8], [0, 16]], ALU.is_ge, 15, -1)
-        sel(R("Tri"), R("bl2"), [[1, 128]], ALU.is_ge, 0, -1)
-        sel(R("TriC"), R("bl2"), [[-1, 128]], ALU.is_gt, 0, 1)
+        for f in range(2):
+            sel(R("TP", 128 * f, 128 * f + 128), R("bl2"), [[16, 8], [2, 16]], ALU.is_gt, -16 * f, -1)
+            sel(R("TP", 256 + 128 * f, 384 + 128 * f), R("bl2"), [[-16, 8], [-2, 16]], ALU.is_ge, 16 * f, 1)
+        sel(I, one, [[-1, 128]], ALU.is_equal, 0, 1)
         sel(R("TrS"), R("bl2"), [[1, 128]], ALU.is_gt, 0, -1)
         sel(R("TrSC"), R("bl2"), [[-1, 128]], ALU.is_ge, 0, 1)
-        sel(R("I2"), one, [[-1, 16], [-16, 8]], ALU.is_equal, 0, 1)
-        ms(R("d", 0, 8), 0.0)
+        sel(R("Tri4", 16, 144), R("bl2"), [[1, 128]], ALU.is_ge, 0, -1)
+        sel(R("TriC4", 16, 144), R("bl2"), [[-1, 128]], ALU.is_gt, 0, 1)
+        ms(R("d"), 0.0)
         cp(d, R("di"))
-        ms(R("W1"), 0.0)
-        ts(R("W1", 15, 143, 16), R("II", 0, 128, 16), -1.0, ALU.mult)
+        cp(R("dj"), R("di"))
+        ts(R("pj", 0, 1), R("pi", 0, 1), 7, ALU.bitwise_and)
+        ts(R("pj", 1, 2), R("pi", 0, 1), 15, ALU.bitwise_and)
+        ts(R("pj", 2, 3), R("pi", 0, 1), 8, ALU.bitwise_and)
+        cp(R("col", 0, 3), R("pj", 0, 3))
+        ts(col(3), col(0), 0.0, ALU.is_equal)
+        ts(R("ot"), R("J", 0, 16), col(0), ALU.is_equal, col(3), ALU.max)
+        ts(R("ot", 0, 1), col(0), 2.0, ALU.is_equal, col(3), ALU.max)
+        ts(R("ot", 8, 9), col(0), 6.0, ALU.is_equal, col(3), ALU.max)
+        for oh in ("OH0", "OH1"):
+            act(R(oh, 0, 8), R("zer", 0, 8))
+            ts(R(oh, 1032, 1064), R("J", 0, 32), 0.0, ALU.is_equal, col(3), ALU.mult)
         ms(R("rst"), 1.0)
-        ms(R("rst", 0, 128, 64), 0.0)
-        ts(R("pj", 0, 1), R("pi", 0, 1), 15, ALU.bitwise_and)
-        cp(col(0), R("pj", 0, 1))
-        ts(R("lastc", 0, 1), col(0), 15.0, ALU.is_equal)
-        ms(R("rt", 0, 1), 0.0)
-        ms(R("rt", 8, 16), 0.0)
-        for k in range(1, 8):
-            ms(R("rt", k, k + 1), REC[k] / 256.0)
+        ms(R("rst", 33, 34), 0.0)
+        ts(R("cv", 0, 1), col(1), 1.0, ALU.add)
+        ms(R("cv", 1, 2), 8192.0)
+        ts(col(4), R("pi", 0, 1), col(2), ALU.subtract, 15.0, ALU.add)
+        ts(R("TB"), R("J"), col(4), ALU.is_equal, 0.5, ALU.mult)
+        ts(R("mk", 0, 7), R("J", 1, 8), col(0), ALU.is_le)
+        ts(R("mk", 7, 14), R("J", 1, 8), col(0), ALU.is_gt)
+        for s in range(1, 8):
+            mul("va"[s % 2], TS(-s), R("TB", 15 + s, 143 + s), R("mk", s - 1, s))
+            mul("av"[s % 2], TS(16 - s), R("TB", s - 1, 127 + s), R("mk", 6 + s, 7 + s))
         ts(nI, I, -1.0, ALU.mult)
-        tt(R("F1"), R("Tri"), R("TrS"), ALU.add)
-        tt(R("F2"), R("TriC"), R("TrSC"), ALU.add)
-        ms(R("Rb", 0, 1), 0.0)
-        ms(R("tab", 2048, 2056), 0.0)
+        tt(R("F1"), R("Tri4", 16, 144), R("TrS"), ALU.add)
+        tt(R("F2"), R("TriC4", 16, 144), R("TrSC"), ALU.add)
+        ms(R("Rb", 0, 8), 0.0)
+        ms(R("tab", 0, 2), 0.0)
+        ms(R("tab", 2050, 2056), 0.0)
+        ts(col(5), col(3), 1024.0, ALU.mult, col(0), ALU.add)
+        rec("v", [lambda: g.vector.reciprocal(col(6)[0], col(5)[0])], [col(5)], [col(6)], (200, 6, 0, 0, 0))
+        ts(col(6), col(6), 256.0, ALU.mult, -0.49, ALU.add)
+        cp(R("pj", 3, 4), col(6))
+        ts(col(7), R("pj", 3, 4), 1 / 512.0, ALU.mult)
+        ts(col(8), col(0), -1.0, ALU.mult, col(7), ALU.mult)
+        ts(col(9), col(3), -0.5, ALU.mult, 0.5, ALU.add)
+        tt(col(9), col(9), col(8), ALU.add)
+        tt(col(8), col(9), col(7), ALU.add)
+        mul("a", R("WR"), R("bl2"), col(7))
+        mul("a", R("WJ"), R("bl2"), col(8))
+        mul("a", R("WL"), R("bl2"), col(9))
+        for y in ("Y0", "Y1"):
+            ms(R(y, S, S + 8), 0.0)
+        tag[0] = "start2"
+        dma("s", back("v", "ve", B))
+        dma("s", back("mi", "mp", 64) + [(R("gn"), R("gain"))])
+        dma("s", [(R("W1", 0, 2064), R("zer")), (R("W1", 2064, 4128), R("zer"))])
+        iota(R("jm"), [[16, 28]], -448, 0)
+        sel(R("B8"), one, [[-8, 16], [0, 8]], ALU.is_ge, 0, 1)
+        sel(R("B8"), R("B8"), [[8, 16], [0, 8]], ALU.is_ge, 7, -1)
         cp(R("II", 128, 144), R("II", 0, 16))
-        ts(p2I, I, 2.0, ALU.mult)
-        ts(n128I, I, -128.0, ALU.mult)
+        mul("a", p2I, I, 2.0)
+        mul("a", n2I, I, -2.0)
+        mul("a", n128I, I, -128.0)
+        mul("a", R("n2kI"), I, -2048.0)
         ms(R("c192"), -192.0)
-        ms(col(2), 191.5 + 2.0 ** -13)
-        for x in XB[:3]:
-            ms(R(x, S, S + 8), 0.0)
-        for t in range(NB):
-            ms(R("dl", 72 * t, 72 * t + 8), 0.0)
-        ms(R("deb", 0, 36), 0.0)
-        if OPT["dvn"] == "a":
-            ms(R("v", B, B + 16), 0.0)
-            ts(R("jm"), R("jm"), col(0), ALU.add)
-        else:
-            ms(R("dtab"), 0.0)
-            ms(R("dtab", 1, 2), -1.0)
+        ms(col(10), 191.5 + 2.0 ** -13)
+        ms(col(11), 127.5 + 2.0 ** -13 - 77.0 / 4096)
+        ms(R("v", B, B + 16), 0.0)
+        ts(R("jm"), R("jm"), col(1), ALU.add)
         ms(R("V1"), 0.0)
         cp(R("V1", 15, 127, 16), R("bl2", 16, 128, 16))
         cp(R("V1", 127, 128), R("bl2", 0, 1))
-        if OPT["emod"] == "a":
-            act(R("I4"), I)
-            act(R("n4kI"), I, AF.Copy, scale=-4096.0)
-            ms(col(8), 127.5 + 2.0 ** -13)
-        act(R("Tri4"), R("Tri"))
-        act(R("TriC4"), R("TriC"))
-        ms(R("Rq", 0, 4), 0.0)
-        ts(col(3), col(0), 1.0, ALU.is_equal, 64.0, ALU.mult)
-        ts(col(4), col(0), 2.0, ALU.is_equal, col(3), ALU.add)
-        ts(col(5), col(0), 3.0, ALU.is_equal, -77.0, ALU.mult)
-        tt(col(6), col(4), col(5), ALU.add)
-        ts(col(7), col(0), 77.0, ALU.mult, -1232.0, ALU.add)
-        ms(R("U1"), 0.0)
-        ts(R("U1", 15, 143, 16), R("bl2", 0, 128, 16), col(6), ALU.mult)
-        ms(R("c77"), 1232.0)
-        act(R("Pw"), R("zer", 0, B))
-        act(R("REP"), R("zer"))
-        act(R("REP", 8, 2056, 16), R("I2"))
+        cp(R("Tri4", 0, 16), R("Tri4", 128, 144))
+        cp(R("TriC4", 0, 16), R("TriC4", 128, 144))
+        ms(R("Cq", 0, 8), 0.0)
+        ms(R("c38"), 38.5)
+        ms(R("G", 0, 8), 0.0)
+        ms(R("val", 512, 528), 0.0)
+        tt(R("MB"), R("B8"), I, ALU.subtract)
+        tt(R("MA"), I, R("MB"), ALU.subtract)
+        ts(col(12), col(2), 51.0 / 8, ALU.mult, -64.0, ALU.add)
+        tt(col(12), col(12), col(0), ALU.mult)
+        mul("a", R("ME"), I, col(12))
+        ms(R("MO"), 0.0)
+        ts(R("MO", 0, 128, 8), R("B8", 0, 128, 8), col(12), ALU.mult)
+        dma("s", [(R("Pw"), R("zer", 0, B))])
         ts(R("ma"), R("mi"), 15, ALU.bitwise_and)
         ts(R("mb"), R("mi"), 4, ALU.logical_shift_right)
         ts(R("ma"), R("ma"), 64.0, ALU.mult)
         tt(R("mb"), R("ma"), R("mb"), ALU.add)
         cp(R("mu"), R("mb"))
+        if NPE:
+            for t in range(NB):
+                mul("a", R("Gd", 128 * t, 128 * t + 128), I, R("gn", t, t + 1))
 
-    def refill(w, src):
-        dma("s", [(R(w, 0, 2056), R(src, 0, 2056)), (R(w, 2056, 4112), R(src, 0, 2056))])
+    def scatter(t, src, step):
+        w = "W%d" % (t % 2)
+        cp(IND(R(w, 16, WIN), R("LP", 0, 16)), RS(src[0], src[1], 256, step))
+        return lambda: cp(IND(R(w, 528, WIN), R("LP", 16, 33)), RS(src[0], src[1] + 256 * step, 272, step))
+
+    def unfold(t, o, a, b):
+        w = "W%d" % (t % 2)
+        group([(o, TS(s), RS(w, 16 + 16 * a + s, b - a, 16)) for s in range(-7, 16)])
 
     def lists(t):
-        o = R("dl", 72 * t + 8, 72 * t + 72)
-        landed(t, o, "ad%d" % t, [send(t, o, d, "ad%d" % t, (newsem(), bits(topo.mask(core, client(t)))))])
-        group([(PS(4, 0, 64), R("Tri"), d), (PS(4, 0, 64), R("TriC"), dprev), (PS(4, 63, 64), I, R("lastc", 0, 1))])
-        group([(PS(4, 64, 128), R("TrS"), d), (PS(4, 64, 128), R("TrSC"), dprev)])
-        group([(PS(4, 128, 192), I, d)])
-        scan(R("IO"), R("rst"), PS(4, 0, 128), 0.0, ALU.mult, ALU.add)
-        cp(R("LU", 0, 64), R("IO", 0, 64))
-        cp(R("dj"), PS(4, 128, 192))
-        act(R("Rr"), IND(R("rt"), R("dj")))
+        act(R("OH", 8, 520), IND(R("ot"), R("dj", 0, 32)))
+        group([(PS(L, 0, 33), R("TP", 128 * k, 128 * k + 128), RS("d", 8 + k % 2 - 2 * (k // 2), 33, 2)) for k in range(4)] + [(PS(L, 32, 33), I, R("cv", 0, 1))])
+        group([(PS(L, 33, 97), R("TrS"), d), (PS(L, 33, 97), R("TrSC"), dprev), (PS(L, 33, 34), I, R("cv", 1, 2))])
+        scan(R("IO", 0, 97), R("rst", 0, 97), PS(L, 0, 97), 0.0, ALU.mult, ALU.add)
+        cp(R("LP", 0, 16), R("IO", 0, 16))
+        ts(R("LP", 16, 33), R("IO", 16, 33), -512.0, ALU.add)
+        second = scatter(t, ("OH", 8), 2)
 
-        def places(a, b):
-            s2 = PS(4, 384, 384 + b - a)
-            group([(PS(5, a, b), R("W1", 15 - i, 143 - i), R("wM", 16 + 16 * a + i, 16 + 16 * b, 16)) for i in range(16)])
-            act(R("Rb", 1 + a, 1 + b), PS(5, a, b), AF.Identity, bias=1.0)
-            group([(s2, R("F1"), R("Rb", 1 + a, 1 + b)), (s2, R("F2"), R("Rb", a, b))])
-            scan(R("xf", a, b), s2, R("zer", 0, b - a), 0.0 if a == 0 else R("xf", a - 1, a), ALU.add, ALU.add)
-            cp(R("xu", a, b), R("xf", a, b))
+        def places(k, a, b):
+            m = BK["M"][k]
+            s1, s2 = PS(m, 256, 256 + b - a), PS(m, 384, 384 + b - a)
+            unfold(t, s1, a, b)
+            scan(R("Rb", 8 + a, 8 + b), s1, R("zer", 0, b - a), R("Rb", 7 + a, 8 + a), ALU.add, ALU.add)
+            group([(s2, R("F1"), R("Rb", 8 + a, 8 + b)), (s2, R("F2"), R("Rb", 7 + a, 7 + b))])
+            cp(R("xu", a, b), s2)
 
-        c = OPT["split"]
-        if c:
-            cp(IND(R("wM", 16, WIN), R("LU", 0, c)), R("zer", 0, 16 * c))
-            ts(R("LV", c, 64), R("IO", c, 64), -16.0 * c, ALU.add)
-            places(0, c)
-            cp(IND(R("wM", 16 + 16 * c, WIN), R("LV", c, 64)), R("zer", 0, B - 16 * c))
-            places(c, 128)
-        else:
-            cp(IND(R("wM", 16, WIN), R("LU", 0, 64)), R("zer", 0, B))
-            places(0, 128)
-        places(128, 256)
+        places(0, 0, 32)
+        table(0, 511)
+        act(R("OH", 520, 1032), IND(R("ot"), R("dj", 32, 64)))
+        second()
+        places(1, 32, 128)
+        table(511, 1023)
+        group([(PS(L, 226, 227), R("WR"), R("OH", 1031, 1032))])
+        group([(PS(L, 227, 228), R("WL"), R("OH", 1031, 1032))])
+        group([(PS(L, 228, 229), I, R("A", 0, 1)), (PS(L, 228, 229), nI, R("A", B - 1, B))])
+        ts(R("tab", 2048, 2050), PS(L, 226, 228), PS(L, 228, 229), ALU.mult)
+        places(2, 128, 256)
         tag[0] = "late"
-        ts(R("LU", 64, 128), R("IO", 64, 128), 4096.0, ALU.min)
-        dma("s", turn("LUs%d" % (t % 2), "LU") + turn("ds%d" % (t % 2), "d", None, None, 8, 72))
+        on = R("IO", 33, 97)
+        hi, lo = R("hl", 128 * t, 128 * t + 64), R("hl", 128 * t + 64, 128 * t + 128)
+        act(hi, on)
+        tt(lo, on, hi, ALU.subtract)
+        post(client(t), partner(t), R("chl", 128 * t, 128 * t + 128), R("hl", 128 * t, 128 * t + 128))
         if t < NB - 1:
-            ts(R("deb", 36, 64), R("IO", 100, 128), 4096.0, ALU.is_ge)
-            if OPT["dvn"] == "a":
-                tt(R("jt"), R("deb", 36, 64), R("jm"), ALU.mult)
-                ts(R("deu", 0, 28), R("jt"), 1024.0, ALU.add)
-                act(R("dvn"), IND(R("v"), R("deu", 0, 28)), AF.Copy, scale=-1.0)
-            else:
-                ts(R("deu", 0, 28), R("IO", 100, 128), 4096.0, ALU.is_ge)
-                tt(R("dvn"), IND(R("dtab"), R("deu", 0, 28)), R("v", 576, B), ALU.mult)
+            ts(R("LU"), on, -8192.0, ALU.add, 4096.0, ALU.min)
+            dma("s", turn("LUs", "LU", 64 * t, 64 * t + 64))
+            post(partner(t), client(t), R("cLU", 64 * t, 64 * t + 64), R("LUs", 64 * t, 64 * t + 64))
+            ts(R("mA", 1088 * t, 1088 * t + 64), on, 8192.0 + 4096.0, ALU.is_ge)
+            post(partner(t), client(t), R("cA", 1088 * t, 1088 * t + 1088), R("mA", 1088 * t, 1088 * t + 1088))
+            tt(R("jt"), R("mA", 1088 * t + 36, 1088 * t + 64), R("jm"), ALU.mult)
+            ts(R("deu", 0, 28), R("jt"), 1024.0, ALU.add)
+            act(R("dvn"), IND(R("v"), R("deu", 0, 28)), AF.Copy, scale=-1.0)
 
-    def table(t):
-        act(R("tab", 1, 2047, 2), R("A", 1, B))
-        act(R("tab", 2047, 2048), R("A", 0, 1))
-        group([(PS(0), nI, R("A", 0, 512)), (PS(0), I, R("A", 1, 513))])
-        group([(PS(1), nI, R("A", 512, B)), (PS(1, 0, 511), I, R("A", 513, B)), (PS(1, 511, 512), I, R("A", 0, 1))])
-        tt(R("tab", 0, 2048, 2), R("ps", 0, B), R("Rr"), ALU.mult)
-        tt(R("ini", 0, 1), R("A", 0, 1), R("tab", 0, 1), ALU.subtract)
+    def table(a, b):
+        n = b - a
+        w = wbank()
+        group([(PS(w, 0, n), nI, R("A", a, b)), (PS(w, 0, n), I, R("A", a + 1, b + 1))])
+        mul(OPT["evD"][a // 500], R("D", a, b), PS(w, 0, n), 1.0)
+        for m, at in (("WR", 2), ("WJ", 3)):
+            w = wbank()
+            group([(PS(w, 0, n), R(m), R("OH", 8 + a, 8 + b))])
+            tt(RS("tab", 2 * a + at, n, 2), PS(w, 0, n), R("D", a, b), ALU.mult)
 
     edges = [sum(CH[:k]) for k in range(len(CH) + 1)]
-    ytok, ysend = {}, {}
+    ytok, ysend, yend = {}, {}, {}
     ring = [0]
+    before = {}
+
+    def send_y(t, phase, after=()):
+        for k, a, b, way, late in pieces(t):
+            if late == phase:
+                stops = helpers(core, client(t), T, topo)[way]
+                o, sem = (R(HB[t], a, b), "s%d" % (8 * t + k)) if stops else (R(XB[t], a, b), "x%d" % t)
+                j = send((stops + [client(t)])[0], o, R("Y%d" % (t % 2), a, b), sem, ytok[t], after=list(after) + before.get(way, []))
+                ysend[t].append(j)
+                before[way] = [j]
+                for link in {"D": [], "P": ["port"], "M": ["mate out", "mate in"]}[way]:
+                    j = rec("f", [], [], [], (0, 0, 0, 0, 0), ("onward", (b - a) * 512, link), after=[j])
+                yend[t].append(j)
+
+    def landed_x(t):
+        last = [([partner(t)] + helpers(partner(t), core, T, topo)[way])[-1] for k, a, b, way, late in pieces(t)]
+        landed(R(XB[t]), "x%d" % t, sum(bits(topo.mask(c, core)) for c in last), yend[t])
 
     def make_y(t):
-        ytok[t] = (newsem(), len(CH) * bits(topo.mask(core, client(t))))
-        ysend[t] = []
-        y = "Y%d" % (t % OPT["ny"])
+        first = [(helpers(core, client(t), T, topo)[way] + [client(t)])[0] for k, a, b, way, late in pieces(t)]
+        ytok[t] = (newsem(), sum(bits(topo.mask(core, c)) for c in first))
+        ysend[t], yend[t] = [], []
+        y = "Y%d" % (t % 2)
         for k in range(len(CH)):
             a, b = edges[k], edges[k + 1]
             o = 1024 * (ring[0] % 3)
             ring[0] += 1
-            act(R("inc", o, o + b - a), IND(R("tab"), R("xu", a // 16, b // 16)))
-            scan(R(y, a, b), R("wM", 16 + a, 16 + b), R("inc", o, o + b - a), R("ini", 0, 1) if k == 0 else R(y, a - 1, a), ALU.mult, ALU.add)
-            guard = [R(XB[0], 0, S)] if t == 2 and k == len(CH) - 1 else []
-            ysend[t].append(send(t, R(XB[t], a, b), R(y, a, b), "ax%d" % t, ytok[t], guard))
-        landed(t, R(XB[t], 0, S), "ax%d" % t, ysend[t])
+            act(R("inc", o, o + b - a), IND(R("tab", 0, 1024 if b <= 512 else None), R("xu", a // 16, b // 16)))
+            scan(R(y, a, b), R("inc", o, o + b - a), R("zer", 0, b - a), R("A", 0, 1) if k == 0 else R(y, a - 1, a), ALU.add, ALU.add,
+                 after=ysend[t - 2] if t > 1 else ())
+        send_y(t, 0)
 
-    def y_turn(t, early):
+    def y_turn(t):
         for k in range(4):
-            late = k >= early
-            dma("s", turn("Ys", "Y%d" % (t % OPT["ny"]), 1024 * k, 1024 * k + 1024, 1024 * k, 1024 * k + 1024),
+            late = t == NB - 1 and k >= OPT["early"]
+            dma("s", turn("Ys%d" % (t % OPT["nys"]), "Y%d" % (t % 2), 1024 * k, 1024 * k + 1024, 1024 * k, 1024 * k + 1024),
                 after=ysend[t] if late else (), pre=ytok[t] if late else None)
 
     def reading(t):
-        group([(PS(6, 0, 64), R("TrS"), R("dl", 72 * t + 8, 72 * t + 72)), (PS(6, 0, 64), R("TrSC"), R("dl", 72 * t + 7, 72 * t + 71))])
-        scan(R("P"), PS(6, 0, 64), R("zer", 0, 64), 0.0, ALU.add, ALU.add)
-        lin(sm, R("H"), R("P"), 1 / 64.0, 128.0)
-        lin(sm, R("tH"), R("H"), -64.0, 8192.0)
-        tt(R("lo"), R("P"), R("tH"), ALU.add)
-        dma("s", [((T.Pw[1:128:16, :],) + R("Pw")[1:], R("H")), ((T.Pw[2:128:16, :],) + R("Pw")[1:], R("lo"))])
-        act(R("G"), IND(R("Pw"), R("mu")))
-        rows = [(PS(6, i, 512, 16), R("REP", 5 + 128 * i, 133 + 128 * i), R("ds%d" % (t % 2), 0, 32)) for i in range(16)]
-        group([(PS(6), nI, R("G", 0, 512)), (PS(6), I, R("G", 1, 513))] + rows)
-        rows = [(PS(7, i, 512 if i < 15 else 496, 16), R("REP", 5 + 128 * i, 133 + 128 * i), R("ds%d" % (t % 2), 32, 64 if i < 15 else 63)) for i in range(16)]
-        group([(PS(7), nI, R("G", 512, B)), (PS(7, 0, 511), I, R("G", 513, B)), (PS(7, 511, 512), I, R("G", B - 1, B))] + rows)
-        act(R("V"), R("ps", 3072, 4096))
-        refill("wQ", "zer")
-        w = 64 // OPT["qs"]
-        for c in range(0, 64, w):
-            cp(IND(R("wQ", 16, WIN), R("LUs%d" % (t % 2), c, c + w)), R("V", 16 * c, 16 * (c + w)))
-        cp(R("wQ", 16, 17), R("G", 0, 1))
-        group([(PS(6, 0, 256), R("U1", 15 - i, 143 - i), R("wQ", 16 + i, 16 + S, 16)) for i in range(16)])
-        act(R("Rq", 4, 260), PS(6, 0, 256))
-        group([(PS(7, 0, 256), R("Tri4"), R("Rq", 4, 260)), (PS(7, 0, 256), R("TriC4"), R("Rq", 3, 259))])
-        scan(R("ef"), PS(7, 0, 256), R("c77"), col(7), ALU.add, ALU.add)
-        if OPT["emod"] == "v":
-            cp(R("ei"), R("ef"))
-            ts(R("ej"), R("ei"), S - 1, ALU.bitwise_and)
-            cp(R("eu%d" % (t % 2)), R("ej"))
+        q = BK["Q"]
+        pw = R("Pw")[1:]
+        dma("s", [((T.Pw[8 * h:112:16, :],) + pw, R("chl", 128 * t + 64 * h, 128 * t + 64 * h + 64, p=(16, 128))) for h in range(2)]
+            + [((T.Pw[112 + 8 * h:113 + 8 * h, :],) + pw, R("chl", 128 * t + 64 * h, 128 * t + 64 * h + 64, p=(0, 16))) for h in range(2)])
+        act(R("G", 8, 8 + B), IND(R("Pw"), R("mu")))
+        group([(PS(q), R("MA"), RS("G", 8, 512, 2)), (PS(q), R("MB"), RS("G", 9, 512, 2)), (PS(q), nI, RS("G", 7, 512, 2)),
+               (PS(q), R("ME"), RS("OH", 8, 512, 2)), (PS(q), R("MO"), RS("OH", 7, 512, 2))])
+        tt(R("val", 0, 512), PS(q), RS("OH", 8, 512, 2), ALU.mult)
+        scatter(t, ("val", 0), 1)()
+        unfold(t, PS(q, 0, 256), 0, 256)
+        scan(R("Cq", 8, 264), PS(q, 0, 256), R("c38"), 0.0, ALU.add, ALU.add)
+        if t < NB - 2:
+            w = "W%d" % (t % 2)
+            dma("s", [(R(w, 0, 2064), R("zer")), (R(w, 2064, 4128), R("zer"))])
+        o = PS(q, 256, 512)
+        sums = [(o, R("Tri4", 0, 128), R("Cq", 8, 264)), (o, R("TriC4", 0, 128), R("Cq", 7, 263))]
+        group(sums, last=not OPT["cont"], hold=[PS(q)])
+        act(R("Hq"), o, AF.Identity, bias=col(11), scale=1 / 2048.0, also=[PS(q)])
+        if OPT["cont"]:
+            group([(o, R("n2kI"), R("Hq"))], first=False, hold=[PS(q)])
         else:
-            act(R("Hq"), R("ef"), AF.Identity, bias=col(8), scale=1 / 4096.0)
-            group([(PS(6, 0, 256), R("I4"), R("ef")), (PS(6, 0, 256), R("n4kI"), R("Hq"))])
-            ts(R("eu%d" % (t % 2)), PS(6, 0, 256), 128.0 * 4096.0, ALU.add)
+            group(sums + [(o, R("n2kI"), R("Hq"))])
+        ts(R("eu%d" % (t % 2)), o, 2.0, ALU.mult, 128.0 * 4096.0 - 77.0, ALU.add)
+
+    tring = [0]
 
     def output(t):
         last = t == NB - 1
-        cuts = list(range(0, S + 1, OPT["oc"]))
-        if last:
-            cuts = sorted(set(cuts + [S - 512]))
-        stores = [1024, 2048, 3072, 3584, S] if last else [2048, S]
+        ys = "Ys%d" % (t % OPT["nys"])
+        nd = S - NPE
+        stores = [x for x in ([1024, 2048, 3072, 3584, S] if last else [2048, S]) if x < nd] + [nd]
         done = 0
-        for a, b in zip(cuts[:-1], cuts[1:]):
-            z = R("Z", a, b)
-            tt(z, IND(R(XB[t], 0, S), R("eu%d" % (t % 2), a // 16, b // 16)), R("Ys", a, b), ALU.mult)
-            act(z, z, AF.Tanh, scale=2.0 ** -14)
-            if OPT["gain"][t][a // 1024] == "a" and not (last and b == S):
-                act(z, z, AF.Copy, scale=R("gn", t, t + 1))
+        for a in range(0, S, OPT["oc"]):
+            b = a + OPT["oc"]
+            if a < nd:
+                z = R("Z", a, b)
             else:
-                ts(z, z, R("gn", t, t + 1), ALU.mult)
+                z = R("Tr", 512 * (tring[0] % 3), 512 * (tring[0] % 3) + b - a)
+                tring[0] += 1
+            tt(z, IND(R(XB[t], 0, S), R("eu%d" % (t % 2), a // 16, b // 16)), R(ys, a, b), ALU.mult)
+            act(z, z, AF.Tanh, scale=2.0 ** -14)
+            if a >= nd:
+                group([(R("ps", a, b), R("Gd", 128 * t, 128 * t + 128), z)], first=t == 0, last=last)
+                if last:
+                    mul(OPT["evO"][(a // 512) % 2], R(ys, a, b), R("ps", a, b), 1.0)
+                    dma("s", [(R("yo", a, b), R(ys, a, b))])
+                continue
+            mul(OPT["gain"][t][a // 1024], z, z, R("gn", t, t + 1))
             if b in stores:
                 dma("s" if t == 0 else "g", [(R("yo", done, b), R("Z", done, b))], add=t > 0)
                 done = b
 
-    def walk(t):
-        xw = R(XB[t], 0, S + 8)
-        at = R("LUs%d" % (t % 2), 64, 128)
-        tt(R("cmp"), IND(xw, at), R("As"), ALU.is_gt)
-        act(R("F"), IND(xw, at), AF.Identity, bias=col(2), scale=1 / 16.0)
-        group([(PS(4, 192, 256), n128I, R("deb"))] + [(PS(4, 192, 256), R("V1", 15 - i, 143 - i), R("cmp", i, B, 16)) for i in range(16)])
-        act(R("sg"), PS(4, 192, 256), AF.Sign, bias=-8.5)
-        o1, o2 = PS(4, 256, 320), PS(4, 320, 384)
-        group([(o1, I, d), (o1, I, R("deb")), (o1, I, R("sg"))])
-        group([(o2, p2I, d), (o2, p2I, R("deb")), (o2, p2I, R("sg"))])
+    def serve(t):
+        yw = R("Y%d" % (t % 2))
+        tt(R("cmp"), IND(yw, R("cLU", 64 * t, 64 * t + 64)), R("cA", 1088 * t + 64, 1088 * t + 1088), ALU.is_gt)
+        group([(PS(L, 98, 162), n128I, R("cA", 1088 * t, 1088 * t + 64))] + [(PS(L, 98, 162), R("V1", 15 - i, 143 - i), R("cmp", i, B, 16)) for i in range(16)])
+        sg = R("sg", 64 * t, 64 * t + 64)
+        act(sg, PS(L, 98, 162), AF.Sign, bias=-8.5)
+        ks = [post(client(t), partner(t), R("csg", 64 * t, 64 * t + 64), sg, [R(XB[0])] if t == 2 else [])]
+        for h in range(2):
+            f = R("F", B * t + 512 * h, B * t + 512 * h + 512)
+            act(f, IND(yw, R("cLU", 64 * t + 32 * h, 64 * t + 32 * h + 32)), AF.Identity, bias=col(10), scale=1 / 16.0)
+            ks.append(post(client(t), partner(t), R("cF", B * t + 512 * h, B * t + 512 * h + 512), f))
+        send_y(t, 1, after=ks)
+
+    def update(t):
+        sg, deb = R("csg", 64 * t, 64 * t + 64), R("mA", 1088 * t, 1088 * t + 64)
+        o1, o2 = PS(L, 98, 162), PS(L, 162, 226)
+        group([(o1, I, d), (o1, I, deb), (o1, I, sg)])
+        group([(o2, p2I, d), (o2, p2I, deb), (o2, p2I, sg)])
+        cp(R("dj"), o1)
         ts(R("c2"), o2, 2.0, ALU.max, 14.0, ALU.min)
         tt(d, R("c2"), o1, ALU.subtract)
-        tag[0] = "walka"
         for h in range(2):
             a, b = 512 * h, 512 * h + 512
-            group([(PS(h), I, R("c192")), (PS(h), I, R("v", a, b)), (PS(h), SB, R("F", a, b))])
-            ts(R("v", a, b), PS(h), -64.0, ALU.max, 64.0, ALU.min)
-        for h in range(2):
-            a, b = 512 * h, 512 * h + 512
-            dead = [(PS(3, 64, 512), I, R("dvn"))] if h else []
-            group([(PS(2 + h), I, R("A", a, b))] + dead + [(PS(2 + h), I, R("v", a, b))])
-            if OPT["fold"][h] == "v":
-                ts(R("cl", a, b), PS(2 + h), -256.0, ALU.max, 256.0, ALU.min)
-                dead = [(PS(3, 64, 512), nI, R("dvn"))] if h else []
-                group([(PS(2 + h), nI, R("A", a, b))] + dead + [(PS(2 + h), nI, R("v", a, b)), (PS(2 + h), p2I, R("cl", a, b))])
-                act(R("A", a, b), PS(2 + h))
+            w = wbank()
+            group([(PS(w), I, R("c192")), (PS(w), I, R("v", a, b)), (PS(w), SB, R("cF", B * t + a, B * t + b))])
+            ts(R("v", a, b), PS(w), -64.0, ALU.max, 64.0, ALU.min)
+            w = wbank()
+            neg = [(PS(w), nI, R("A", a, b))] + ([(PS(w, 64, 512), nI, R("dvn"))] if h else []) + [(PS(w), nI, R("v", a, b))]
+            group(neg, last=not OPT["cont"])
+            ts(R("cl", a, b), PS(w), -256.0, ALU.max, 256.0, ALU.min)
+            if OPT["cont"]:
+                group([(PS(w), n2I, R("cl", a, b))], first=False)
             else:
-                c = R("c4", a, b)
-                act(c, PS(2 + h), AF.Abs, bias=256.0, scale=-1.0)
-                act(c, c, AF.Abs, bias=512.0, scale=-1.0)
-        for h in range(2):
-            if OPT["fold"][h] == "a":
-                act(R("A", 512 * h, 512 * h + 512), R("c4", 512 * h, 512 * h + 512), AF.Identity, bias=-256.0)
+                group(neg + [(PS(w), n2I, R("cl", a, b))])
+            mul(OPT["evA"][h], R("A", a, b), PS(w), 1.0)
         if t + 1 < NB - 1:
-            dma("s", turn("As", "A"))
+            dma("s", turn("mA", "A", 1088 * (t + 1) + 64, 1088 * (t + 2)))
 
     start()
     for t in range(NB):
+        now[0] = t
+        if t > 0:
+            tag[0] = "upd"
+            update(t - 1)
         tag[0] = "lists"
         lists(t)
-        tag[0] = "table"
-        table(t)
         tag[0] = "y"
         make_y(t)
         if t < NB - 1:
-            refill("wM", "one")
+            tag[0] = "serve"
+            serve(t)
+        landed_x(t)
         tag[0] = "read"
         reading(t)
         tag[0] = "out"
         if t > 0:
             output(t - 1)
-        y_turn(t, OPT["early"] if t == NB - 1 else 0)
-        if t < NB - 1:
-            tag[0] = "walk"
-            walk(t)
+        y_turn(t)
     output(NB - 1)
 
     cnt = {"v": 0, "a": 0, "p": 0, "g": 0}
@@ -575,12 +800,14 @@ def rank_program(g, core, T, topo):
     def whole(sp):
         return (sp[0], sp[1] // 512 * 512, (sp[2] + 511) // 512 * 512) if sp[0] == "ps" else sp
 
-    key = tuple((o["e"], o["cost"], o["wire"]) for o in ops)
+    key = tuple((o["e"], o["cost"]) for o in ops)
     if key not in ORDER:
         ORDER[key] = plan(ops)
     for k in ORDER[key]:
         o = ops[k]
         e = o["e"]
+        if e == "f":
+            continue
         rs, ws = [whole(x) for x in o["rs"]], [whole(x) for x in o["ws"]]
         if e != "r":
             need = {}
@@ -607,6 +834,8 @@ def rank_program(g, core, T, topo):
                 fn()
         tok = tok or (csem[e], cnt[e])
         for sp in ws:
+            if o["move"] and o["move"][0] == "remote":
+                continue
             acc[sp[0]] = [x for x in acc.get(sp[0], []) if not (sp[1] <= x[0][1] and x[0][2] <= sp[2])] + [(sp, True, e, tok)]
         for sp in rs:
             acc[sp[0]] = [x for x in acc.get(sp[0], []) if x[1] or x[3][0] != tok[0] or not (sp[1] <= x[0][1] and x[0][2] <= sp[2])] + [(sp, False, e, tok)]

@@ -9,17 +9,18 @@ OPT = {
     "ways": [[(1024, "M", 0), (2048, "P", 0), (3072, "M", 0), (4096, "P", 0)],
              [(1024, "D", 0), (2048, "D", 0), (3072, "D", 1), (4096, "D", 1)],
              [(1024, "M", 0), (2048, "M", 0), (3072, "P", 1), (4096, "P", 1)],
-             [(512, "M", 0), (1024, "M", 0), (2048, "M", 0), (3072, "D", 0), (4096, "D", 0)]],
-    "npe": 1024,
-    "oc": 512,
-    "gain": ["aaaa", "aaaa", "aaaa", "aaaa"],
-    "banks": {"L": 0, "M": [0, 1, 0], "Q": 2, "W": [3, 4, 5]},
-    "evA": "aa", "evD": "aa", "evO": "aa", "cont": 0, "nys": 1, "early": 1, "rounds": 6, "seq": 1, "flow": 0, "look": 300.0, "tries": 6000, "seed": 1,
+             [(512, "M", 0), (1024, "P", 0), (2048, "M", 0), (3072, "Q", 0), (3584, "P", 0), (4096, "D", 0)]],
+    "npe": 1536,
+    "oc": [512, 512, 512, 512],
+    "fold": ["aa", "aa", "aa"], "cut": 128,
+    "gain": ["aaaaaaaa"] * 4, "two": [0, 0], "end": 512, "stores": [[2048], [1024, 2048, 3072]], "viaA": 1,
+    "banks": {"L": 0, "M": [0, 0, 0], "Q": 1, "W": [2, 3, 4], "O": [1]},
+    "evA": "aa", "evD": "aa", "evO": "avaa", "nys": 2, "early": 4, "rounds": 6, "seq": 1, "flow": 0, "look": 300.0, "just": 1, "slack": 0.01, "qcut": 64, "swaps": 25000, "heat": 0.004, "tries": 2500, "seed": 1,
     "weigh": {},
     "boost": {"upd": 0.0, "lists": 0.0, "table": 0.0, "y": 0.0, "serve": 0.0, "late": -60.0, "read": -150.0, "out": -100.0, "start": 0.0, "start2": -150.0},
-    "fig": {"cy": 1.04, "pe": 0.52, "ga": 1.56, "sc": 3.8, "fix": 60, "hop": 120, "bw": 140.0, "bwon": 350.0, "lbw": 600.0, "row": 30.0,
+    "fig": {"cy": 0.95, "pe": 0.48, "ga": 1.56, "sc": 3.8, "fix": 60, "hop": 100, "bw": 120.0, "bwon": 350.0, "lbw": 600.0, "row": 15.0,
             "far": 750.0, "wake": 300.0, "call": 600.0},
-    "cases": [{}, {"bw": 70.0, "wake": 600.0, "call": 900.0}, {"cy": 0.88, "pe": 0.45, "ga": 1.2, "sc": 2.2}, {"cy": 1.2, "pe": 0.62, "ga": 1.9, "sc": 5.2}],
+    "cases": [{}, {"bw": 70.0, "wake": 600.0, "call": 900.0, "row": 30.0}, {"cy": 0.85, "pe": 0.43, "ga": 1.2, "sc": 2.2}, {"cy": 1.2, "pe": 0.62, "ga": 1.9, "sc": 5.2}],
 }
 XB = ["X0", "X1", "X2", "X0"]
 HB = ["X0", "X1", "X2", "Y0"]
@@ -31,10 +32,10 @@ def _sb(n, dt):
 
 SCRATCH = {
     "X0": _sb(S, F32), "X1": _sb(S, F32), "X2": _sb(S, F32), "Y0": _sb(S + 8, F32), "Y1": _sb(S + 8, F32),
-    "Ys0": _sb(S, F32), "Z": _sb(3072, F32), "Tr": _sb(1536, F32), "inc": _sb(3072, F32), "tab": _sb(2056, F32),
-    "W0": _sb(WIN, BF), "W1": _sb(WIN, BF), "zer": _sb(2064, BF), "one": _sb(128, BF), "c192": _sb(512, BF),
+    "Ys0": _sb(S, F32), "Ys1": _sb(S, F32), "Z": _sb(3072, F32), "Tr": _sb(1024, F32), "inc": _sb(3072, F32), "tab": _sb(2056, F32),
+    "W0": _sb(WIN, BF), "W1": _sb(WIN, BF), "zer": _sb(1040, BF), "one": _sb(128, BF), "c192": _sb(512, BF),
     "A": _sb(B, BF), "v": _sb(B + 16, BF), "cmp": _sb(B, BF), "cl": _sb(B, BF), "D": _sb(B, F32), "dvn": _sb(448, BF),
-    "mA": _sb(3 * 1088, BF), "cA": _sb(3 * 1088, BF), "F": _sb(3 * B, BF), "cF": _sb(3 * B, BF),
+    "mA": _sb(1088, BF), "cA": _sb(3 * 1088, BF), "F": _sb(B, BF), "cF": _sb(B, BF),
     "sg": _sb(3 * 64, BF), "csg": _sb(3 * 64, BF), "LU": _sb(64, U16), "LUs": _sb(3 * 64, U16), "cLU": _sb(3 * 64, U16),
     "hl": _sb(4 * 128, BF), "chl": _sb(4 * 128, BF),
     "OH0": _sb(8 + 1056, BF), "OH1": _sb(8 + 1056, BF), "LP0": _sb(34, U16), "LP1": _sb(34, U16), "ot": _sb(16, BF), "Pw": _sb(B, BF), "G": _sb(8 + B, BF), "val": _sb(528, BF),
@@ -50,7 +51,7 @@ SCRATCH = {
     "Gd": _sb(512, F32), "pi": _sb(4, I32), "pj": _sb(4, I32), "col": _sb(24, F32),
     "ps": ("psum", [128, 4096], F32),
 }
-SEMAPHORES = ["cv", "ca", "cp", "cg"] + ["s%d" % i for i in range(112)] + ["r%d" % i for i in range(24)] + ["x%d" % t for t in range(NB)]
+SEMAPHORES = ["cv", "ca", "cp", "cg"] + ["s%d" % i for i in range(112)] + ["r%d" % i for i in range(24)] + ["x%d" % t for t in range(NB)] + ["a%d" % t for t in range(NB)]
 PLANNED = []
 DEBUG = []
 ORDER = {}
@@ -105,32 +106,59 @@ def plan(ops):
         hold.append(h)
     pred = [sorted(o["deps"]) for o in ops]
 
-    def replay(order, tm):
-        done, at = [0.0] * n, {}
+    eng = [o["e"] for o in ops]
+    banks = [sorted(o["banks"]) for o in ops]
+    link = [o["move"] and o["move"][2] for o in ops]
+    none = (0.0, -1)
+
+    def replay(order, tm, why=None, begin=None):
+        done, at, last = [0.0] * n, {}, [-1] * n
         for k in order:
-            o, x = ops[k], tm[k]
-            e = o["e"]
-            t = max([at.get(e, 0.0) if x[0] else 0.0] + [done[j] for j in pred[k]])
-            for b in o["banks"]:
+            c, pre, move, wire, post = tm[k]
+            e = eng[k]
+            t, by = at.get(e, none) if c else none
+            by = -2 - by
+            for j in pred[k]:
+                if done[j] > t:
+                    t, by = done[j], j
+            for b in banks[k]:
                 u = at.get(b)
-                if u and u[0] != e:
-                    t = max(t, u[1])
-            t += x[0]
-            if x[0]:
-                at[e] = t
-            t += x[1]
-            if x[2]:
-                t = max(t, at.get("dma", 0.0))
-                at["dma"] = t + x[2]
-            end = t + x[2]
-            if x[3]:
-                r = o["move"][2]
-                at[r] = max(t, at.get(r, 0.0)) + x[3]
-                end = max(end, at[r])
-            done[k] = end + x[4]
-            for b in o["banks"]:
-                at[b] = (e, done[k])
-        return max(done)
+                if u and eng[u[1]] != e and u[0] > t:
+                    t, by = u[0], -2 - u[1]
+            if begin:
+                begin[k] = t
+            t += c
+            if c:
+                at[e] = (t, k)
+            if move or wire:
+                t += pre
+                if move:
+                    u = at.get("dma", none)
+                    if u[0] > t:
+                        t, by = u[0], -2 - u[1]
+                    at["dma"] = (t + move, k)
+                end = t + move
+                if wire:
+                    u = at.get(link[k], none)
+                    if u[0] > t:
+                        t, by = u[0], -2 - u[1]
+                    at[link[k]] = (t + wire, k)
+                    end = max(end, t + wire)
+                t = end
+            done[k] = t + post
+            last[k] = by
+            for b in banks[k]:
+                at[b] = (done[k], k)
+        end = max(done)
+        if why is not None:
+            k = done.index(end)
+            while k >= 0:
+                j = last[k]
+                if j < -1:
+                    j = -2 - j
+                    why.append((j, k))
+                k = j
+        return end
 
     def judge(start):
         order = sorted(range(n), key=lambda k: (start[k], k))
@@ -165,8 +193,10 @@ def plan(ops):
                         moved = len(hs) > 1
                         i += 1
             for r, a, w in hs:
-                busy[r].append((t + a, t + a + w))
-                busy[r].sort()
+                line = busy[r]
+                line.append((t + a, t + a + w))
+                if len(line) > 1 and line[-2] > line[-1]:
+                    line.sort()
             start[k] = t
             for j in after[k]:
                 ready[j] = max(ready[j], t + dur[k])
@@ -217,18 +247,62 @@ def plan(ops):
         start, span = place([back[k] + dur[k] for k in range(n)], False)
         best = min(best, (score(start), start, span))
     rnd = np.random.RandomState(OPT["seed"])
+    cur = best
+    tags = np.array([o["tag"] for o in ops])
     for it in range(OPT["tries"]):
-        width = (300.0, 1000.0, 3000.0)[it % 3]
-        lo = rnd.rand() * best[2]
-        prio = [-best[1][k] + (width * rnd.randn() if lo - 15000 < best[1][k] < lo + 15000 else 0.0) for k in range(n)]
-        start, span = flow(prio, OPT["look"] * 2 * rnd.rand()) if OPT["flow"] > 1 and it % 2 == 0 else place(prio, False)
-        if it % 4 == 3:
+        at = np.array(cur[1])
+        near = np.abs(at - rnd.rand() * cur[2]) < (4000.0, 8000.0, 15000.0)[rnd.randint(3)]
+        if it % 3 == 0:
+            at = at + near * (tags == tags[rnd.randint(n)]) * 2500.0 * rnd.randn()
+        else:
+            at = at + near * rnd.randn(n) * (200.0, 600.0, 1500.0)[rnd.randint(3)]
+        start, span = place((-at).tolist(), False)
+        if it % OPT["just"] == 0:
             back, _s = place([start[k] + dur[k] for k in range(n)], True)
             start, span = place([back[k] + dur[k] for k in range(n)], False)
-        best = min(best, (score(start), start, span))
-    PLANNED.append([round(x / 1000.0, 1) for x in [best[2]] + judge(best[1])])
-    DEBUG.append((ops, dur, best[1]))
-    return sorted(range(n), key=lambda k: (best[1][k], k))
+        if span < cur[2] * 1.03:
+            new = (score(start), start, span)
+            if new[0] <= cur[0] + OPT["slack"] * (1.0 - it / OPT["tries"]) * rnd.rand():
+                cur = new
+            best = min(best, new)
+    order = sorted(range(n), key=lambda k: (best[1][k], k))
+    now = top = (best[0], order)
+    for it in range(OPT["swaps"]):
+        order = now[1]
+        why = []
+        replay(order, times[rnd.randint(len(times))], why)
+        j, k = why[rnd.randint(len(why))]
+        a, b = order.index(j), order.index(k)
+        if rnd.rand() < 0.3:
+            a = max(0, a - rnd.randint(12))
+        part = order[a:b + 1]
+        if rnd.rand() < 0.5:
+            take = {k}
+            for x in part[::-1]:
+                if x in take:
+                    take.update(pred[x])
+            if j in take:
+                continue
+            part = [x for x in part if x in take] + [x for x in part if x not in take]
+        else:
+            take = {j}
+            for x in part:
+                if x in take:
+                    take.update(succ[x])
+            if k in take:
+                continue
+            part = [x for x in part if x not in take] + [x for x in part if x in take]
+        order = order[:a] + part + order[b + 1:]
+        new = (sum(replay(order, tm) / u for tm, u in zip(times, base)), order)
+        if new[0] <= now[0] + OPT["heat"] * (1.0 - it / OPT["swaps"]) * rnd.rand():
+            now = new
+        if new[0] < top[0]:
+            top = new
+    begin = [0.0] * n
+    replay(top[1], times[0], None, begin)
+    PLANNED.append([round(x / 1000.0, 1) for x in [best[2]] + [replay(top[1], tm) for tm in times]])
+    DEBUG.append((ops, dur, begin))
+    return top[1]
 
 
 def timing(o, p):
@@ -244,7 +318,7 @@ def timing(o, p):
     wire = by / p["bw"] if link else 0.0
     if kind == "onward":
         return (0.0, 2 * p["far"] + p["wake"] + p["call"], 0.0, wire, 0.0)
-    return (p["call"], p["far"], by / (300.0 if link else p["bwon"]) + (16 if link else 8) * p["row"], wire, p["hop"])
+    return (p["call"], p["far"], by / (p["bw"] if link else p["bwon"]) + (16 if link else 8) * p["row"], wire, p["hop"])
 
 
 def helpers(core, dst, T, topo):
@@ -255,7 +329,12 @@ def helpers(core, dst, T, topo):
         return {"D": []}
     near = [c for c in idle if topo.chip(c) == topo.chip(core)]
     out = [c for c in near if topo.may_write(c, far[0])][0]
-    return {"D": [], "P": [[c for c in near if c != out][0]], "M": [out, far[0]]}
+    rest = [c for c in near if c != out]
+    return {"D": [], "P": rest[:1], "Q": rest[1:2], "M": [out, far[0]]}
+
+
+def handed(core, dst, T, topo):
+    return helpers(core, dst, T, topo).get("Q", []) if OPT["viaA"] else []
 
 
 def pieces(t):
@@ -269,6 +348,14 @@ def handing_on(g, core, T, topo):
     n_r = len(T.cores)
     left = 0
     for t in range(NB):
+        for r, src in enumerate(T.cores):
+            dst = T.cores[(r + 1 + t % (n_r - 1)) % n_r]
+            if t < NB - 1 and core in handed(src, dst, T, topo):
+                rid, pid, _ = topo.addr(dst)
+                slot = T.cA[:, 1088 * t:1088 * t + 1088]
+                g.wait_ge(T.sem["a%d" % t], bits(topo.mask(src, core)))
+                g.remote_dma(slot, slot, T.sem["a%d" % t], T.sem["cg"], pid, rid, topo.mask(core, dst))
+                left += bits(topo.mask(core, dst))
         for k, a, b, way, late in pieces(t):
             for r, src in enumerate(T.cores):
                 dst = T.cores[(r - 1 - t % (n_r - 1)) % n_r]
@@ -418,11 +505,11 @@ def rank_program(g, core, T, topo):
     def client(t):
         return T.cores[(rank - 1 - t % (n_r - 1)) % n_r]
 
-    def send(dst, o, i, rsem, ltok, guard=(), after=()):
+    def send(dst, o, i, rsem, ltok, guard=(), after=(), also=()):
         rid, pid, _ = topo.addr(dst)
         m = topo.mask(core, dst)
         link = None if topo.chip(dst) == topo.chip(core) else "port"
-        return rec("g", [lambda: g.remote_dma(o[0], i[0], T.sem[rsem], T.sem[ltok[0]], pid, rid, m)], [i], list(guard), (0, 0, 0, 0, 0),
+        return rec("g", [lambda: g.remote_dma(o[0], i[0], T.sem[rsem], T.sem[ltok[0]], pid, rid, m)], [i] + list(also), list(guard), (0, 0, 0, 0, 0),
                    ("remote", i[5] * SIZE[kind[i[1]]] * 128, link), tok=ltok, after=after)
 
     def landed(o, rsem, count, sends):
@@ -432,12 +519,9 @@ def rank_program(g, core, T, topo):
         nsem[1] += 1
         return "r%d" % (nsem[1] - 1)
 
-    small = ("s0", sum(bits(topo.mask(core, client(t))) * (4 if t < NB - 1 else 1) + bits(topo.mask(core, partner(t))) * (2 if t < NB - 1 else 0) for t in range(NB)))
-    nsem[0] = 1
-
-    def post(dst, src, o, i, guard=()):
+    def post(dst, src, o, i, guard=(), also=()):
         r = newr()
-        k = send(dst, o, i, r, small, guard)
+        k = send(dst, o, i, r, (newsem(), bits(topo.mask(core, dst))), guard, also=also)
         landed(o, r, bits(topo.mask(src, core)), [k])
         return k
 
@@ -461,6 +545,9 @@ def rank_program(g, core, T, topo):
             return R("TM", 128 * (22 - s), 128 * (23 - s))
         return R("TB", 15 - s, 143 - s)
 
+    def clear(w):
+        dma("s", [(R(w, a, a + 1032), R("zer", 0, 1032)) for a in range(0, 4128, 1032)])
+
     def start():
         dma("s", back("di", "du", 64))
         dma("s", back("A", "am", B))
@@ -468,16 +555,16 @@ def rank_program(g, core, T, topo):
         one = R("one")
         ms(one, 1.0)
         ms(R("zer"), 0.0)
-        ms(R("W0", 0, 544), 0.0)
-        dma("s", [(R("W0", 544, 2064), R("zer", 0, 1520)), (R("W0", 2064, 4128), R("zer"))])
+        clear("W0")
         iota(R("pi", 0, 1), [[1, 1]], 0, 1)
         iota(R("J"), [[1, 160]], 0, 0)
         sel(R("bl2"), one, [[-16, 8], [0, 16]], ALU.is_ge, 0, 1)
         sel(R("bl2"), R("bl2"), [[16, 8], [0, 16]], ALU.is_ge, 15, -1)
         for f in range(2):
             sel(R("TP", 128 * f, 128 * f + 128), R("bl2"), [[16, 8], [2, 16]], ALU.is_gt, -16 * f, -1)
-            sel(R("TP", 256 + 128 * f, 384 + 128 * f), R("bl2"), [[-16, 8], [-2, 16]], ALU.is_ge, 16 * f, 1)
-        sel(I, one, [[-1, 128]], ALU.is_equal, 0, 1)
+            mul("a", R("TP", 256 + 128 * f, 384 + 128 * f), R("TP", 128 * f, 128 * f + 128), -1.0)
+        cp(col(13), R("pi", 0, 1))
+        ts(I, R("J", 0, 128), col(13), ALU.is_equal)
         sel(R("TrS"), R("bl2"), [[1, 128]], ALU.is_gt, 0, -1)
         sel(R("TrSC"), R("bl2"), [[-1, 128]], ALU.is_ge, 0, 1)
         sel(R("Tri4", 16, 144), R("bl2"), [[1, 128]], ALU.is_ge, 0, -1)
@@ -498,8 +585,9 @@ def rank_program(g, core, T, topo):
             ts(R(oh, 1032, 1064), R("J", 0, 32), 0.0, ALU.is_equal, col(3), ALU.mult)
         ms(R("rst"), 1.0)
         ms(R("rst", 33, 34), 0.0)
-        ts(R("cv", 0, 1), col(1), 1.0, ALU.add)
-        ms(R("cv", 1, 2), 8192.0)
+        ms(R("cv", 0, 1), -512.0)
+        ts(R("cv", 1, 2), col(1), 1.0, ALU.add)
+        ms(R("cv", 2, 3), 8192.0)
         ts(col(4), R("pi", 0, 1), col(2), ALU.subtract, 15.0, ALU.add)
         ts(R("TB"), R("J"), col(4), ALU.is_equal, 0.5, ALU.mult)
         ts(R("mk", 0, 7), R("J", 1, 8), col(0), ALU.is_le)
@@ -530,7 +618,7 @@ def rank_program(g, core, T, topo):
         tag[0] = "start2"
         dma("s", back("v", "ve", B))
         dma("s", back("mi", "mp", 64) + [(R("gn"), R("gain"))])
-        dma("s", [(R("W1", 0, 2064), R("zer")), (R("W1", 2064, 4128), R("zer"))])
+        clear("W1")
         iota(R("jm"), [[16, 28]], -448, 0)
         sel(R("B8"), one, [[-8, 16], [0, 8]], ALU.is_ge, 0, 1)
         sel(R("B8"), R("B8"), [[8, 16], [0, 8]], ALU.is_ge, 7, -1)
@@ -581,16 +669,16 @@ def rank_program(g, core, T, topo):
 
     def lists(t):
         act(R("OH", 8, 520), IND(R("ot"), R("dj", 0, 32)))
-        group([(PS(L, 0, 33), R("TP", 128 * k, 128 * k + 128), RS("d", 8 + k % 2 - 2 * (k // 2), 33, 2)) for k in range(4)] + [(PS(L, 32, 33), I, R("cv", 0, 1))])
-        group([(PS(L, 33, 97), R("TrS"), d), (PS(L, 33, 97), R("TrSC"), dprev), (PS(L, 33, 34), I, R("cv", 1, 2))])
+        group([(PS(L, 0, 33), R("TP", 128 * k, 128 * k + 128), RS("d", 8 + k % 2 - 2 * (k // 2), 33, 2)) for k in range(4)]
+              + [(PS(L, 0, 33), R("bl2"), RS("d", 6 + f, 33, 2)) for f in range(2)] + [(PS(L, 16, 33, 16), I, R("cv", 0, 2))])
+        group([(PS(L, 33, 97), R("TrS"), d), (PS(L, 33, 97), R("TrSC"), dprev), (PS(L, 33, 34), I, R("cv", 2, 3))])
         scan(R("IO", 0, 97), R("rst", 0, 97), PS(L, 0, 97), 0.0, ALU.mult, ALU.add)
-        cp(R("LP", 0, 16), R("IO", 0, 16))
-        ts(R("LP", 16, 33), R("IO", 16, 33), -512.0, ALU.add)
+        cp(R("LP", 0, 33), R("IO", 0, 33))
         second = scatter(t, ("OH", 8), 2)
 
         def places(k, a, b):
             m = BK["M"][k]
-            s1, s2 = PS(m, 256, 256 + b - a), PS(m, 384, 384 + b - a)
+            s1, s2 = (PS(m, 256, 256 + b - a), PS(m, 384, 384 + b - a)) if b - a <= 128 else (PS(m, 0, b - a), PS(m, 256, 256 + b - a))
             unfold(t, s1, a, b)
             scan(R("Rb", 8 + a, 8 + b), s1, R("zer", 0, b - a), R("Rb", 7 + a, 8 + a), ALU.add, ALU.add)
             group([(s2, R("F1"), R("Rb", 8 + a, 8 + b)), (s2, R("F2"), R("Rb", 7 + a, 7 + b))])
@@ -600,13 +688,14 @@ def rank_program(g, core, T, topo):
         table(0, 511)
         act(R("OH", 520, 1032), IND(R("ot"), R("dj", 32, 64)))
         second()
-        places(1, 32, 128)
+        places(1, 32, OPT["cut"])
         table(511, 1023)
         group([(PS(L, 226, 227), R("WR"), R("OH", 1031, 1032))])
         group([(PS(L, 227, 228), R("WL"), R("OH", 1031, 1032))])
         group([(PS(L, 228, 229), I, R("A", 0, 1)), (PS(L, 228, 229), nI, R("A", B - 1, B))])
         ts(R("tab", 2048, 2050), PS(L, 226, 228), PS(L, 228, 229), ALU.mult)
-        places(2, 128, 256)
+        if OPT["cut"] < 256:
+            places(2, OPT["cut"], 256)
         tag[0] = "late"
         on = R("IO", 33, 97)
         hi, lo = R("hl", 128 * t, 128 * t + 64), R("hl", 128 * t + 64, 128 * t + 128)
@@ -617,9 +706,15 @@ def rank_program(g, core, T, topo):
             ts(R("LU"), on, -8192.0, ALU.add, 4096.0, ALU.min)
             dma("s", turn("LUs", "LU", 64 * t, 64 * t + 64))
             post(partner(t), client(t), R("cLU", 64 * t, 64 * t + 64), R("LUs", 64 * t, 64 * t + 64))
-            ts(R("mA", 1088 * t, 1088 * t + 64), on, 8192.0 + 4096.0, ALU.is_ge)
-            post(partner(t), client(t), R("cA", 1088 * t, 1088 * t + 1088), R("mA", 1088 * t, 1088 * t + 1088))
-            tt(R("jt"), R("mA", 1088 * t + 36, 1088 * t + 64), R("jm"), ALU.mult)
+            ts(R("mA", 0, 64), on, 8192.0 + 4096.0, ALU.is_ge)
+            o, i = R("cA", 1088 * t, 1088 * t + 1088), R("mA")
+            via = handed(core, partner(t), T, topo)
+            to = (via + [partner(t)])[0]
+            j = send(to, o, i, "a%d" % t, (newsem(), bits(topo.mask(core, to))))
+            if via:
+                j = rec("f", [], [], [], (0, 0, 0, 0, 0), ("onward", 1088 * 256, "port"), after=[j])
+            landed(o, "a%d" % t, bits(topo.mask(([client(t)] + handed(client(t), core, T, topo))[-1], core)), [j])
+            tt(R("jt"), R("mA", 36, 64), R("jm"), ALU.mult)
             ts(R("deu", 0, 28), R("jt"), 1024.0, ALU.add)
             act(R("dvn"), IND(R("v"), R("deu", 0, 28)), AF.Copy, scale=-1.0)
 
@@ -646,7 +741,7 @@ def rank_program(g, core, T, topo):
                 j = send((stops + [client(t)])[0], o, R("Y%d" % (t % 2), a, b), sem, ytok[t], after=list(after) + before.get(way, []))
                 ysend[t].append(j)
                 before[way] = [j]
-                for link in {"D": [], "P": ["port"], "M": ["mate out", "mate in"]}[way]:
+                for link in {"D": [], "P": ["port"], "Q": ["port"], "M": ["mate out", "mate in"]}[way]:
                     j = rec("f", [], [], [], (0, 0, 0, 0, 0), ("onward", (b - a) * 512, link), after=[j])
                 yend[t].append(j)
 
@@ -684,19 +779,16 @@ def rank_program(g, core, T, topo):
                (PS(q), R("ME"), RS("OH", 8, 512, 2)), (PS(q), R("MO"), RS("OH", 7, 512, 2))])
         tt(R("val", 0, 512), PS(q), RS("OH", 8, 512, 2), ALU.mult)
         scatter(t, ("val", 0), 1)()
-        unfold(t, PS(q, 0, 256), 0, 256)
+        for c in range(0, 256, OPT["qcut"]):
+            unfold(t, PS(q, c, c + OPT["qcut"]), c, c + OPT["qcut"])
         scan(R("Cq", 8, 264), PS(q, 0, 256), R("c38"), 0.0, ALU.add, ALU.add)
         if t < NB - 2:
-            w = "W%d" % (t % 2)
-            dma("s", [(R(w, 0, 2064), R("zer")), (R(w, 2064, 4128), R("zer"))])
+            clear("W%d" % (t % 2))
         o = PS(q, 256, 512)
         sums = [(o, R("Tri4", 0, 128), R("Cq", 8, 264)), (o, R("TriC4", 0, 128), R("Cq", 7, 263))]
-        group(sums, last=not OPT["cont"], hold=[PS(q)])
-        act(R("Hq"), o, AF.Identity, bias=col(11), scale=1 / 2048.0, also=[PS(q)])
-        if OPT["cont"]:
-            group([(o, R("n2kI"), R("Hq"))], first=False, hold=[PS(q)])
-        else:
-            group(sums + [(o, R("n2kI"), R("Hq"))])
+        group(sums)
+        act(R("Hq"), o, AF.Identity, bias=col(11), scale=1 / 2048.0)
+        group(sums + [(o, R("n2kI"), R("Hq"))])
         ts(R("eu%d" % (t % 2)), o, 2.0, ALU.mult, 128.0 * 4096.0 - 77.0, ALU.add)
 
     tring = [0]
@@ -705,24 +797,40 @@ def rank_program(g, core, T, topo):
         last = t == NB - 1
         ys = "Ys%d" % (t % OPT["nys"])
         nd = S - NPE
-        stores = [x for x in ([1024, 2048, 3072, 3584, S] if last else [2048, S]) if x < nd] + [nd]
+        n2 = nd - OPT["two"][t // 2]
+        stores = [x for x in OPT["stores"][last] if x < nd] + [n2, nd]
         done = 0
-        for a in range(0, S, OPT["oc"]):
-            b = a + OPT["oc"]
-            if a < nd:
+        oc = OPT["oc"][t]
+        cuts = sorted(set(list(range(0, S + 1, oc)) + [n2, nd] + ([S - OPT["end"]] if last else [])))
+        for a, b in zip(cuts[:-1], cuts[1:]):
+            o = tring[0] if tring[0] + b - a <= 1024 else 0
+            if a < n2 or (a < nd and t % 2 == 0):
                 z = R("Z", a, b)
             else:
-                z = R("Tr", 512 * (tring[0] % 3), 512 * (tring[0] % 3) + b - a)
-                tring[0] += 1
+                z = R("Tr", o, o + b - a)
+                tring[0] = o + b - a
             tt(z, IND(R(XB[t], 0, S), R("eu%d" % (t % 2), a // 16, b // 16)), R(ys, a, b), ALU.mult)
             act(z, z, AF.Tanh, scale=2.0 ** -14)
-            if a >= nd:
-                group([(R("ps", a, b), R("Gd", 128 * t, 128 * t + 128), z)], first=t == 0, last=last)
-                if last:
-                    mul(OPT["evO"][(a // 512) % 2], R(ys, a, b), R("ps", a, b), 1.0)
-                    dma("s", [(R("yo", a, b), R(ys, a, b))])
+            if n2 <= a < nd:
+                if t % 2:
+                    for c in range(a, b, 512):
+                        w = BK["O"][(c // 512) % len(BK["O"])]
+                        group([(PS(w), R("Gd", 128 * t - 128, 128 * t), R("Z", c, c + 512)),
+                               (PS(w), R("Gd", 128 * t, 128 * t + 128), R("Tr", o + c - a, o + c - a + 512))])
+                        mul(OPT["gain"][t][c // 512], R("Z", c, c + 512), PS(w), 1.0)
+                    if b in stores:
+                        dma("s" if t == 1 else "g", [(R("yo", done, b), R("Z", done, b))], add=t > 1)
+                        done = b
                 continue
-            mul(OPT["gain"][t][a // 1024], z, z, R("gn", t, t + 1))
+            if a >= nd:
+                for c in range(a, b, 512):
+                    e = min(c + 512, b)
+                    group([(R("ps", c, e), R("Gd", 128 * t, 128 * t + 128), R("Tr", o + c - a, o + e - a))], first=t == 0, last=last and e % 512 == 0)
+                    if last and e % 512 == 0:
+                        mul(OPT["evO"][(c - nd) // 512], R(ys, e - 512, e), R("ps", e - 512, e), 1.0)
+                        dma("s", [(R("yo", e - 512, e), R(ys, e - 512, e))])
+                continue
+            mul(OPT["gain"][t][a // 512], z, z, R("gn", t, t + 1))
             if b in stores:
                 dma("s" if t == 0 else "g", [(R("yo", done, b), R("Z", done, b))], add=t > 0)
                 done = b
@@ -735,13 +843,13 @@ def rank_program(g, core, T, topo):
         act(sg, PS(L, 98, 162), AF.Sign, bias=-8.5)
         ks = [post(client(t), partner(t), R("csg", 64 * t, 64 * t + 64), sg, [R(XB[0])] if t == 2 else [])]
         for h in range(2):
-            f = R("F", B * t + 512 * h, B * t + 512 * h + 512)
+            f = R("F", 512 * h, 512 * h + 512)
             act(f, IND(yw, R("cLU", 64 * t + 32 * h, 64 * t + 32 * h + 32)), AF.Identity, bias=col(10), scale=1 / 16.0)
-            ks.append(post(client(t), partner(t), R("cF", B * t + 512 * h, B * t + 512 * h + 512), f))
+            ks.append(post(client(t), partner(t), R("cF", 512 * h, 512 * h + 512), f, also=[R("cA", 1088 * t, 1088 * t + 8)]))
         send_y(t, 1, after=ks)
 
     def update(t):
-        sg, deb = R("csg", 64 * t, 64 * t + 64), R("mA", 1088 * t, 1088 * t + 64)
+        sg, deb = R("csg", 64 * t, 64 * t + 64), R("mA", 0, 64)
         o1, o2 = PS(L, 98, 162), PS(L, 162, 226)
         group([(o1, I, d), (o1, I, deb), (o1, I, sg)])
         group([(o2, p2I, d), (o2, p2I, deb), (o2, p2I, sg)])
@@ -751,19 +859,25 @@ def rank_program(g, core, T, topo):
         for h in range(2):
             a, b = 512 * h, 512 * h + 512
             w = wbank()
-            group([(PS(w), I, R("c192")), (PS(w), I, R("v", a, b)), (PS(w), SB, R("cF", B * t + a, B * t + b))])
+            group([(PS(w), I, R("c192")), (PS(w), I, R("v", a, b)), (PS(w), SB, R("cF", a, b))])
             ts(R("v", a, b), PS(w), -64.0, ALU.max, 64.0, ALU.min)
             w = wbank()
             neg = [(PS(w), nI, R("A", a, b))] + ([(PS(w, 64, 512), nI, R("dvn"))] if h else []) + [(PS(w), nI, R("v", a, b))]
-            group(neg, last=not OPT["cont"])
-            ts(R("cl", a, b), PS(w), -256.0, ALU.max, 256.0, ALU.min)
-            if OPT["cont"]:
-                group([(PS(w), n2I, R("cl", a, b))], first=False)
-            else:
+            group(neg)
+            if OPT["fold"][t][h] == "v":
+                ts(R("cl", a, b), PS(w), -256.0, ALU.max, 256.0, ALU.min)
                 group(neg + [(PS(w), n2I, R("cl", a, b))])
-            mul(OPT["evA"][h], R("A", a, b), PS(w), 1.0)
+                mul(OPT["evA"][h], R("A", a, b), PS(w), 1.0)
+            else:
+                c = R("D", a, b)
+                act(c, PS(w), AF.Abs, bias=256.0)
+                act(c, c, AF.Abs, bias=512.0, scale=-1.0)
+                if OPT["fold"][t][h] == "a":
+                    act(R("A", a, b), c, AF.Identity, bias=-256.0)
+                else:
+                    ts(R("A", a, b), c, -256.0, ALU.add)
         if t + 1 < NB - 1:
-            dma("s", turn("mA", "A", 1088 * (t + 1) + 64, 1088 * (t + 2)))
+            dma("s", turn("mA", "A", 64, 1088))
 
     start()
     for t in range(NB):

import numpy as np
from concourse.mybir import AluOpType as ALU, ActivationFunctionType as AF

S, B, NB = 4096, 1024, 4
WIN = 7216
F32, BF, I32, U16 = "float32", "bfloat16", "int32", "uint16"
OPT = {
    "ch": [512, 512, 1024, 1024, 1024],
    "ways": [[(1024, "M", 0), (2048, "P", 0), (3072, "M", 0), (4096, "P", 0)],
             [(1024, "D", 0), (2048, "D", 0), (3072, "D", 1), (4096, "D", 1)],
             [(1024, "M", 0), (2048, "M", 0), (3072, "P", 1), (4096, "P", 1)],
             [(512, "M", 0), (1024, "P", 0), (2048, "M", 0), (3072, "Q", 0), (3584, "P", 0), (4096, "D", 0)]],
    "npe": 1536,
    "oc": [512, 512, 512, 512],
    "fold": ["aa", "aa", "aa"], "cut": 128,
    "gain": ["aaaaaaaa"] * 4, "two": [0, 0], "end": 512, "stores": [[2048], [1024, 2048, 3072]], "viaA": 1,
    "banks": {"L": 0, "M": [0, 0, 0], "Q": 1, "W": [2, 3, 4], "O": [1]},
    "evA": "aa", "evD": "aa", "evO": "avaa", "nys": 2, "early": 4, "rounds": 6, "seq": 1, "flow": 0, "look": 300.0, "just": 1, "slack": 0.01, "qcut": 64, "swaps": 25000, "heat": 0.004, "tries": 2500, "seed": 1,
    "weigh": {},
    "boost": {"upd": 0.0, "lists": 0.0, "table": 0.0, "y": 0.0, "serve": 0.0, "late": -60.0, "read": -150.0, "out": -100.0, "start": 0.0, "start2": -150.0},
    "fig": {"cy": 0.95, "pe": 0.48, "ga": 1.56, "sc": 3.8, "fix": 60, "hop": 100, "bw": 120.0, "bwon": 350.0, "lbw": 600.0, "row": 15.0,
            "far": 750.0, "wake": 300.0, "call": 600.0},
    "cases": [{}, {"bw": 70.0, "wake": 600.0, "call": 900.0, "row": 30.0}, {"cy": 0.85, "pe": 0.43, "ga": 1.2, "sc": 2.2}, {"cy": 1.2, "pe": 0.62, "ga": 1.9, "sc": 5.2}],
}
XB = ["X0", "X1", "X2", "X0"]
HB = ["X0", "X1", "X2", "Y0"]


def _sb(n, dt):
    return ("sbuf", [128, n], dt)


SCRATCH = {
    "X0": _sb(S, F32), "X1": _sb(S, F32), "X2": _sb(S, F32), "Y0": _sb(S + 8, F32), "Y1": _sb(S + 8, F32),
    "Ys0": _sb(S, F32), "Ys1": _sb(S, F32), "Z": _sb(3072, F32), "Tr": _sb(1024, F32), "inc": _sb(3072, F32), "tab": _sb(2056, F32),
    "W0": _sb(WIN, BF), "W1": _sb(WIN, BF), "zer": _sb(1040, BF), "one": _sb(128, BF), "c192": _sb(512, BF),
    "A": _sb(B, BF), "v": _sb(B + 16, BF), "cmp": _sb(B, BF), "cl": _sb(B, BF), "D": _sb(B, F32), "dvn": _sb(448, BF),
    "mA": _sb(1088, BF), "cA": _sb(3 * 1088, BF), "F": _sb(B, BF), "cF": _sb(B, BF),
    "sg": _sb(3 * 64, BF), "csg": _sb(3 * 64, BF), "LU": _sb(64, U16), "LUs": _sb(3 * 64, U16), "cLU": _sb(3 * 64, U16),
    "hl": _sb(4 * 128, BF), "chl": _sb(4 * 128, BF),
    "OH0": _sb(8 + 1056, BF), "OH1": _sb(8 + 1056, BF), "LP0": _sb(34, U16), "LP1": _sb(34, U16), "ot": _sb(16, BF), "Pw": _sb(B, BF), "G": _sb(8 + B, BF), "val": _sb(528, BF),
    "d": _sb(80, BF), "di": _sb(64, I32), "mi": _sb(64, I32), "ma": _sb(64, I32), "mb": _sb(64, I32), "mu": _sb(64, U16), "gn": _sb(4, F32),
    "IO": _sb(98, F32), "dj": _sb(64, U16), "deu": _sb(32, U16), "jm": _sb(28, F32), "jt": _sb(28, F32),
    "c2": _sb(64, F32), "rst": _sb(98, BF), "cv": _sb(8, BF), "Rb": _sb(264, BF), "xu": _sb(256, U16),
    "Cq": _sb(264, F32), "Hq": _sb(256, BF), "eu0": _sb(256, U16), "eu1": _sb(256, U16), "c38": _sb(256, BF),
    "II": _sb(144, BF), "nI": _sb(128, BF), "p2I": _sb(128, BF), "n2I": _sb(128, BF), "n128I": _sb(128, BF), "n2kI": _sb(128, BF),
    "bl2": _sb(128, BF), "B8": _sb(128, BF), "TrS": _sb(128, BF), "TrSC": _sb(128, BF), "TP": _sb(512, BF),
    "F1": _sb(128, BF), "F2": _sb(128, BF), "V1": _sb(144, BF), "Tri4": _sb(144, F32), "TriC4": _sb(144, F32),
    "J": _sb(160, BF), "TB": _sb(160, BF), "TM": _sb(14 * 128, BF), "mk": _sb(16, F32),
    "WR": _sb(128, BF), "WJ": _sb(128, BF), "WL": _sb(128, BF), "MA": _sb(128, BF), "MB": _sb(128, BF), "ME": _sb(128, BF), "MO": _sb(128, BF),
    "Gd": _sb(512, F32), "pi": _sb(4, I32), "pj": _sb(4, I32), "col": _sb(24, F32),
    "ps": ("psum", [128, 4096], F32),
}
SEMAPHORES = ["cv", "ca", "cp", "cg"] + ["s%d" % i for i in range(112)] + ["r%d" % i for i in range(24)] + ["x%d" % t for t in range(NB)] + ["a%d" % t for t in range(NB)]
PLANNED = []
DEBUG = []
ORDER = {}
SIZE = {F32: 4, BF: 2, I32: 4, U16: 2}


def bits(m):
    return bin(m).count("1")


def hits(a, b):
    return a[0] == b[0] and a[1] < b[2] and b[1] < a[2]


def plan(ops):
    n = len(ops)
    acc = {}
    for k, o in enumerate(ops):
        deps = set(o["after"])
        for lst, isw in ((o["rs"], False), (o["ws"], True)):
            for sp in lst:
                for asp, aw, j in acc.get(sp[0], []):
                    if (aw or isw) and hits(sp, asp):
                        deps.add(j)
        for sp in o["ws"]:
            acc[sp[0]] = [x for x in acc.get(sp[0], []) if not (sp[1] <= x[0][1] and x[0][2] <= sp[2])] + [(sp, True, k)]
        for sp in o["rs"]:
            acc.setdefault(sp[0], []).append((sp, False, k))
        o["deps"] = deps
    succ = [[] for _ in ops]
    for k, o in enumerate(ops):
        for j in o["deps"]:
            succ[j].append(k)
    times = [[timing(o, dict(OPT["fig"], **m)) for o in ops] for m in OPT["cases"]]
    dur = [x[0] + x[1] + max(x[2], x[3]) + x[4] for x in times[0]]
    if OPT["seq"]:
        lev = [OPT["boost"].get(ops[k]["tag"], 0.0) - k for k in range(n)]
        for k in range(n - 1, -1, -1):
            lev[k] = max([lev[k]] + [lev[j] + 1e-3 for j in succ[k]])
    else:
        lev = [0.0] * n
        for k in range(n - 1, -1, -1):
            lev[k] = dur[k] * OPT["weigh"].get(ops[k]["tag"], 1.0) + max([lev[j] for j in succ[k]] + [0.0])
    hold = []
    for o, x in zip(ops, times[0]):
        h = [(o["e"], 0.0, x[0])] if x[0] else []
        h += [(b, 0.0, x[0] + (0 if o["e"] == "p" else 100)) for b in o["banks"]]
        if x[2]:
            h.append(("dma", x[0] + x[1], x[2]))
        if x[3]:
            h.append((o["move"][2], x[0] + x[1], x[3]))
        hold.append(h)
    pred = [sorted(o["deps"]) for o in ops]

    eng = [o["e"] for o in ops]
    banks = [sorted(o["banks"]) for o in ops]
    link = [o["move"] and o["move"][2] for o in ops]
    none = (0.0, -1)

    def replay(order, tm, why=None, begin=None):
        done, at, last = [0.0] * n, {}, [-1] * n
        for k in order:
            c, pre, move, wire, post = tm[k]
            e = eng[k]
            t, by = at.get(e, none) if c else none
            by = -2 - by
            for j in pred[k]:
                if done[j] > t:
                    t, by = done[j], j
            for b in banks[k]:
                u = at.get(b)
                if u and eng[u[1]] != e and u[0] > t:
                    t, by = u[0], -2 - u[1]
            if begin:
                begin[k] = t
            t += c
            if c:
                at[e] = (t, k)
            if move or wire:
                t += pre
                if move:
                    u = at.get("dma", none)
                    if u[0] > t:
                        t, by = u[0], -2 - u[1]
                    at["dma"] = (t + move, k)
                end = t + move
                if wire:
                    u = at.get(link[k], none)
                    if u[0] > t:
                        t, by = u[0], -2 - u[1]
                    at[link[k]] = (t + wire, k)
                    end = max(end, t + wire)
                t = end
            done[k] = t + post
            last[k] = by
            for b in banks[k]:
                at[b] = (done[k], k)
        end = max(done)
        if why is not None:
            k = done.index(end)
            while k >= 0:
                j = last[k]
                if j < -1:
                    j = -2 - j
                    why.append((j, k))
                k = j
        return end

    def judge(start):
        order = sorted(range(n), key=lambda k: (start[k], k))
        return [replay(order, tm) for tm in times]

    def place(prio, back):
        before, after = (succ, pred) if back else (pred, succ)
        left = [len(x) for x in before]
        ready = [0.0] * n
        start = [0.0] * n
        busy = {}
        free = [k for k in range(n) if not left[k]]
        while free:
            k = max(free, key=lambda j: prio[j])
            free.remove(k)
            hs = [(r, dur[k] - a - w if back else a, w) for r, a, w in hold[k]]
            t = ready[k]
            moved = True
            while moved:
                moved = False
                for r, a, w in hs:
                    line = busy.setdefault(r, [])
                    i, j = 0, len(line)
                    while i < j:
                        m = (i + j) // 2
                        if line[m][1] > t + a + 1e-6:
                            j = m
                        else:
                            i = m + 1
                    while i < len(line) and line[i][0] < t + a + w - 1e-6:
                        t = line[i][1] - a
                        moved = len(hs) > 1
                        i += 1
            for r, a, w in hs:
                line = busy[r]
                line.append((t + a, t + a + w))
                if len(line) > 1 and line[-2] > line[-1]:
                    line.sort()
            start[k] = t
            for j in after[k]:
                ready[j] = max(ready[j], t + dur[k])
                left[j] -= 1
                if not left[j]:
                    free.append(j)
        return start, max(start[k] + dur[k] for k in range(n))

    def flow(prio, look):
        left = [len(x) for x in pred]
        ready = [0.0] * n
        start = [0.0] * n
        at = {}
        free = {}
        for k in range(n):
            if not left[k]:
                free.setdefault(ops[k]["e"], []).append(k)
        for _ in range(n):
            pick = None
            for e, line in free.items():
                if line:
                    can = [max([ready[k]] + [at.get(r, 0.0) - a for r, a, w in hold[k]]) for k in line]
                    t = min(can)
                    if pick is None or t < pick[0]:
                        pick = (t, e, can)
            t, e, can = pick
            i = max((i for i in range(len(can)) if can[i] <= t + look), key=lambda i: prio[free[e][i]])
            k = free[e].pop(i)
            start[k] = can[i]
            for r, a, w in hold[k]:
                at[r] = can[i] + a + w
            for j in succ[k]:
                ready[j] = max(ready[j], can[i] + dur[k])
                left[j] -= 1
                if not left[j]:
                    free.setdefault(ops[j]["e"], []).append(j)
        return start, max(start[k] + dur[k] for k in range(n))

    start, span = flow(lev, OPT["look"]) if OPT["flow"] else place(lev, False)
    base = judge(start)

    def score(start):
        return sum(a / b for a, b in zip(judge(start), base))

    best = (score(start), start, span)
    for _ in range(OPT["rounds"]):
        back, _s = place([start[k] + dur[k] for k in range(n)], True)
        start, span = place([back[k] + dur[k] for k in range(n)], False)
        best = min(best, (score(start), start, span))
    rnd = np.random.RandomState(OPT["seed"])
    cur = best
    tags = np.array([o["tag"] for o in ops])
    for it in range(OPT["tries"]):
        at = np.array(cur[1])
        near = np.abs(at - rnd.rand() * cur[2]) < (4000.0, 8000.0, 15000.0)[rnd.randint(3)]
        if it % 3 == 0:
            at = at + near * (tags == tags[rnd.randint(n)]) * 2500.0 * rnd.randn()
        else:
            at = at + near * rnd.randn(n) * (200.0, 600.0, 1500.0)[rnd.randint(3)]
        start, span = place((-at).tolist(), False)
        if it % OPT["just"] == 0:
            back, _s = place([start[k] + dur[k] for k in range(n)], True)
            start, span = place([back[k] + dur[k] for k in range(n)], False)
        if span < cur[2] * 1.03:
            new = (score(start), start, span)
            if new[0] <= cur[0] + OPT["slack"] * (1.0 - it / OPT["tries"]) * rnd.rand():
                cur = new
            best = min(best, new)
    order = sorted(range(n), key=lambda k: (best[1][k], k))
    now = top = (best[0], order)
    for it in range(OPT["swaps"]):
        order = now[1]
        why = []
        replay(order, times[rnd.randint(len(times))], why)
        j, k = why[rnd.randint(len(why))]
        a, b = order.index(j), order.index(k)
        if rnd.rand() < 0.3:
            a = max(0, a - rnd.randint(12))
        part = order[a:b + 1]
        if rnd.rand() < 0.5:
            take = {k}
            for x in part[::-1]:
                if x in take:
                    take.update(pred[x])
            if j in take:
                continue
            part = [x for x in part if x in take] + [x for x in part if x not in take]
        else:
            take = {j}
            for x in part:
                if x in take:
                    take.update(succ[x])
            if k in take:
                continue
            part = [x for x in part if x not in take] + [x for x in part if x in take]
        order = order[:a] + part + order[b + 1:]
        new = (sum(replay(order, tm) / u for tm, u in zip(times, base)), order)
        if new[0] <= now[0] + OPT["heat"] * (1.0 - it / OPT["swaps"]) * rnd.rand():
            now = new
        if new[0] < top[0]:
            top = new
    begin = [0.0] * n
    replay(top[1], times[0], None, begin)
    PLANNED.append([round(x / 1000.0, 1) for x in [best[2]] + [replay(top[1], tm) for tm in times]])
    DEBUG.append((ops, dur, begin))
    return top[1]


def timing(o, p):
    c = o["cost"]
    busy = c[0] + p["cy"] * (c[1] + c[2] * p["ga"] + c[3] * p["sc"]) + c[4] * p["pe"]
    if o["move"] is None:
        return (busy, 0.0, 0.0, 0.0, p["hop"])
    kind, by, link = o["move"]
    if kind == "local":
        return (busy, 900.0, by / p["lbw"] + 8 * p["row"] * link, 0.0, 900.0 + p["hop"])
    if kind == "landed":
        return (0.0, 0.0, 0.0, 0.0, p["far"] + p["wake"])
    wire = by / p["bw"] if link else 0.0
    if kind == "onward":
        return (0.0, 2 * p["far"] + p["wake"] + p["call"], 0.0, wire, 0.0)
    return (p["call"], p["far"], by / (p["bw"] if link else p["bwon"]) + (16 if link else 8) * p["row"], wire, p["hop"])


def helpers(core, dst, T, topo):
    every = range(128)
    idle = [c for c in every if c not in T.cores and topo.die(c) == topo.die(core)]
    far = [c for c in idle if topo.mates(topo.chip(c), topo.chip(dst)) and topo.may_write(c, dst)] if topo.chip(dst) != topo.chip(core) else []
    if not far:
        return {"D": []}
    near = [c for c in idle if topo.chip(c) == topo.chip(core)]
    out = [c for c in near if topo.may_write(c, far[0])][0]
    rest = [c for c in near if c != out]
    return {"D": [], "P": rest[:1], "Q": rest[1:2], "M": [out, far[0]]}


def handed(core, dst, T, topo):
    return helpers(core, dst, T, topo).get("Q", []) if OPT["viaA"] else []


def pieces(t):
    a = 0
    for k, (b, way, late) in enumerate(OPT["ways"][t]):
        yield k, a, b, way, late
        a = b


def handing_on(g, core, T, topo):
    n_r = len(T.cores)
    left = 0
    for t in range(NB):
        for r, src in enumerate(T.cores):
            dst = T.cores[(r + 1 + t % (n_r - 1)) % n_r]
            if t < NB - 1 and core in handed(src, dst, T, topo):
                rid, pid, _ = topo.addr(dst)
                slot = T.cA[:, 1088 * t:1088 * t + 1088]
                g.wait_ge(T.sem["a%d" % t], bits(topo.mask(src, core)))
                g.remote_dma(slot, slot, T.sem["a%d" % t], T.sem["cg"], pid, rid, topo.mask(core, dst))
                left += bits(topo.mask(core, dst))
        for k, a, b, way, late in pieces(t):
            for r, src in enumerate(T.cores):
                dst = T.cores[(r - 1 - t % (n_r - 1)) % n_r]
                stops = [src] + helpers(src, dst, T, topo)[way] + [dst]
                if core in stops:
                    i = stops.index(core)
                    to = stops[i + 1]
                    rid, pid, _ = topo.addr(to)
                    g.wait_ge(T.sem["s%d" % (8 * t + k)], bits(topo.mask(stops[i - 1], core)))
                    g.remote_dma(T[XB[t] if to == dst else HB[t]][:, a:b], T[HB[t]][:, a:b], T.sem["x%d" % t if to == dst else "s%d" % (8 * t + k)],
                                 T.sem["cg"], pid, rid, topo.mask(core, to))
                    left += bits(topo.mask(core, to))
    if left:
        g.wait_ge(T.sem["cg"], left)


def rank_program(g, core, T, topo):
    rank = T.rank_of(core)
    if rank is None:
        handing_on(g, core, T, topo)
        return
    n_r = len(T.cores)
    Q = {"v": g.vector, "a": g.scalar, "p": g.tensor, "s": g.sync, "g": g}
    csem = {"v": "cv", "a": "ca", "p": "cp", "g": "cg"}
    kind = {k: SCRATCH[k][2] for k in SCRATCH}
    kind.update({"am": BF, "ve": BF, "du": I32, "mp": I32, "gain": F32, "yo": F32})
    ops = []
    nsem = [0, 0]
    tag = ["start"]
    now = [0]
    fix = OPT["fig"]["fix"]
    CH = OPT["ch"]
    NPE = OPT["npe"]
    BK = OPT["banks"]

    def R(name, a=None, b=None, s=1, p=None):
        if name in ("OH", "LP"):
            name += str(now[0] % 2)
        t = T[name]
        a0 = 0 if a is None else a
        b0 = t.shape[1] if b is None else b
        rows = slice(None) if p is None else slice(p[0], p[1])
        return (t[rows, a0:b0:s] if s != 1 else t[rows, a0:b0], name, a0, b0, None, len(range(a0, b0, s)))

    def RS(name, a, n, s):
        return R(name, a, a + (n - 1) * s + 1, s)

    def PS(bank, a=0, b=512, s=1):
        return R("ps", 512 * bank + a, 512 * bank + b, s)

    def IND(win, off):
        return (win[0].indirect(off[0]), win[1], win[2], win[3], off, 16 * off[5])

    def ap(x):
        return x[0] if isinstance(x, tuple) else x

    def newsem():
        nsem[0] += 1
        return "s%d" % (nsem[0] - 1)

    def rec(e, fns, reads, writes, cost, move=None, tok=None, after=(), pre=None):
        reads = [x for x in reads if isinstance(x, tuple)]
        reads = reads + [x[4] for x in reads + list(writes) if x[4] is not None]
        rs, ws = [x[1:4] for x in reads], [x[1:4] for x in writes]
        banks = set(b for x in rs + ws if x[0] == "ps" for b in range(x[1] // 512, (x[2] + 511) // 512))
        ops.append({"e": e, "fns": fns, "rs": rs, "ws": ws, "cost": cost, "move": move, "tok": tok,
                    "after": list(after), "banks": banks, "pre": pre, "tag": tag[0]})
        return len(ops) - 1

    def price(o, i, base):
        if o[4] is not None:
            return (fix, 0, 0, o[5], 0)
        if i[4] is not None:
            return (fix, 0, o[5], 0, 0)
        return (fix, max(64, o[5] * base), 0, 0, 0)

    def half(*xs):
        return 0.5 if all(SIZE[kind[x[1]]] == 2 for x in xs) else 1.0

    def dma(e, pairs, add=False, after=(), pre=None):
        s = newsem()
        if add:
            fns = [lambda o=o, i=i: Q[e].dma_start(o[0], i[0], accum_op=ALU.add).then_inc(T.sem[s], 16) for o, i in pairs]
        else:
            fns = [lambda o=o, i=i: Q[e].dma_start(o[0], i[0]).then_inc(T.sem[s], 16) for o, i in pairs]
        by = sum(int(np.prod(i[0].shape)) * SIZE[kind[o[1]]] for o, i in pairs) * (2 if add else 1)
        rec(e, fns, [p[1] for p in pairs], [p[0] for p in pairs], (len(pairs) * (1000 if e == "g" else 60), 0, 0, 0, 0), ("local", by, len(pairs)),
            tok=(s, 16 * len(pairs)), after=after, pre=pre)

    def turn(o, i, a=None, b=None, c=None, d=None):
        return [(R(o, a, b, p=(16, 128)), R(i, c, d, p=(0, 112))), (R(o, a, b, p=(0, 16)), R(i, c, d, p=(112, 128)))]

    def back(o, i, n):
        return [(R(o, 0, n, p=(0, 112)), R(i, p=(16, 128))), (R(o, 0, n, p=(112, 128)), R(i, p=(0, 16)))]

    def cp(o, i):
        rec("v", [lambda: g.vector.tensor_copy(o[0], i[0])], [i], [o], price(o, i, half(o, i)))

    def tt(o, a, b, f):
        rec("v", [lambda: g.vector.tensor_tensor(o[0], a[0], b[0], f)], [a, b], [o], price(o, a, 1 if "ps" in (a[1], b[1]) else 2))

    def ts(o, a, s1, f0, s2=None, f1=None, also=()):
        if f1 is None:
            fn = lambda: g.vector.tensor_scalar(o[0], a[0], ap(s1), None, f0)
        else:
            fn = lambda: g.vector.tensor_scalar(o[0], a[0], ap(s1), ap(s2), f0, f1)
        rec("v", [fn], [a, s1, s2] + list(also), [o], price(o, a, half(o, a)))

    def scan(o, a, b, ini, f0, f1, after=(), pre=None):
        rec("v", [lambda: g.vector.tensor_tensor_scan(o[0], a[0], b[0], ap(ini), f0, f1)], [a, b, ini], [o], price(o, a, 1), after=after, pre=pre)

    def ms(o, c):
        rec("v", [lambda: g.vector.memset(o[0], c)], [], [o], price(o, o, half(o)))

    def act(o, i, f=AF.Copy, bias=None, scale=1.0, also=()):
        if bias is None:
            fn = lambda: g.scalar.activation(o[0], i[0], f, scale=ap(scale))
        else:
            fn = lambda: g.scalar.activation(o[0], i[0], f, bias=ap(bias), scale=ap(scale))
        rec("a", [fn], [i, bias, scale] + list(also), [o], price(o, i, 1))

    def mul(e, o, i, c):
        if e == "a":
            act(o, i, AF.Copy, scale=c)
        else:
            ts(o, i, c, ALU.mult)

    def group(items, first=True, last=True, hold=()):
        end = len(items) - 1
        fns = [lambda k=k, o=o, l=l, r=r: g.tensor.matmul(o[0], l[0], r[0], first and k == 0, last and k == end) for k, (o, l, r) in enumerate(items)]
        cost = (0, 0, 0, 0, sum(max(64, r[5]) * (4 if kind[r[1]] == F32 else 1) for o, l, r in items))
        rec("p", fns, [x for o, l, r in items for x in (l, r)], [o for o, l, r in items] + list(hold), cost)

    def sel(o, i, pat, cmp_op, base, cm):
        rec("g", [lambda: g.affine_select(o[0], i[0], pat, cmp_op, 0.0, base, cm)], [i], [o], (170, 2 * o[5], 0, 0, 0))

    def iota(o, pat, base, cm):
        if kind[o[1]] == I32:
            fn = lambda: g.iota(o[0], pat, base, cm)
        else:
            fn = lambda: g.iota(o[0], pat, base, cm, allow_small_or_imprecise_dtypes=True)
        rec("g", [fn], [], [o], (130, 2 * o[5], 0, 0, 0))

    def partner(t):
        return T.cores[(rank + 1 + t % (n_r - 1)) % n_r]

    def client(t):
        return T.cores[(rank - 1 - t % (n_r - 1)) % n_r]

    def send(dst, o, i, rsem, ltok, guard=(), after=(), also=()):
        rid, pid, _ = topo.addr(dst)
        m = topo.mask(core, dst)
        link = None if topo.chip(dst) == topo.chip(core) else "port"
        return rec("g", [lambda: g.remote_dma(o[0], i[0], T.sem[rsem], T.sem[ltok[0]], pid, rid, m)], [i] + list(also), list(guard), (0, 0, 0, 0, 0),
                   ("remote", i[5] * SIZE[kind[i[1]]] * 128, link), tok=ltok, after=after)

    def landed(o, rsem, count, sends):
        rec("r", [], [], [o], (0, 0, 0, 0, 0), ("landed", 0, None), tok=(rsem, count), after=sends)

    def newr():
        nsem[1] += 1
        return "r%d" % (nsem[1] - 1)

    def post(dst, src, o, i, guard=(), also=()):
        r = newr()
        k = send(dst, o, i, r, (newsem(), bits(topo.mask(core, dst))), guard, also=also)
        landed(o, r, bits(topo.mask(src, core)), [k])
        return k

    I, SB = R("II", 0, 128), R("II", 16, 144)
    nI, p2I, n2I, n128I = R("nI"), R("p2I"), R("n2I"), R("n128I")
    d, dprev = R("d", 8, 72), R("d", 7, 71)
    L = BK["L"]
    wide = [0]

    def wbank():
        wide[0] += 1
        return BK["W"][wide[0] % len(BK["W"])]

    def col(k):
        return R("col", k, k + 1)

    def TS(s):
        if s < 0:
            return R("TM", 128 * (-s - 1), 128 * -s)
        if s > 8:
            return R("TM", 128 * (22 - s), 128 * (23 - s))
        return R("TB", 15 - s, 143 - s)

    def clear(w):
        dma("s", [(R(w, a, a + 1032), R("zer", 0, 1032)) for a in range(0, 4128, 1032)])

    def start():
        dma("s", back("di", "du", 64))
        dma("s", back("A", "am", B))
        dma("s", [(R("mA", 64, 1088), R("am"))])
        one = R("one")
        ms(one, 1.0)
        ms(R("zer"), 0.0)
        clear("W0")
        iota(R("pi", 0, 1), [[1, 1]], 0, 1)
        iota(R("J"), [[1, 160]], 0, 0)
        sel(R("bl2"), one, [[-16, 8], [0, 16]], ALU.is_ge, 0, 1)
        sel(R("bl2"), R("bl2"), [[16, 8], [0, 16]], ALU.is_ge, 15, -1)
        for f in range(2):
            sel(R("TP", 128 * f, 128 * f + 128), R("bl2"), [[16, 8], [2, 16]], ALU.is_gt, -16 * f, -1)
            mul("a", R("TP", 256 + 128 * f, 384 + 128 * f), R("TP", 128 * f, 128 * f + 128), -1.0)
        cp(col(13), R("pi", 0, 1))
        ts(I, R("J", 0, 128), col(13), ALU.is_equal)
        sel(R("TrS"), R("bl2"), [[1, 128]], ALU.is_gt, 0, -1)
        sel(R("TrSC"), R("bl2"), [[-1, 128]], ALU.is_ge, 0, 1)
        sel(R("Tri4", 16, 144), R("bl2"), [[1, 128]], ALU.is_ge, 0, -1)
        sel(R("TriC4", 16, 144), R("bl2"), [[-1, 128]], ALU.is_gt, 0, 1)
        ms(R("d"), 0.0)
        cp(d, R("di"))
        cp(R("dj"), R("di"))
        ts(R("pj", 0, 1), R("pi", 0, 1), 7, ALU.bitwise_and)
        ts(R("pj", 1, 2), R("pi", 0, 1), 15, ALU.bitwise_and)
        ts(R("pj", 2, 3), R("pi", 0, 1), 8, ALU.bitwise_and)
        cp(R("col", 0, 3), R("pj", 0, 3))
        ts(col(3), col(0), 0.0, ALU.is_equal)
        ts(R("ot"), R("J", 0, 16), col(0), ALU.is_equal, col(3), ALU.max)
        ts(R("ot", 0, 1), col(0), 2.0, ALU.is_equal, col(3), ALU.max)
        ts(R("ot", 8, 9), col(0), 6.0, ALU.is_equal, col(3), ALU.max)
        for oh in ("OH0", "OH1"):
            act(R(oh, 0, 8), R("zer", 0, 8))
            ts(R(oh, 1032, 1064), R("J", 0, 32), 0.0, ALU.is_equal, col(3), ALU.mult)
        ms(R("rst"), 1.0)
        ms(R("rst", 33, 34), 0.0)
        ms(R("cv", 0, 1), -512.0)
        ts(R("cv", 1, 2), col(1), 1.0, ALU.add)
        ms(R("cv", 2, 3), 8192.0)
        ts(col(4), R("pi", 0, 1), col(2), ALU.subtract, 15.0, ALU.add)
        ts(R("TB"), R("J"), col(4), ALU.is_equal, 0.5, ALU.mult)
        ts(R("mk", 0, 7), R("J", 1, 8), col(0), ALU.is_le)
        ts(R("mk", 7, 14), R("J", 1, 8), col(0), ALU.is_gt)
        for s in range(1, 8):
            mul("va"[s % 2], TS(-s), R("TB", 15 + s, 143 + s), R("mk", s - 1, s))
            mul("av"[s % 2], TS(16 - s), R("TB", s - 1, 127 + s), R("mk", 6 + s, 7 + s))
        ts(nI, I, -1.0, ALU.mult)
        tt(R("F1"), R("Tri4", 16, 144), R("TrS"), ALU.add)
        tt(R("F2"), R("TriC4", 16, 144), R("TrSC"), ALU.add)
        ms(R("Rb", 0, 8), 0.0)
        ms(R("tab", 0, 2), 0.0)
        ms(R("tab", 2050, 2056), 0.0)
        ts(col(5), col(3), 1024.0, ALU.mult, col(0), ALU.add)
        rec("v", [lambda: g.vector.reciprocal(col(6)[0], col(5)[0])], [col(5)], [col(6)], (200, 6, 0, 0, 0))
        ts(col(6), col(6), 256.0, ALU.mult, -0.49, ALU.add)
        cp(R("pj", 3, 4), col(6))
        ts(col(7), R("pj", 3, 4), 1 / 512.0, ALU.mult)
        ts(col(8), col(0), -1.0, ALU.mult, col(7), ALU.mult)
        ts(col(9), col(3), -0.5, ALU.mult, 0.5, ALU.add)
        tt(col(9), col(9), col(8), ALU.add)
        tt(col(8), col(9), col(7), ALU.add)
        mul("a", R("WR"), R("bl2"), col(7))
        mul("a", R("WJ"), R("bl2"), col(8))
        mul("a", R("WL"), R("bl2"), col(9))
        for y in ("Y0", "Y1"):
            ms(R(y, S, S + 8), 0.0)
        tag[0] = "start2"
        dma("s", back("v", "ve", B))
        dma("s", back("mi", "mp", 64) + [(R("gn"), R("gain"))])
        clear("W1")
        iota(R("jm"), [[16, 28]], -448, 0)
        sel(R("B8"), one, [[-8, 16], [0, 8]], ALU.is_ge, 0, 1)
        sel(R("B8"), R("B8"), [[8, 16], [0, 8]], ALU.is_ge, 7, -1)
        cp(R("II", 128, 144), R("II", 0, 16))
        mul("a", p2I, I, 2.0)
        mul("a", n2I, I, -2.0)
        mul("a", n128I, I, -128.0)
        mul("a", R("n2kI"), I, -2048.0)
        ms(R("c192"), -192.0)
        ms(col(10), 191.5 + 2.0 ** -13)
        ms(col(11), 127.5 + 2.0 ** -13 - 77.0 / 4096)
        ms(R("v", B, B + 16), 0.0)
        ts(R("jm"), R("jm"), col(1), ALU.add)
        ms(R("V1"), 0.0)
        cp(R("V1", 15, 127, 16), R("bl2", 16, 128, 16))
        cp(R("V1", 127, 128), R("bl2", 0, 1))
        cp(R("Tri4", 0, 16), R("Tri4", 128, 144))
        cp(R("TriC4", 0, 16), R("TriC4", 128, 144))
        ms(R("Cq", 0, 8), 0.0)
        ms(R("c38"), 38.5)
        ms(R("G", 0, 8), 0.0)
        ms(R("val", 512, 528), 0.0)
        tt(R("MB"), R("B8"), I, ALU.subtract)
        tt(R("MA"), I, R("MB"), ALU.subtract)
        ts(col(12), col(2), 51.0 / 8, ALU.mult, -64.0, ALU.add)
        tt(col(12), col(12), col(0), ALU.mult)
        mul("a", R("ME"), I, col(12))
        ms(R("MO"), 0.0)
        ts(R("MO", 0, 128, 8), R("B8", 0, 128, 8), col(12), ALU.mult)
        dma("s", [(R("Pw"), R("zer", 0, B))])
        ts(R("ma"), R("mi"), 15, ALU.bitwise_and)
        ts(R("mb"), R("mi"), 4, ALU.logical_shift_right)
        ts(R("ma"), R("ma"), 64.0, ALU.mult)
        tt(R("mb"), R("ma"), R("mb"), ALU.add)
        cp(R("mu"), R("mb"))
        if NPE:
            for t in range(NB):
                mul("a", R("Gd", 128 * t, 128 * t + 128), I, R("gn", t, t + 1))

    def scatter(t, src, step):
        w = "W%d" % (t % 2)
        cp(IND(R(w, 16, WIN), R("LP", 0, 16)), RS(src[0], src[1], 256, step))
        return lambda: cp(IND(R(w, 528, WIN), R("LP", 16, 33)), RS(src[0], src[1] + 256 * step, 272, step))

    def unfold(t, o, a, b):
        w = "W%d" % (t % 2)
        group([(o, TS(s), RS(w, 16 + 16 * a + s, b - a, 16)) for s in range(-7, 16)])

    def lists(t):
        act(R("OH", 8, 520), IND(R("ot"), R("dj", 0, 32)))
        group([(PS(L, 0, 33), R("TP", 128 * k, 128 * k + 128), RS("d", 8 + k % 2 - 2 * (k // 2), 33, 2)) for k in range(4)]
              + [(PS(L, 0, 33), R("bl2"), RS("d", 6 + f, 33, 2)) for f in range(2)] + [(PS(L, 16, 33, 16), I, R("cv", 0, 2))])
        group([(PS(L, 33, 97), R("TrS"), d), (PS(L, 33, 97), R("TrSC"), dprev), (PS(L, 33, 34), I, R("cv", 2, 3))])
        scan(R("IO", 0, 97), R("rst", 0, 97), PS(L, 0, 97), 0.0, ALU.mult, ALU.add)
        cp(R("LP", 0, 33), R("IO", 0, 33))
        second = scatter(t, ("OH", 8), 2)

        def places(k, a, b):
            m = BK["M"][k]
            s1, s2 = (PS(m, 256, 256 + b - a), PS(m, 384, 384 + b - a)) if b - a <= 128 else (PS(m, 0, b - a), PS(m, 256, 256 + b - a))
            unfold(t, s1, a, b)
            scan(R("Rb", 8 + a, 8 + b), s1, R("zer", 0, b - a), R("Rb", 7 + a, 8 + a), ALU.add, ALU.add)
            group([(s2, R("F1"), R("Rb", 8 + a, 8 + b)), (s2, R("F2"), R("Rb", 7 + a, 7 + b))])
            cp(R("xu", a, b), s2)

        places(0, 0, 32)
        table(0, 511)
        act(R("OH", 520, 1032), IND(R("ot"), R("dj", 32, 64)))
        second()
        places(1, 32, OPT["cut"])
        table(511, 1023)
        group([(PS(L, 226, 227), R("WR"), R("OH", 1031, 1032))])
        group([(PS(L, 227, 228), R("WL"), R("OH", 1031, 1032))])
        group([(PS(L, 228, 229), I, R("A", 0, 1)), (PS(L, 228, 229), nI, R("A", B - 1, B))])
        ts(R("tab", 2048, 2050), PS(L, 226, 228), PS(L, 228, 229), ALU.mult)
        if OPT["cut"] < 256:
            places(2, OPT["cut"], 256)
        tag[0] = "late"
        on = R("IO", 33, 97)
        hi, lo = R("hl", 128 * t, 128 * t + 64), R("hl", 128 * t + 64, 128 * t + 128)
        act(hi, on)
        tt(lo, on, hi, ALU.subtract)
        post(client(t), partner(t), R("chl", 128 * t, 128 * t + 128), R("hl", 128 * t, 128 * t + 128))
        if t < NB - 1:
            ts(R("LU"), on, -8192.0, ALU.add, 4096.0, ALU.min)
            dma("s", turn("LUs", "LU", 64 * t, 64 * t + 64))
            post(partner(t), client(t), R("cLU", 64 * t, 64 * t + 64), R("LUs", 64 * t, 64 * t + 64))
            ts(R("mA", 0, 64), on, 8192.0 + 4096.0, ALU.is_ge)
            o, i = R("cA", 1088 * t, 1088 * t + 1088), R("mA")
            via = handed(core, partner(t), T, topo)
            to = (via + [partner(t)])[0]
            j = send(to, o, i, "a%d" % t, (newsem(), bits(topo.mask(core, to))))
            if via:
                j = rec("f", [], [], [], (0, 0, 0, 0, 0), ("onward", 1088 * 256, "port"), after=[j])
            landed(o, "a%d" % t, bits(topo.mask(([client(t)] + handed(client(t), core, T, topo))[-1], core)), [j])
            tt(R("jt"), R("mA", 36, 64), R("jm"), ALU.mult)
            ts(R("deu", 0, 28), R("jt"), 1024.0, ALU.add)
            act(R("dvn"), IND(R("v"), R("deu", 0, 28)), AF.Copy, scale=-1.0)

    def table(a, b):
        n = b - a
        w = wbank()
        group([(PS(w, 0, n), nI, R("A", a, b)), (PS(w, 0, n), I, R("A", a + 1, b + 1))])
        mul(OPT["evD"][a // 500], R("D", a, b), PS(w, 0, n), 1.0)
        for m, at in (("WR", 2), ("WJ", 3)):
            w = wbank()
            group([(PS(w, 0, n), R(m), R("OH", 8 + a, 8 + b))])
            tt(RS("tab", 2 * a + at, n, 2), PS(w, 0, n), R("D", a, b), ALU.mult)

    edges = [sum(CH[:k]) for k in range(len(CH) + 1)]
    ytok, ysend, yend = {}, {}, {}
    ring = [0]
    before = {}

    def send_y(t, phase, after=()):
        for k, a, b, way, late in pieces(t):
            if late == phase:
                stops = helpers(core, client(t), T, topo)[way]
                o, sem = (R(HB[t], a, b), "s%d" % (8 * t + k)) if stops else (R(XB[t], a, b), "x%d" % t)
                j = send((stops + [client(t)])[0], o, R("Y%d" % (t % 2), a, b), sem, ytok[t], after=list(after) + before.get(way, []))
                ysend[t].append(j)
                before[way] = [j]
                for link in {"D": [], "P": ["port"], "Q": ["port"], "M": ["mate out", "mate in"]}[way]:
                    j = rec("f", [], [], [], (0, 0, 0, 0, 0), ("onward", (b - a) * 512, link), after=[j])
                yend[t].append(j)

    def landed_x(t):
        last = [([partner(t)] + helpers(partner(t), core, T, topo)[way])[-1] for k, a, b, way, late in pieces(t)]
        landed(R(XB[t]), "x%d" % t, sum(bits(topo.mask(c, core)) for c in last), yend[t])

    def make_y(t):
        first = [(helpers(core, client(t), T, topo)[way] + [client(t)])[0] for k, a, b, way, late in pieces(t)]
        ytok[t] = (newsem(), sum(bits(topo.mask(core, c)) for c in first))
        ysend[t], yend[t] = [], []
        y = "Y%d" % (t % 2)
        for k in range(len(CH)):
            a, b = edges[k], edges[k + 1]
            o = 1024 * (ring[0] % 3)
            ring[0] += 1
            act(R("inc", o, o + b - a), IND(R("tab", 0, 1024 if b <= 512 else None), R("xu", a // 16, b // 16)))
            scan(R(y, a, b), R("inc", o, o + b - a), R("zer", 0, b - a), R("A", 0, 1) if k == 0 else R(y, a - 1, a), ALU.add, ALU.add,
                 after=ysend[t - 2] if t > 1 else ())
        send_y(t, 0)

    def y_turn(t):
        for k in range(4):
            late = t == NB - 1 and k >= OPT["early"]
            dma("s", turn("Ys%d" % (t % OPT["nys"]), "Y%d" % (t % 2), 1024 * k, 1024 * k + 1024, 1024 * k, 1024 * k + 1024),
                after=ysend[t] if late else (), pre=ytok[t] if late else None)

    def reading(t):
        q = BK["Q"]
        pw = R("Pw")[1:]
        dma("s", [((T.Pw[8 * h:112:16, :],) + pw, R("chl", 128 * t + 64 * h, 128 * t + 64 * h + 64, p=(16, 128))) for h in range(2)]
            + [((T.Pw[112 + 8 * h:113 + 8 * h, :],) + pw, R("chl", 128 * t + 64 * h, 128 * t + 64 * h + 64, p=(0, 16))) for h in range(2)])
        act(R("G", 8, 8 + B), IND(R("Pw"), R("mu")))
        group([(PS(q), R("MA"), RS("G", 8, 512, 2)), (PS(q), R("MB"), RS("G", 9, 512, 2)), (PS(q), nI, RS("G", 7, 512, 2)),
               (PS(q), R("ME"), RS("OH", 8, 512, 2)), (PS(q), R("MO"), RS("OH", 7, 512, 2))])
        tt(R("val", 0, 512), PS(q), RS("OH", 8, 512, 2), ALU.mult)
        scatter(t, ("val", 0), 1)()
        for c in range(0, 256, OPT["qcut"]):
            unfold(t, PS(q, c, c + OPT["qcut"]), c, c + OPT["qcut"])
        scan(R("Cq", 8, 264), PS(q, 0, 256), R("c38"), 0.0, ALU.add, ALU.add)
        if t < NB - 2:
            clear("W%d" % (t % 2))
        o = PS(q, 256, 512)
        sums = [(o, R("Tri4", 0, 128), R("Cq", 8, 264)), (o, R("TriC4", 0, 128), R("Cq", 7, 263))]
        group(sums)
        act(R("Hq"), o, AF.Identity, bias=col(11), scale=1 / 2048.0)
        group(sums + [(o, R("n2kI"), R("Hq"))])
        ts(R("eu%d" % (t % 2)), o, 2.0, ALU.mult, 128.0 * 4096.0 - 77.0, ALU.add)

    tring = [0]

    def output(t):
        last = t == NB - 1
        ys = "Ys%d" % (t % OPT["nys"])
        nd = S - NPE
        n2 = nd - OPT["two"][t // 2]
        stores = [x for x in OPT["stores"][last] if x < nd] + [n2, nd]
        done = 0
        oc = OPT["oc"][t]
        cuts = sorted(set(list(range(0, S + 1, oc)) + [n2, nd] + ([S - OPT["end"]] if last else [])))
        for a, b in zip(cuts[:-1], cuts[1:]):
            o = tring[0] if tring[0] + b - a <= 1024 else 0
            if a < n2 or (a < nd and t % 2 == 0):
                z = R("Z", a, b)
            else:
                z = R("Tr", o, o + b - a)
                tring[0] = o + b - a
            tt(z, IND(R(XB[t], 0, S), R("eu%d" % (t % 2), a // 16, b // 16)), R(ys, a, b), ALU.mult)
            act(z, z, AF.Tanh, scale=2.0 ** -14)
            if n2 <= a < nd:
                if t % 2:
                    for c in range(a, b, 512):
                        w = BK["O"][(c // 512) % len(BK["O"])]
                        group([(PS(w), R("Gd", 128 * t - 128, 128 * t), R("Z", c, c + 512)),
                               (PS(w), R("Gd", 128 * t, 128 * t + 128), R("Tr", o + c - a, o + c - a + 512))])
                        mul(OPT["gain"][t][c // 512], R("Z", c, c + 512), PS(w), 1.0)
                    if b in stores:
                        dma("s" if t == 1 else "g", [(R("yo", done, b), R("Z", done, b))], add=t > 1)
                        done = b
                continue
            if a >= nd:
                for c in range(a, b, 512):
                    e = min(c + 512, b)
                    group([(R("ps", c, e), R("Gd", 128 * t, 128 * t + 128), R("Tr", o + c - a, o + e - a))], first=t == 0, last=last and e % 512 == 0)
                    if last and e % 512 == 0:
                        mul(OPT["evO"][(c - nd) // 512], R(ys, e - 512, e), R("ps", e - 512, e), 1.0)
                        dma("s", [(R("yo", e - 512, e), R(ys, e - 512, e))])
                continue
            mul(OPT["gain"][t][a // 512], z, z, R("gn", t, t + 1))
            if b in stores:
                dma("s" if t == 0 else "g", [(R("yo", done, b), R("Z", done, b))], add=t > 0)
                done = b

    def serve(t):
        yw = R("Y%d" % (t % 2))
        tt(R("cmp"), IND(yw, R("cLU", 64 * t, 64 * t + 64)), R("cA", 1088 * t + 64, 1088 * t + 1088), ALU.is_gt)
        group([(PS(L, 98, 162), n128I, R("cA", 1088 * t, 1088 * t + 64))] + [(PS(L, 98, 162), R("V1", 15 - i, 143 - i), R("cmp", i, B, 16)) for i in range(16)])
        sg = R("sg", 64 * t, 64 * t + 64)
        act(sg, PS(L, 98, 162), AF.Sign, bias=-8.5)
        ks = [post(client(t), partner(t), R("csg", 64 * t, 64 * t + 64), sg, [R(XB[0])] if t == 2 else [])]
        for h in range(2):
            f = R("F", 512 * h, 512 * h + 512)
            act(f, IND(yw, R("cLU", 64 * t + 32 * h, 64 * t + 32 * h + 32)), AF.Identity, bias=col(10), scale=1 / 16.0)
            ks.append(post(client(t), partner(t), R("cF", 512 * h, 512 * h + 512), f, also=[R("cA", 1088 * t, 1088 * t + 8)]))
        send_y(t, 1, after=ks)

    def update(t):
        sg, deb = R("csg", 64 * t, 64 * t + 64), R("mA", 0, 64)
        o1, o2 = PS(L, 98, 162), PS(L, 162, 226)
        group([(o1, I, d), (o1, I, deb), (o1, I, sg)])
        group([(o2, p2I, d), (o2, p2I, deb), (o2, p2I, sg)])
        cp(R("dj"), o1)
        ts(R("c2"), o2, 2.0, ALU.max, 14.0, ALU.min)
        tt(d, R("c2"), o1, ALU.subtract)
        for h in range(2):
            a, b = 512 * h, 512 * h + 512
            w = wbank()
            group([(PS(w), I, R("c192")), (PS(w), I, R("v", a, b)), (PS(w), SB, R("cF", a, b))])
            ts(R("v", a, b), PS(w), -64.0, ALU.max, 64.0, ALU.min)
            w = wbank()
            neg = [(PS(w), nI, R("A", a, b))] + ([(PS(w, 64, 512), nI, R("dvn"))] if h else []) + [(PS(w), nI, R("v", a, b))]
            group(neg)
            if OPT["fold"][t][h] == "v":
                ts(R("cl", a, b), PS(w), -256.0, ALU.max, 256.0, ALU.min)
                group(neg + [(PS(w), n2I, R("cl", a, b))])
                mul(OPT["evA"][h], R("A", a, b), PS(w), 1.0)
            else:
                c = R("D", a, b)
                act(c, PS(w), AF.Abs, bias=256.0)
                act(c, c, AF.Abs, bias=512.0, scale=-1.0)
                if OPT["fold"][t][h] == "a":
                    act(R("A", a, b), c, AF.Identity, bias=-256.0)
                else:
                    ts(R("A", a, b), c, -256.0, ALU.add)
        if t + 1 < NB - 1:
            dma("s", turn("mA", "A", 64, 1088))

    start()
    for t in range(NB):
        now[0] = t
        if t > 0:
            tag[0] = "upd"
            update(t - 1)
        tag[0] = "lists"
        lists(t)
        tag[0] = "y"
        make_y(t)
        if t < NB - 1:
            tag[0] = "serve"
            serve(t)
        landed_x(t)
        tag[0] = "read"
        reading(t)
        tag[0] = "out"
        if t > 0:
            output(t - 1)
        y_turn(t)
    output(NB - 1)

    cnt = {"v": 0, "a": 0, "p": 0, "g": 0}
    known = {e: {} for e in Q}
    total = {}
    acc = {}

    def wait(e, tok):
        if known[e].get(tok[0], 0) < tok[1]:
            Q[e].wait_ge(T.sem[tok[0]], tok[1])
            known[e][tok[0]] = tok[1]

    def whole(sp):
        return (sp[0], sp[1] // 512 * 512, (sp[2] + 511) // 512 * 512) if sp[0] == "ps" else sp

    key = tuple((o["e"], o["cost"]) for o in ops)
    if key not in ORDER:
        ORDER[key] = plan(ops)
    for k in ORDER[key]:
        o = ops[k]
        e = o["e"]
        if e == "f":
            continue
        rs, ws = [whole(x) for x in o["rs"]], [whole(x) for x in o["ws"]]
        if e != "r":
            need = {}
            for lst, isw in ((rs, False), (ws, True)):
                for sp in lst:
                    for asp, aw, ae, tok in acc.get(sp[0], []):
                        if hits(sp, asp):
                            if sp[0] == "ps":
                                if ae == e and (e == "p" or not (aw or isw)):
                                    continue
                            elif not (aw or isw):
                                continue
                            need[tok[0]] = max(need.get(tok[0], 0), tok[1])
            if o["pre"]:
                wait(e, o["pre"])
            for s in need:
                wait(e, (s, need[s]))
        tok = o["tok"]
        for fn in o["fns"]:
            if tok is None:
                cnt[e] += 1
                fn().then_inc(T.sem[csem[e]], 1)
            else:
                fn()
        tok = tok or (csem[e], cnt[e])
        for sp in ws:
            if o["move"] and o["move"][0] == "remote":
                continue
            acc[sp[0]] = [x for x in acc.get(sp[0], []) if not (sp[1] <= x[0][1] and x[0][2] <= sp[2])] + [(sp, True, e, tok)]
        for sp in rs:
            acc[sp[0]] = [x for x in acc.get(sp[0], []) if x[1] or x[3][0] != tok[0] or not (sp[1] <= x[0][1] and x[0][2] <= sp[2])] + [(sp, False, e, tok)]
        total[tok[0]] = max(total.get(tok[0], 0), tok[1])
    for s in total:
        if max(known[e].get(s, 0) for e in known) < total[s]:
            wait("g", (s, total[s]))
